import numpy as np, ml_dtypes
CORES = [6,15,38,47]
N = 4
BF = ml_dtypes.bfloat16
def gentries(a):
    return np.ascontiguousarray(a.reshape(8, 16, -1).transpose(0, 2, 1)).reshape(8, -1)
def gtable(e):
    e = np.asarray(e); return np.ascontiguousarray(e.reshape(8, -1, 16).transpose(0, 2, 1)).reshape(128, -1).astype(np.int32)
L, V, W, RO, MP = 256, 2048, 4096, 4, 8
HN, HZ = [1, 1, 1, 1], [1, 1, 1, 1]
def parts(rng):
    return (rng.integers(0, 256, (N, 8, 16, W)), rng.integers(0, W, (N, 8, 16, V)), rng.integers(0, 256, (N, 8, 16, L)),
            rng.integers(0, V, (N, 8, L)), rng.integers(1, 4096, (N, 8, 16, 1)), rng.integers(0, 256, (N, 8, RO)))
def pack(x, b, z, v, w, t):
    return {"xt": np.ascontiguousarray(x.reshape(N, 128, W)).astype(np.float32).astype(BF), "bag": np.ascontiguousarray(b.reshape(N, 128, V)).astype(np.int32),
            "z0": np.ascontiguousarray(z.reshape(N, 128, L)).astype(np.float32).astype(BF), "v0": np.stack([gtable(a) for a in v]),
            "uw": np.ascontiguousarray(w.reshape(N, 128, 1)).astype(np.int32), "bt": np.ascontiguousarray(t).astype(np.int32)}
def setup_inputs(rng):
    return pack(*parts(rng))
def setup_inputs_spread(rng):
    x, b, z, v, w, t = parts(rng)
    x = np.minimum((np.exp2(8 * rng.random((N, 8, 1, W))) * rng.random(x.shape) * 1.2).astype(np.int64), 255)
    z = np.minimum((np.exp2(8 * rng.random((N, 8, 1, L))) * rng.random(z.shape) * 1.2).astype(np.int64), 255)
    p = rng.choice(np.array([1, 2, 3, 5]), (N, 8, 1, 1))
    b = np.minimum((W * rng.random(b.shape) ** p).astype(np.int64), W - 1); v = np.minimum((V * rng.random(v.shape) ** p[..., 0]).astype(np.int64), V - 1)
    w = np.minimum(np.maximum(np.exp2(12 * rng.random(w.shape)).astype(np.int64), 1), 4095); t = np.minimum(np.exp2(8 * rng.random(t.shape)).astype(np.int64) - 1, 255)
    return pack(x, b, z, v, w, t)
def twos(rng, n):
    a = rng.integers(0, 2, (N, 8, 16, n))
    return 255 * np.where(rng.random((N, 8, 1, n)) < 0.5, a[:, :, :1], a)
def setup_inputs_ends(rng):
    x, b, z, v, w, t = parts(rng)
    x = twos(rng, W); z = twos(rng, L); x[:, 1::2, :, 0] = 0; x[:, 1::2, :, W - 1] = 255
    eb = (W - 1) * rng.integers(0, 2, b.shape); ev = (V - 1) * rng.integers(0, 2, v.shape)
    kb = rng.random(b.shape) < 0.7; kv = rng.random(v.shape) < 0.7; kb[:, 3::4] = True; kv[:, 3::4] = True
    b = np.where(kb, eb, b); v = np.where(kv, ev, v)
    b[:, 7, :, V - 1] = W - 1; b[:, 7, 0, V - 1] = 0
    b[:, 7, :, 0] = W - 1; b[:, 7, 1::2, 0] = 0
    v[:, :, 0] = 0; v[:, :, L - 1] = V - 1; v[:, 7, 4] = V - 1; v[:, 7, 7] = 0
    z[:, 7, :, L - 1] = 255; z[:, 7, :, 4] = 255; z[:, 7, :, 7] = 0; z[:, 6, :, L - 1] = 255; z[:, 6, :, 2] = 0
    w = np.where(rng.random(w.shape) < 0.5, 1, 4095); w[:, 7] = 4095; w[:, 6] = 1
    t = 255 * rng.integers(0, 2, t.shape); t[:, 7, 0] = 255; t[:, 6, 0] = 0
    return pack(x, b, z, v, w, t)
def setup_inputs_corners(rng):
    x, b, z, v, w, t = parts(rng); lane = np.arange(L)
    for g in range(3):
        h = 5 * g + 1; x[:, g] = 0; x[:, g, h] = np.arange(W) & 255; z[:, g] = 0
        be = rng.integers(0, 61, N); be[0] = (0, 1, 60)[g]; be[N - 1] = (60, 0, 1)[g]; t[:, g, 0] = be
        v[:, g] = np.argsort(rng.random((N, V)), axis=1)[:, :L]
        for r in range(N):
            e = int(be[r]); m = rng.integers(100, 180, (L, 1)); c = np.array([0, max(e - 1, 0), e, e + 1])
            q = np.concatenate([m - rng.choice(c, (L, MP - 1)), m, m + rng.choice(c, (L, 15 - MP))], axis=1)
            q = np.concatenate([np.zeros((L, 1), np.int64), rng.permuted(q, axis=1)], axis=1)
            b[r, g, :, v[r, g]] = q + 256 * rng.integers(0, W // 256, (L, 16))
            z[r, g, h] = m[:, 0] + rng.choice(np.array([-e - 1, -e, -1, 0, e, e + 1]), L)
    v[:, 3] = lane; t[:, 3] = 255
    v[:, 4] = np.where(rng.random((N, L)) < 0.5, rng.choice(np.array([0, V - 1, V // 2 - 1, V // 2]), (N, L)), lane); t[:, 4] = 0
    v[:, 5] = (lane >> 1) + V // 2 * (lane & 1); b[:, 5, :, V // 2:] = b[:, 5, :, :V // 2]
    b[:, 6] = np.where(rng.random((N, 1, V)) < 0.5, b[:, 6, :1], b[:, 6])
    p0 = np.take_along_axis(b[:, 6, 0], v[:, 6], 1); z[:, 6, :, ::2] = np.take_along_axis(x[:, 6], p0[:, None, :], 2)[:, :, ::2]
    own = 16 * ((V - 1 - np.arange(V)) & (L - 1)) + rng.integers(0, 16, (N, 16, V))
    b[:, 7] = np.where(rng.random((N, 16, V)) < 0.7, own, rng.choice(np.array([0, W - 1]), (N, 16, V))); v[:, 7] = V - 1 - lane
    z[:, 7] = 255 * rng.integers(0, 2, (N, 1, L)); w[:, 7] = rng.choice(np.array([1, 4095]), (N, 16, 1))
    return pack(x, b, z, v, w, t)
def setup_inputs_crowd(rng):
    x, b, z, v, w, t = parts(rng); lane = np.arange(L)
    for g in range(8):
        p = int(rng.integers(1, V // 2 - 2)) if g != 7 else V - 1; c = int(rng.integers(0, W)); q = int(rng.integers(0, L - 1))
        x[:, g, :, c] = 0; b[:, g, 0, p] = c; v[:, g] = p
        small = rng.integers(0, 21, (N, 16, L))
        if g in (0, 1, 2, 7): z[:, g] = small
        if g in (3, 4): z[:, g] = 255 - small
        if g == 1: v[:, g, q] = p + 1
        if g == 2: v[:, g] = p + V // 2 * (lane & 1); b[:, g, :, p + V // 2] = b[:, g, :, p]
        if g == 4: z[:, g, :, q] = small[:, :, q]
        if g == 5: v[:, g] = rng.choice(np.array([p, 0, V - 1]), (N, L)); b[:, g] = rng.choice(np.array([0, c, W // 2, W // 2 + 5, W - 1]), (N, 16, V))
        if g == 7: v[:, g, L - 1] = 0
    return pack(x, b, z, v, w, t)
def check_inputs(d):
    bad = []
    for k, lo, hi in (("xt", 0, 255), ("bag", 0, W - 1), ("z0", 0, 255), ("v0", 0, V - 1), ("uw", 1, 4095), ("bt", 0, 255)):
        a = np.asarray(d[k]).astype(np.float64)
        if not np.all((a >= lo) & (a <= hi)): bad.append("range of " + k)
        elif not np.all(a == np.floor(a)): bad.append("whole numbers of " + k)
    return bad
def reference(xt, bag, z0, v0, uw, bt):
    X = xt.astype(np.float32).astype(np.int64).reshape(N, 8, 16, W); B = bag.astype(np.int64).reshape(N, 8, 16, V)
    z = z0.astype(np.float32).astype(np.int64).reshape(N, 8, 16, L); v = np.stack([gentries(a) for a in v0]).astype(np.int64)
    wt = uw.astype(np.int64).reshape(N, 8, 16, 1); bands = bt.astype(np.int64); A = np.zeros((N, 8, L), np.int64)
    lane = np.arange(L); k = np.arange(16).reshape(1, 1, 16, 1); ri = np.arange(N).reshape(N, 1, 1); gi = np.arange(8).reshape(1, 8, 1)
    u = np.add.reduce(wt * z, axis=2) & (W - 1)
    for t in range(RO):
        P = np.take_along_axis(B, v[:, :, None, :], 3)
        flat = np.ascontiguousarray(P.transpose(0, 1, 3, 2)).reshape(N, 8, 1, 16 * L)
        x = np.take_along_axis(X, flat, 3).reshape(N, 8, 16, L, 16)
        D = np.add.reduce(np.abs(x - x[..., :1]), axis=2)
        o = np.argsort(D, axis=3, kind="stable")
        m = np.take_along_axis(D, o[..., MP:MP + 1], 3)[..., 0]; e = o[..., 15][:, :, None, :]
        beta = bands[:, :, t][:, :, None] + 32 * A; q = np.add.reduce(np.abs(z - x[..., 0]), axis=2)
        far = q >= m; amb = np.abs(q - m) <= beta
        D = D.transpose(0, 1, 3, 2); m = m[:, :, None]; be = beta[:, :, None]
        M = np.where(np.abs(D - m) <= be, P, -1)
        sn = [(r - HN[t]) % N for r in range(N)]; sz = [(r - HZ[t]) % N for r in range(N)]
        M2 = M[sn]; z2 = z[sz]; a2 = amb[sz]
        side = np.where(far[:, :, None], D > m + be, D < m - be)
        F = np.where(side, P, np.where(M2 >= 0, M2, (P + (2 * k + 1) * u[:, :, None]) & (W - 1)))
        fe = np.take_along_axis(F, e, 2); F = np.where(k == e, F[:, :, :1], np.where(k == 0, fe, F))
        w = (2 * v + 1 + far) & (V - 1)
        top = np.full((N, 8, V), -1, np.int64); np.maximum.at(top, (ri, gi, w), np.broadcast_to(lane, w.shape))
        r_, g_, i_ = np.nonzero(np.take_along_axis(top, w, 2) == lane)
        B[r_, g_, :, w[r_, g_, i_]] = F[r_, g_, :, i_]
        c = np.broadcast_to((16 * lane + (u & 15))[:, :, None, :], z.shape)
        np.put_along_axis(X, c, (np.take_along_axis(X, c, 3) + z) & 255, 3)
        z = np.where(a2[:, :, None], (z + z2) >> 1, z); u = np.add.reduce(wt * z, axis=2) & (W - 1)
        v = np.where(a2, u & (V - 1), w); A = amb.astype(np.int64)
    return {"yx": X.reshape(N, 128, W).astype(np.float32).astype(BF), "yb": (B[..., :V // 2] + W * B[..., V // 2:]).reshape(N, 128, V // 2).astype(np.float32),
            "yz": z.reshape(N, 128, L).astype(np.float32).astype(BF), "yv": np.stack([gtable(a) for a in v]).astype(np.float32)}

@@ -1,0 +1,775 @@
+from concourse.mybir import AluOpType, AxisListType, ActivationFunctionType
+
+RO = 4
+ALU = AluOpType
+ACT = ActivationFunctionType
+
+SCRATCH = {
+    "X": ("sbuf", [128, 4096], "bfloat16"),
+    "B": ("sbuf", [128, 2304], "int32"),
+    "xg": ("sbuf", [128, 4096], "bfloat16"),
+    "mx": ("sbuf", [128, 4096], "bfloat16"),
+    "Pu": ("sbuf", [128, 256], "uint16"),
+    "Ph": ("sbuf", [128, 256], "float16"),
+    "Uh": ("sbuf", [128, 256], "float16"),
+    "Dh": ("sbuf", [128, 256], "float16"),
+    "cm": ("sbuf", [128, 1792], "bfloat16"),
+    "ys": ("sbuf", [128, 256], "float16"),
+    "hl": ("sbuf", [128, 512], "bfloat16"),
+    "sd": ("sbuf", [128, 256], "bfloat16"),
+    "Q0": ("sbuf", [128, 256], "bfloat16"),
+    "Q1": ("sbuf", [128, 256], "bfloat16"),
+    "Es": ("sbuf", [128, 256], "bfloat16"),
+    "Hs": ("sbuf", [128, 256], "int32"),
+    "H": ("sbuf", [128, 256], "int32"),
+    "Ge": ("sbuf", [128, 256], "float32"),
+    "Fe": ("sbuf", [128, 256], "float32"),
+    "tE": ("sbuf", [128, 256], "float32"),
+    "Fs": ("sbuf", [128, 256], "int32"),
+    "Ff": ("sbuf", [128, 256], "int32"),
+    "old": ("sbuf", [128, 256], "bfloat16"),
+    "sg": ("sbuf", [128, 256], "bfloat16"),
+    "xn": ("sbuf", [128, 256], "bfloat16"),
+    "av": ("sbuf", [128, 256], "float32"),
+    "wR": ("sbuf", [128, 256], "uint16"),
+    "eq": ("sbuf", [128, 16, 272], "bfloat16"),
+    "one": ("sbuf", [128, 2], "bfloat16"),
+    "sc": ("sbuf", [128, 256], "float32"),
+    "iot": ("sbuf", [128, 2048], "float32"),
+    "wF": ("sbuf", [128, 128], "float32"),
+    "wA": ("sbuf", [128, 576], "float32"),
+    "yo": ("sbuf", [128, 1024], "float32"),
+    "vc": ("sbuf", [128, 32], "uint16"),
+    "wU": ("sbuf", [128, 16], "uint16"),
+    "oU": ("sbuf", [128, 16], "uint16"),
+    "v21": ("sbuf", [128, 16], "float32"),
+    "wi": ("sbuf", [128, 32], "int32"),
+    "ui": ("sbuf", [128, 32], "int32"),
+    "alt": ("sbuf", [128, 32], "int32"),
+    "dd": ("sbuf", [128, 32], "float32"),
+    "am": ("sbuf", [128, 32], "float32"),
+    "o1": ("sbuf", [128, 32], "float32"),
+    "v0i": ("sbuf", [128, 16], "int32"),
+    "uwi": ("sbuf", [128, 1], "int32"),
+    "bti": ("sbuf", [8, 4], "int32"),
+    "btb": ("sbuf", [8, 4], "bfloat16"),
+    "s8": ("sbuf", [8, 128], "bfloat16"),
+    "s8i": ("sbuf", [8, 128], "float32"),
+    "th": ("sbuf", [128, 20], "float32"),
+    "col": ("sbuf", [128, 40], "float32"),
+    "coi": ("sbuf", [128, 2], "int32"),
+    "io144": ("sbuf", [128, 144], "float32"),
+    "i16": ("sbuf", [128, 256], "float32"),
+    "cL": ("sbuf", [128, 48], "float32"),
+    "cLh": ("sbuf", [128, 16], "float16"),
+    "g8": ("sbuf", [128, 16], "bfloat16"),
+    "pa": ("sbuf", [128, 6, 112], "float32"),
+    "pat": ("sbuf", [128, 14, 16], "bfloat16"),
+    "pq": ("sbuf", [128, 224], "bfloat16"),
+    "SR": ("sbuf", [128, 14, 128], "bfloat16"),
+    "M": ("sbuf", [128, 19, 128], "bfloat16"),
+    "BI": ("sbuf", [128, 128], "float32"),
+    "Wi": ("sbuf", [128, 2, 128], "int32"),
+    "Wf": ("sbuf", [128, 128], "float32"),
+    "W": ("sbuf", [128, 128], "float16"),
+    "TT": ("sbuf", [128, 4, 144], "bfloat16"),
+    "Tu": ("sbuf", [128, 144], "float16"),
+    "thr": ("sbuf", [128, 256], "bfloat16"),
+    "rst": ("sbuf", [128, 256], "float32"),
+    "tmp": ("sbuf", [128, 768], "float32"),
+}
+WIDE = True
+for _t in range(RO):
+    for _s in ("ma", "mb", "la", "lb"):
+        SCRATCH[_s + str(_t)] = ("sbuf", [128, 128], "float32" if WIDE else "uint16")
+    SCRATCH["mc%d" % _t] = ("sbuf", [128, 16], "uint16")
+    SCRATCH["lc%d" % _t] = ("sbuf", [128, 16], "uint16")
+    SCRATCH["zl%d" % _t] = ("sbuf", [128, 256], "bfloat16")
+for _t in range(RO + 1):
+    SCRATCH["zw%d" % _t] = ("sbuf", [128, 512], "bfloat16")
+    SCRATCH["st%d" % _t] = ("sbuf", [128, 32], "float32")
+for _b in range(8):
+    SCRATCH["b%d" % _b] = ("psum", [128, 512], "float32")
+
+NDMA = 16
+SEMAPHORES = ["qV", "qS", "qP", "qG", "sent"] + ["d%d" % _i for _i in range(NDMA)] \
+    + [_s + str(_t) for _t in range(RO) for _s in ("az", "aa", "ab", "ac")]
+
+GATHERS = [(0, 64, "V"), (64, 128, "S"), (128, 192, "S"), (192, 256, "S")]
+CHUNKS = [(0, 64), (64, 128), (128, 192), (192, 256)]
+OPT = {"ulay": True, "cmpv": ((False, False), (False, False)), "hlv": (False, False), "early": False,
+       "selS": False, "eqS": 0, "cyc": 1.04, "pe": 0.52, "gat": 1.56, "sca": 3.8, "hop": 70.0, "far": 2600.0,
+       "seed": 0, "tries": 12, "rounds": 2, "noise": 1000.0, "boost": (0.0, 0.0, 0.0)}
+ORDER = {}
+MAGIC = 12582912.0
+SIZE = {"bfloat16": 2, "float16": 2, "uint16": 2, "float32": 4, "int32": 4}
+
+
+def rank_program(g, core, T, topo):
+    rank = T.rank_of(core)
+    if rank is None:
+        return
+    n = len(T.cores)
+    ops = []
+    boost = [0.0]
+
+    def v(name, a=None, b=None, s=None, keys=None):
+        w = SCRATCH[name][1][-1]
+        lo = 0 if a is None else a
+        hi = w if b is None else b
+        ap_ = T[name][:, lo:hi] if s is None else T[name][:, lo:hi:s]
+        return (ap_, name, lo, hi, keys, len(range(lo, hi, s or 1)))
+
+    def v3(name, i0, a=None, b=None):
+        w = SCRATCH[name][1][-1]
+        lo = 0 if a is None else a
+        hi = w if b is None else b
+        return (T[name][:, i0, lo:hi], name, i0 * w + lo, i0 * w + hi, None, hi - lo)
+
+    def vk(name, a, b, k, step=16):
+        return v(name, 16 * a + k, 16 * b, step, tuple(range(k, 16, step)))
+
+    def ind(win, off):
+        return (win[0].indirect(off[0]), win, off)
+
+    def regs(x):
+        if not isinstance(x, tuple):
+            return []
+        if isinstance(x[1], tuple):
+            return [x[1], x[2]]
+        return [x]
+
+    def ap(x):
+        return x[0] if isinstance(x, tuple) else x
+
+    def add(q, call, outs, ins, cyc, kind="c", extra=None, done=None):
+        rd, wr = [], []
+        t = max(64, cyc) * OPT["cyc"] if q != "P" and kind == "c" else cyc
+        for x in ins:
+            rd += regs(x)
+            if len(regs(x)) == 2:
+                t = 70 + 16 * x[2][5] * OPT["gat"] * OPT["cyc"]
+        for x in outs:
+            r = regs(x)
+            wr.append(r[0])
+            rd += r[1:]
+            if len(r) == 2:
+                t = 70 + 16 * x[2][5] * OPT["sca"] * OPT["cyc"]
+        ops.append((q, call, rd, wr, kind, extra, t, done or t, boost[0]))
+
+    def cnt(out, a):
+        x, y = regs(out)[0], regs(a)[0]
+        return x[5] * (0.5 if SIZE[SCRATCH[x[1]][2]] == 2 and SIZE[SCRATCH[y[1]][2]] == 2 else 1)
+
+    def copy(out, in_):
+        add("V", lambda: g.vector.tensor_copy(ap(out), ap(in_)), [out], [in_], cnt(out, in_))
+
+    def tt(out, a, b, op):
+        two = 1 if "psum" in (SCRATCH[a[1]][0], SCRATCH[b[1]][0]) else 2
+        add("V", lambda: g.vector.tensor_tensor(ap(out), ap(a), ap(b), op), [out], [a, b], two * out[5])
+
+    def ts(out, a, s1, op0, s2=None, op1=None):
+        if op1 is None:
+            add("V", lambda: g.vector.tensor_scalar(ap(out), ap(a), ap(s1), None, op0), [out], [a, s1], cnt(out, a))
+        else:
+            add("V", lambda: g.vector.tensor_scalar(ap(out), ap(a), ap(s1), ap(s2), op0, op1), [out], [a, s1, s2], cnt(out, a))
+
+    def scan(out, d0, d1, init, op0, op1):
+        add("V", lambda: g.vector.tensor_tensor_scan(ap(out), ap(d0), ap(d1), init, op0, op1), [out], [d0, d1], out[5])
+
+    def memset(out, c_):
+        add("V", lambda: g.vector.memset(ap(out), c_), [out], [], out[5])
+
+    def act(out, a, f, bias=0.0, scale=1.0):
+        add("S", lambda: g.scalar.activation(ap(out), ap(a), f, bias=ap(bias), scale=ap(scale)), [out], [a, bias, scale], out[5])
+
+    def mm(out, l, r, start, stop):
+        t = max(min(64, l[5]), r[5]) * OPT["pe"] * (4 if SCRATCH[l[1]][2] == "float32" else 1)
+        add("P", lambda: g.tensor.matmul(ap(out), ap(l), ap(r), start, stop), [out], [l, r], t)
+
+    def iota(out, pattern, base, cmul):
+        if SCRATCH[out[1]][2] == "int32":
+            add("G", lambda: g.iota(ap(out), pattern, base, cmul), [out], [], 160 + 2 * out[5])
+        else:
+            add("G", lambda: g.iota(ap(out), pattern, base, cmul, allow_small_or_imprecise_dtypes=True), [out], [], 160 + 2 * out[5])
+
+    ndma = [0]
+
+    def dma(q, out, in_, done):
+        eng = g.sync if q == "Y" else g.scalar
+        add(q, lambda: eng.dma_start(ap(out), ap(in_)), [out] if isinstance(out, tuple) else [], [in_], 100, "d",
+            "d%d" % ndma[0], done)
+        ndma[0] += 1
+
+    def send(src, dst, sem, hop):
+        to = T.cores[(rank + hop) % n]
+        rid, pid, _ = topo.addr(to)
+        mask = topo.mask(core, to)
+        add("G", lambda: g.remote_dma(T[dst][:], ap(src), T.sem[sem], T.sem.sent, pid, rid, mask), [], [src], 300, "r",
+            len(topo.engines(core, to)), OPT["far"])
+        frm = T.cores[(rank - hop) % n]
+        add("X", None, [v(dst)], [], 0, "a", (sem, len(topo.engines(frm, core))))
+
+    hn = T.tables.get("HN", [1] * RO)
+    hz = T.tables.get("HZ", [1] * RO)
+
+    dma("Y", v("uwi"), T.uw[:], 2000)
+    dma("S", v("zw0", 0, 256), T.z0[:], 2200)
+    dma("Y", v("v0i"), T.v0[:], 2000)
+    dma("Y", v("B", 0, 2048), T.bag[:], 7000)
+    dma("S", v("X"), T.xt[:], 8000)
+    dma("S", v("bti"), T.bt[:], 3000)
+
+    ncol = [0]
+
+    def col():
+        ncol[0] += 1
+        return v("col", ncol[0] - 1, ncol[0])
+    iota(v("io144"), [[1, 144]], 0, 0)
+    iota(v("coi", 0, 1), [[1, 1]], 0, 1)
+    iota(v("i16"), [[0, 16], [1, 16]], 0, 0)
+    iota(v3("pa", 0), [[-1, 7], [1, 16]], -1, 0)
+    iota(v3("pa", 1), [[1, 7], [1, 16]], 1, 0)
+    iota(v("s8i"), [[1, 8], [0, 16]], 0, -1)
+    send(v("zw0", 0, 256), "zl0", "az0", hz[0])
+    iota(v("iot"), [[1, 2048]], 0, 0)
+
+    cr, cg, ct, c0, c1, cp, cu = col(), col(), col(), col(), col(), col(), col()
+    ts(v("coi", 1, 2), v("coi", 0, 1), 15, ALU.bitwise_and)
+    copy(cr, v("coi", 1, 2))
+    tt(cg, v("coi", 0, 1), cr, ALU.subtract)
+    ts(ct, cg, 15.0, ALU.add)
+    ts(c0, cr, 0.0, ALU.is_equal)
+    ts(c1, cr, 1.0, ALU.is_ge)
+    I, NBO, IP, NIP, BOP, NBOP, QY, AQ, AQ2, IM, IG, SQ, CQ, IZ, BOA, BOD, IX, IH, NIH = range(19)
+
+    def m(i):
+        return v3("M", i)
+    copy(cp, v("coi", 0, 1))
+    ts(m(I), v("io144", 0, 128), cp, ALU.is_equal)
+    ts(v("tmp", 0, 128), v("io144", 0, 128), cg, ALU.is_ge)
+    ts(v("tmp", 128, 256), v("io144", 0, 128), ct, ALU.is_le, -1.0, ALU.mult)
+    tt(m(NBO), v("tmp", 0, 128), v("tmp", 128, 256), ALU.mult)
+    T2, TM1, TAM, TFA = range(4)
+    gsel = v("col", 32, 40)
+    ts(gsel, v("io144", 0, 8), 16.0, ALU.mult, cg, ALU.is_equal)
+    if OPT["ulay"]:
+        ts(v("g8", 0, 8), gsel, 2.0, ALU.mult)
+        ts(v("g8", 8, 16), gsel, -1.0, ALU.mult)
+    else:
+        ts(v3("TT", T2), v("io144"), ct, ALU.is_equal, 2.0, ALU.mult)
+        ts(v3("TT", TM1), v("io144"), ct, ALU.is_equal, -1.0, ALU.mult)
+    copy(cu, v("uwi"))
+    ts(v("Wf"), v("i16", 0, 128), 2.0, ALU.mult, 1.0, ALU.add)
+    ts(v3("Wi", 0), v("Wf"), cu, ALU.mult, 2048.0, ALU.add)
+    ts(v3("Wi", 1), v3("Wi", 0), 4095, ALU.bitwise_and)
+    ts(v("Wf"), v3("Wi", 1), -1.0, ALU.mult, 2048.0, ALU.add)
+    tt(v("W"), v("Wf"), m(NBO), ALU.mult)
+    ts(cu, v("Wf", 0, 1), -1.0, ALU.mult)
+    ts(v("Tu"), v("io144"), ct, ALU.is_equal, cu, ALU.mult)
+    ts(v("cL", 0, 16), v("io144", 0, 16), 16.0, ALU.mult, cr, ALU.add)
+    ts(v("cL", 16, 32), v("cL", 0, 16), 16.0, ALU.mult)
+    ts(v("cL", 32, 48), v("cL", 0, 16), 2048.0, ALU.add)
+    ts(v("cLh"), v("cL", 0, 16), 8.0, ALU.mult)
+    ts(v("cL", 0, 16), v("cL", 0, 16), -4.0, ALU.mult, 0.5, ALU.add)
+
+    def ulist(zv, bank):
+        for p in range(16):
+            mm(bank, v("Tu", 15 - p, 143 - p), v(zv[1], zv[2] + p, zv[3], 16), p == 0, p == 15)
+
+    ulist(v("zw0", 0, 256), v("b6", 0, 16))
+    copy(v("st0", 0, 16), v("v0i"))
+    copy(v("vc", 0, 16), v("v0i"))
+    copy(v("ui", 0, 16), v("b6", 0, 16))
+    ts(v("ui", 16, 32), v("ui", 0, 16), 15, ALU.bitwise_and)
+    tt(v("st0", 16, 32), v("ui", 16, 32), v("cL", 16, 32), ALU.add)
+    copy(v("vc", 16, 32), v("st0", 16, 32))
+
+    def pa(i):
+        return v3("pa", i)
+    cm15, cp15 = col(), col()
+    ts(cm15, cr, -15.0, ALU.add)
+    ts(pa(2), pa(1), 15.5, ALU.is_lt, 0.5, ALU.subtract)
+    ts(pa(3), v("i16", 0, 112), cr, ALU.is_equal, -2.0, ALU.mult)
+    tt(pa(2), pa(2), pa(3), ALU.mult)
+    ts(pa(3), pa(0), cr, ALU.is_equal)
+    ts(pa(4), pa(0), cm15, ALU.is_equal)
+    tt(pa(3), pa(3), pa(4), ALU.subtract)
+    tt(pa(3), pa(3), pa(2), ALU.add)
+    ts(pa(5), v("i16", 0, 112), 1.0, ALU.is_ge, c1, ALU.mult)
+    tt(v("pq", 112, 224), pa(3), pa(5), ALU.mult)
+    ts(cp15, cr, 15.0, ALU.add)
+    ts(pa(4), pa(1), cr, ALU.is_equal)
+    ts(pa(0), pa(1), cp15, ALU.is_equal)
+    tt(pa(4), pa(4), pa(0), ALU.subtract)
+    tt(pa(4), pa(4), pa(2), ALU.add)
+    tt(v("pq", 0, 112), pa(4), pa(5), ALU.mult)
+    pat = (T.pat[:], "pat", 0, 224, None, 224)
+    dma("Y", pat, v("pq"), 2000)
+    for gg in range(8):
+        o = (T.SR[:, :, 16 * gg:16 * gg + 16], "SR", 0, 14 * 128, (gg,), 224)
+        if gg % 2:
+            act(o, pat, ACT.Identity, scale=v("col", 32 + gg, 33 + gg))
+        else:
+            ts(o, pat, v("col", 32 + gg, 33 + gg), ALU.mult)
+    act(m(IP), m(I), ACT.Identity, scale=c1)
+    act(m(NIP), m(IP), ACT.Identity, scale=-1.0)
+    act(m(NBOP), m(NBO), ACT.Identity, scale=c1)
+    act(m(BOP), m(NBOP), ACT.Identity, scale=-1.0)
+    act(m(IM), m(I), ACT.Identity, scale=-4096.0)
+    act(m(IG), m(I), ACT.Identity, scale=16384.0)
+    act(m(IZ), m(I), ACT.Identity, scale=32768.0)
+    act(m(IX), m(I), ACT.Identity, scale=-128.0)
+    act(m(IH), m(I), ACT.Identity, scale=0.5)
+    act(m(NIH), m(I), ACT.Identity, scale=-0.5)
+    act(m(BOA), m(NBO), ACT.Identity, scale=-float(2 ** 28))
+    ca, c2, c3, cam, cfa, c12, c13, c14, c15, c16, csg, ce0 = [col() for _ in range(12)]
+    ts(ca, cr, 1.5, ALU.is_lt, -16.0, ALU.mult)
+    act(m(AQ), m(NBO), ACT.Identity, scale=ca)
+    ts(v("tmp", 256, 384), v("i16", 0, 128), 1.5, ALU.is_lt)
+    tt(m(AQ2), m(AQ), v("tmp", 256, 384), ALU.mult)
+    ts(v("tmp", 512, 640), v("i16", 0, 128), 1.0, ALU.is_equal, 2.0, ALU.mult)
+    ts(v("tmp", 384, 512), v("i16", 0, 128), 2.0, ALU.not_equal)
+    tt(v("tmp", 384, 512), v("tmp", 512, 640), v("tmp", 384, 512), ALU.subtract)
+    tt(m(QY), v("tmp", 384, 512), m(NBO), ALU.mult)
+    ts(c2, cr, 2.0, ALU.is_equal, 22528.0, ALU.mult)
+    ts(c3, cr, 3.0, ALU.is_equal, -1.0, ALU.mult)
+    act(m(CQ), m(NBO), ACT.Identity, scale=c2)
+    act(m(SQ), m(NBO), ACT.Identity, scale=c3)
+    ts(cam, ca, 64.0, ALU.mult)
+    tt(cfa, c2, c3, ALU.not_equal)
+    ts(cfa, cfa, 0.5, ALU.mult, cam, ALU.add)
+    ts(v3("TT", TAM), v("io144"), ct, ALU.is_equal, cfa, ALU.mult)
+    tt(v("BI"), m(NBO), m(I), ALU.add)
+    act(v("BI"), v("BI"), ACT.Identity, scale=-1.0)
+    memset(v("tmp", 640, 656), 2.0)
+    memset(v("tmp", 656, 672), 0.0)
+    scan(v("tmp", 672, 688), v("tmp", 640, 656), v("tmp", 656, 672), 2048.0, ALU.mult, ALU.add)
+    ts(v("tmp", 688, 704), v("i16", 0, 16), cr, ALU.is_equal)
+    tt(v("tmp", 672, 688), v("tmp", 672, 688), v("tmp", 688, 704), ALU.mult)
+    add("V", lambda: g.vector.tensor_reduce(c12[0], T.tmp[:, 672:688], AxisListType.X, ALU.add, negate=True),
+        [c12], [v("tmp", 672, 688)], 16)
+    act(m(BOD), m(NBO), ACT.Identity, scale=c12)
+    ts(c13, c12, 2.0, ALU.mult, float(2 ** 36), ALU.add)
+    ts(v("sc"), v("i16"), cr, ALU.is_equal, c13, ALU.mult)
+    act(v("thr"), v("sc"), ACT.Identity, bias=-float(2 ** 36))
+    ts(v("rst"), v("i16"), 0.5, ALU.is_ge, 0.5, ALU.subtract)
+    act(v("rst"), v("rst"), ACT.Identity, scale=float(2 ** 41))
+    ts(v("s8"), v("s8i"), 0.0, ALU.is_equal)
+    copy(v("btb"), v("bti"))
+    mm(v("b7", 0, 4), v("s8"), v("btb"), True, True)
+    ts(c14, c0, -2040.0, ALU.mult, -0.5, ALU.add)
+    ts(c16, c0, 2040.0, ALU.mult, -0.5, ALU.add)
+    ts(v("th", 0, 4), v("b7", 0, 4), -1.0, ALU.mult, c14, ALU.add)
+    ts(v("th", 4, 8), v("b7", 0, 4), -1.0, ALU.mult, c16, ALU.add)
+    ts(c14, cr, 1.5, ALU.is_lt, -1.0, ALU.mult)
+    ts(c15, c14, 0.5, ALU.add)
+    ts(v("th", 8, 12), v("b7", 0, 4), c14, ALU.mult, c15, ALU.add)
+    ts(csg, c0, 2.0, ALU.mult, -1.0, ALU.add)
+    ts(ce0, c0, 14.0, ALU.mult, -13.0, ALU.add)
+    if True in OPT["hlv"]:
+        ts(v("th", 12, 20), v("th", 0, 8), -1.0, ALU.mult)
+
+    def sr(i):
+        return v3("SR", i)
+    memset(v("one"), 1.0)
+    coff, ce, cx = [], [], []
+    for h in range(2):
+        onv = [s for s in range(7) if OPT["cmpv"][h][s // 4]]
+        ce.append(col())
+        cx.append(col())
+        if onv:
+            coff.append(col())
+            for s in onv:
+                mm(v("b5", 0, 2), sr(7 + s), v("one"), s == onv[0], s == onv[-1])
+            copy(coff[h], v("b5", 0, 1))
+            tt(ce[h], ce0, coff[h], ALU.subtract)
+        else:
+            coff.append(0.0)
+            copy(ce[h], ce0)
+        ts(cx[h], ce[h], -0.5, ALU.add)
+
+    def slide(i, p):
+        return v3("TT", i, 15 - p, 143 - p)
+
+    for t in range(RO):
+        last = t == RO - 1
+        zw, zn, st, sn = "zw%d" % t, "zw%d" % (t + 1), "st%d" % t, "st%d" % (t + 1)
+        z = v(zw, 0, 256)
+        Q, Qp = "Q%d" % (t % 2), "Q%d" % ((t + 1) % 2)
+        copy(v("Pu"), ind(v("B", 0, 2048), v("vc", 0, 16)))
+        ts(v("Ph"), v("Pu"), -2048.0, ALU.add)
+        mm(v("b4", 0, 256), v("W"), z, True, False)
+        mm(v("b4", 0, 256), m(I), v("Ph"), False, True)
+        ts(v("Hs"), v("b4", 0, 256), 2048.0, ALU.add)
+        ts(v("H"), v("Hs"), 4095, ALU.bitwise_and)
+        tt(v("v21"), v(st, 0, 16), v("cL", 0, 16), ALU.add)
+        act(v("v21"), v("v21"), ACT.Identity, scale=2.0)
+        act(v("old"), ind(v("X"), v("vc", 16, 32)), ACT.Identity)
+        mm(v("b7", 256, 512), m(I), v("old"), True, False)
+        mm(v("b7", 256, 512), m(I), z, False, True)
+        act(v("sg"), v("b7", 256, 512), ACT.Sign, bias=-255.5)
+        mm(v("b7", 256, 512), m(I), v("old"), True, False)
+        mm(v("b7", 256, 512), m(I), z, False, False)
+        mm(v("b7", 256, 512), m(IX), v("sg"), False, True)
+        act(v("xn"), v("b7", 256, 512), ACT.Identity, bias=-128.0)
+        mm(v("b6", 0, 256), m(I), z, True, False)
+        mm(v("b6", 0, 256), m(I), v("zl%d" % t), False, True)
+        act(v("av"), v("b6", 0, 256), ACT.Identity, bias=MAGIC, scale=0.5 - 2.0 ** -11)
+        act(v(zw, 256, 512), v("av"), ACT.Identity, bias=-MAGIC)
+        ulist(v(zw, 256, 512), v("b7", 0, 16))
+        copy(v("ui", 0, 16), v("b7", 0, 16))
+        ts(v("alt", 0, 16), v("ui", 0, 16), 2047, ALU.bitwise_and)
+        if not last:
+            ts(v("ui", 16, 32), v("ui", 0, 16), 15, ALU.bitwise_and)
+            tt(v("alt", 16, 32), v("ui", 16, 32), v("cL", 16, 32), ALU.add)
+
+        def hv(name, h, off=0):
+            return v(name, off + 128 * h, off + 128 * h + 128)
+
+        def distances(i):
+            a, b = CHUNKS[i]
+            bank, w = "b%d" % (i % 2), 4 * (b - a)
+            for r in range(4):
+                mm(v(bank, r, w, 4), m(I), vk("xg", a, b, 0), True, True)
+            d = v("b%d" % (2 + a // 128), a % 128, a % 128 + b - a)
+            if not OPT["ulay"]:
+                mm(d, m(NBO), vk("xg", a, b, 0), True, False)
+                mm(d, slide(TM1, 0), v(zw, a, b), False, False)
+                for k in range(1, 16):
+                    mm(d, slide(TM1, k), vk("xg", a, b, k), False, False)
+            parts = [(1, 4), (2, 4), (3, 4), (4, 8), (8, 16), (0, 16)]
+            for k0, s in parts:
+                tt(vk("mx", a, b, k0, s), vk("xg", a, b, k0, s) if k0 else v(zw, a, b), v(bank, 0, w, s // 4), ALU.max)
+                if not OPT["ulay"]:
+                    for k in range(k0, 16, s):
+                        mm(d, slide(T2, k), vk("mx", a, b, k), False, k == 0)
+            if OPT["ulay"] and b % 128 == 0:
+                h, bank = a // 128, "b%d" % (2 + a // 128)
+                a, b = 128 * h, 128 * h + 128
+                mm(v(bank, 384, 512), vk("xg", a, b, 0), m(NBO), True, False)
+                for k in range(16):
+                    mm(v(bank, 384 + k, 512, 16), vk("xg", a, b, k) if k else v(zw, a, b), v("g8", 8, 16), False, False)
+                ks = [k for k0, s in parts for k in range(k0, 16, s)]
+                for k in ks:
+                    mm(v(bank, 384 + k, 512, 16), vk("mx", a, b, k), v("g8", 0, 8), False, k == ks[-1])
+                ts(hv("Uh", h), v(bank, 384, 512), -2040.0, ALU.add)
+                mm(v(bank, 0, 128), hv("Uh", h), m(I), True, True)
+
+        def ranks(h):
+            bd, br = "b%d" % (2 + h), "b%d" % (6 + h)
+            Dh, R, ys = hv("Dh", h), v(br, 0, 128), hv("ys", h)
+            ts(Dh, v(bd, 0, 128), 0.0 if OPT["ulay"] else -2040.0, ALU.add)
+            for bank, s0, s1, onv in (("b4", 0, 4, OPT["cmpv"][h][0]), ("b5", 4, 7, OPT["cmpv"][h][1])):
+                for s in range(s0, s1):
+                    mm(v(bank, 128 * (s - s0), 128 * (s - s0) + 128), sr(s), Dh, True, True)
+                o, i_ = v("cm", 896 * h + 128 * s0, 896 * h + 128 * s1), v(bank, 0, 128 * (s1 - s0))
+                if onv:
+                    ts(o, i_, -0.5, ALU.is_gt, 2.0, ALU.mult)
+                else:
+                    act(o, i_, ACT.Sign, bias=0.5)
+            for s in range(7):
+                mm(R, sr(7 + s), v("cm", 896 * h + 128 * s, 896 * h + 128 * s + 128), s == 0, s == 6)
+            if OPT["selS"]:
+                act(v(bd, 128, 256), R, ACT.Square)
+                act(v(bd, 128, 256), v(bd, 128, 256), ACT.Sign)
+                act(v(bd, 128, 256), v(bd, 128, 256), ACT.Identity, bias=csg, scale=cns)
+            else:
+                ts(v(bd, 128, 256), R, coff[h], ALU.is_equal, csg, ALU.mult)
+            tt(ys, Dh, v(bd, 128, 256), ALU.mult)
+            qb, hi, lo = v(br, 128, 256), v(bd, 256, 384), v(bd, 384, 512)
+            if t:
+                mm(qb, m(AQ2), hv(Qp, h), True, False)
+            mm(qb, m(QY), ys, t == 0, True)
+            for o, mi, mb in ((hi, IP, BOP), (lo, NIP, NBOP)):
+                mm(o, m(mi), Dh, True, False)
+                if t:
+                    mm(o, m(AQ), hv(Qp, h), False, False)
+                mm(o, m(mb), ys, False, True)
+            act(hv(Q, h), qb, ACT.Sign, bias=v("th", 8 + t, 9 + t))
+            if OPT["hlv"][h]:
+                ts(hv("hl", h), hi, v("th", 12 + t, 13 + t), ALU.is_gt, 2.0, ALU.mult)
+                ts(hv("hl", h, 256), lo, v("th", 16 + t, 17 + t), ALU.is_gt, 2.0, ALU.mult)
+            else:
+                act(hv("hl", h), hi, ACT.Sign, bias=v("th", t, t + 1))
+                act(hv("hl", h, 256), lo, ACT.Sign, bias=v("th", 4 + t, 5 + t))
+            mm(v(br, 256, 384), m(I), hv("Ph", h), True, False)
+            mm(v(br, 256, 384), m(IM), hv("hl", h), False, False)
+            mm(v(br, 256, 384), m(IM), hv("hl", h, 256), False, True)
+            ms = v("m" + "ab"[h] + str(t))
+            if WIDE:
+                act(ms, v(br, 256, 384), ACT.Identity, bias=6144.0 if OPT["hlv"][h] else -2048.0)
+            else:
+                ts(ms, v(br, 256, 384), 10240.0 if OPT["hlv"][h] else 2048.0, ALU.add)
+            send(ms, "l" + "ab"[h] + str(t), "a" + "ab"[h] + str(t), hn[t])
+
+        def own(h):
+            bd, R = "b%d" % (2 + h), v("b%d" % (6 + h), 0, 128)
+            act(hv("Es", h), R, ACT.Sign, bias=cx[h])
+            act(R, R, ACT.Relu, bias=ce[h])
+            mm(v(bd, 0, 128), m(IH), hv("hl", h), True, False)
+            mm(v(bd, 0, 128), m(NIH), hv("hl", h, 256), False, False)
+            mm(v(bd, 0, 128), m(SQ), hv(Q, h), False, True)
+            act(hv("sd", h), v(bd, 0, 128), ACT.Abs)
+            mm(v(bd, 128, 256), m(I), hv("Ph", h), True, False)
+            mm(v(bd, 128, 256), m(CQ), hv(Q, h), False, False)
+            mm(v(bd, 128, 256), m(IG), hv("sd", h), False, True)
+            tt(v(bd, 256, 384) if WIDE else hv("Ge", h), hv("H", h), v(bd, 128, 256), ALU.max)
+            mm(v(bd, 384, 512), m(IZ), hv("Es", h), True, False)
+
+        def merge(h):
+            bd, R = "b%d" % (2 + h), v("b%d" % (6 + h), 0, 128)
+            if WIDE:
+                tt(hv("Fe", h), v("l" + "ab"[h] + str(t)), v(bd, 256, 384), ALU.max)
+            else:
+                ts(v(bd, 256, 384), v("l" + "ab"[h] + str(t), 0, 128), -4096.0, ALU.add)
+                tt(hv("Fe", h), hv("Ge", h), v(bd, 256, 384), ALU.max)
+            tt(hv("tE", h), hv("Fe", h), R, ALU.mult)
+            mm(v(bd, 384, 512), v("BI"), hv("tE", h), False, True)
+            tt(hv("Fs", h), hv("Fe", h), v(bd, 384, 512), ALU.max)
+            ts(hv("Ff", h), hv("Fs", h), 4095, ALU.bitwise_and)
+
+        def lists(j0, j1, bank):
+            y = v(bank, 384, 384 + j1 - j0)
+            mm(y, m(I), v("cLh", j0, j1), True, False)
+            for p in range(16):
+                mm(y, slide(TAM, p), v(Q, 16 * j0 + p, 16 * j1, 16), False, p == 15)
+            tt(v("wi", j0, j1), v("v21", j0, j1), y, ALU.add)
+            ts(v("mc%d" % t, j0, j1), y, 0.125, ALU.mult)
+            ts(v("wi", 16 + j0, 16 + j1), v("wi", j0, j1), 2047, ALU.bitwise_and)
+            copy(v("wU", j0, j1), v("wi", 16 + j0, 16 + j1))
+            copy(v(st, j0, j1), v("wi", 16 + j0, 16 + j1))
+            copy(v("wR", 16 * j0, 16 * j1), ind(v("iot"), v("wU", j0, j1)))
+
+        def equal(j0, j1):
+            ns = OPT["eqS"] if j0 == 0 else 0
+            if ns:
+                act(v("wF", 0, 16 * ns), ind(v("iot"), v("wU", 0, ns)), ACT.Identity)
+                for j in range(ns):
+                    act(v("wA", 16 * j * (j + 1) // 2, 16 * (j + 1) * (j + 2) // 2), v("wF", 0, 16 * j + 16), ACT.Abs,
+                        bias=v(st, j, j + 1), scale=-1.0)
+                for j in range(ns):
+                    act(v3("eq", j, 256 - 16 * j, 272), v("wA", 16 * j * (j + 1) // 2, 16 * (j + 1) * (j + 2) // 2), ACT.Relu,
+                        bias=1.0, scale=-1.0)
+            for j in range(j1 - 1, j0 + ns - 1, -1):
+                ts(v3("eq", j, 256 - 16 * j, 272), v("wR", 0, 16 * j + 16), v(st, j, j + 1), ALU.is_equal)
+
+        for a, b, e in GATHERS:
+            src = ind(v("X"), v("Pu", a, b))
+            if e == "V":
+                copy(v("xg", 16 * a, 16 * b), src)
+            else:
+                act(v("xg", 16 * a, 16 * b), src, ACT.Identity)
+        for i, ch in enumerate(CHUNKS):
+            distances(i)
+            if ch[1] == 128:
+                boost[0] = OPT["boost"][0]
+                ranks(0)
+                boost[0] = OPT["boost"][1]
+                if OPT["early"]:
+                    lists(0, 8, "b6")
+                    equal(0, 8)
+                boost[0] = OPT["boost"][2]
+                own(0)
+                boost[0] = 0.0
+        ranks(1)
+        j0 = 8 if OPT["early"] else 0
+        lists(j0, 16, "b7" if j0 else "b1")
+        send(v("mc%d" % t), "lc%d" % t, "ac%d" % t, hz[t])
+        equal(j0, 16)
+        merge(0)
+        own(1)
+        for h in range(2):
+            copy(ind(v("X"), v("vc", 16 + 8 * h, 24 + 8 * h)), hv("xn", h))
+        if last:
+            dma("Y", T.yx[:], v("X"), 6000)
+        tot = v("b0", 0, 256)
+        mm(tot, m(I), v("thr"), True, False)
+        for j in list(range(j0 - 1, 0, -1)) + list(range(15, max(j0 - 1, 0), -1)):
+            mm(v("b0", 0, 16 * j), m(BOA), v3("eq", j, 256 - 16 * j, 256), False, False)
+        for h in range(2):
+            mm(v("b0", 128 * h, 128 * h + 128), m(BOD),
+               (T.eq[:, 8 * h:8 * h + 8, 256:272], "eq", 272 * 8 * h, 272 * (8 * h + 8), None, 128), False, h == 1)
+        scan(v("sc"), v("rst"), tot, 0.0, ALU.min, ALU.max)
+        tt(v("o1", 0, 16), v("sc", 15, 256, 16), v("cL", 32, 48), ALU.min)
+        tt(v("o1", 16, 32), v("o1", 0, 16), v(st, 0, 16), ALU.max)
+        copy(v("oU"), v("o1", 16, 32))
+        nw = 16 if last else 32
+        tt(v("dd", 0, nw), v("alt", 0, nw), v(st, 0, nw), ALU.subtract)
+        copy(ind(v("B"), v("oU", 0, 8)), hv("Ff", 0))
+        merge(1)
+        amb = v("lc%d" % t)
+        act(v(zn, 0, 256), ind(v(zw), amb), ACT.Identity)
+        ts(v("am", 0, 16), amb, 255.5, ALU.is_gt)
+        if not last:
+            ts(v("am", 16, 32), amb, 255.5, ALU.is_gt)
+        tt(v("dd", 0, nw), v("dd", 0, nw), v("am", 0, nw), ALU.mult)
+        tt(v(sn, 0, nw), v("dd", 0, nw), v(st, 0, nw), ALU.add)
+        if last:
+            dma("Y", T.yz[:], v(zn, 0, 256), 2500)
+            dma("Y", T.yv[:], v(sn, 0, 16), 2500)
+        else:
+            send(v(zn, 0, 256), "zl%d" % (t + 1), "az%d" % (t + 1), hz[t + 1])
+            copy(v("vc"), v(sn))
+        copy(ind(v("B"), v("oU", 8, 16)), hv("Ff", 1))
+    for h in range(2):
+        bank = v("b%d" % h)
+        ts(bank, v("B", 1024 + 512 * h, 1536 + 512 * h), 4096.0, ALU.mult)
+        tt(v("yo", 512 * h, 512 * h + 512), v("B", 512 * h, 512 * h + 512), bank, ALU.add)
+        dma("YS"[h], T.yb[:, 512 * h:512 * h + 512], v("yo", 512 * h, 512 * h + 512), 3000)
+
+    emit(g, T, arrange(ops))
+
+
+def overlap(a, b):
+    if a[3] <= b[2] or b[3] <= a[2]:
+        return False
+    if a[4] is not None and b[4] is not None:
+        return any(k in b[4] for k in a[4])
+    return True
+
+
+def needs(ops):
+    seen, wrote, out = {}, {}, []
+    for i, op in enumerate(ops):
+        q, rd, wr, kind = op[0], op[2], op[3], op[4]
+        need = set()
+        for x, w in [(x, False) for x in rd] + [(x, True) for x in wr]:
+            psum = SCRATCH[x[1]][0] == "psum"
+            hist = (seen if w or psum else wrote).get(x[1], [])
+            for e in range(len(hist) - 1, -1, -1):
+                j, y, wy = hist[e]
+                same = ops[j][0] == q and ops[j][4] == "c" and kind == "c"
+                if psum and (not same or q == "P"):
+                    need.add(j)
+                    if ops[j][0] == "P":
+                        break
+                elif (w or wy) and overlap(x, y):
+                    need.add(j)
+        out.append(need)
+        for x in wr:
+            seen.setdefault(x[1], []).append((i, x, True))
+            wrote.setdefault(x[1], []).append((i, x, True))
+        for x in rd:
+            seen.setdefault(x[1], []).append((i, x, False))
+    return out
+
+
+def arrange(ops):
+    if len(ops) in ORDER:
+        return [ops[i] for i in ORDER[len(ops)]]
+    need = needs(ops)
+    prev = {}
+    for i, op in enumerate(ops):
+        if op[4] == "a":
+            need[i].add(i - 1)
+        if op[4] == "d":
+            if op[0] in prev:
+                need[i].add(-1 - prev[op[0]])
+            prev[op[0]] = i
+    num = len(ops)
+    fwd, bwd = [[] for _ in ops], [[] for _ in ops]
+    for i in range(num):
+        for j in need[i]:
+            if j < 0:
+                j, gap = -1 - j, ops[-1 - j][6]
+            else:
+                gap = ops[j][7] + (0.0 if ops[i][0] == "P" and ops[j][0] == "P" else OPT["hop"])
+            fwd[i].append((j, gap))
+            bwd[j].append((i, gap + ops[i][6] - ops[j][6]))
+    level = [op[7] for op in ops]
+    for i in range(num - 1, -1, -1):
+        for j, gap in fwd[i]:
+            level[j] = max(level[j], level[i] + gap)
+
+    def place(order, before, least):
+        start, busy = [0.0] * num, {}
+        for i in order:
+            t = least[i]
+            for j, gap in before[i]:
+                t = max(t, start[j] + gap)
+            lst = busy.setdefault(ops[i][0], [])
+            lo, hi = 0, len(lst)
+            while lo < hi:
+                mid = (lo + hi) // 2
+                if lst[mid][1] <= t:
+                    lo = mid + 1
+                else:
+                    hi = mid
+            while lo < len(lst) and lst[lo][0] < t + ops[i][6] - 1e-6:
+                t = max(t, lst[lo][1])
+                lo += 1
+            if ops[i][4] != "a":
+                lst.insert(lo, (t, t + ops[i][6]))
+            start[i] = t
+        return start
+    zero, tail = [0.0] * num, [op[7] - op[6] for op in ops]
+    best, seed = None, OPT["seed"]
+    for trial in range(OPT["tries"]):
+        key = list(level)
+        for i in range(num - 1, -1, -1):
+            seed = (seed * 1103515245 + 12345) % 2147483648
+            key[i] = level[i] + ops[i][8] + (OPT["noise"] * seed / 2147483648.0 if trial else 0.0)
+            for j, gap in bwd[i]:
+                key[i] = max(key[i], key[j] + 1e-3)
+        start = place(sorted(range(num), key=lambda e: (-key[e], e)), fwd, zero)
+        for rnd in range(OPT["rounds"] + 1):
+            end = max(start[i] + ops[i][7] for i in range(num))
+            if best is None or end < best[0]:
+                best = (end, start)
+            if rnd < OPT["rounds"]:
+                back = place(sorted(range(num), key=lambda e: (-start[e] - ops[e][6], -e)), bwd, tail)
+                start = place(sorted(range(num), key=lambda e: (-back[e] - ops[e][6], e)), fwd, zero)
+    start = best[1]
+    ORDER[num] = sorted(range(num), key=lambda e: (start[e], e))
+    return [ops[i] for i in ORDER[num]]
+
+
+def emit(g, T, ops):
+    queue = {"V": g.vector, "S": g.scalar, "P": g.tensor, "G": g, "Y": g.sync}
+    know = {q: {} for q in queue}
+    at, waits, pos, count = [], [], [], {}
+    for i, need in enumerate(needs(ops)):
+        q, kind = ops[i][0], ops[i][4]
+        src = q if kind == "c" else ("o", i)
+        count[src] = count.get(src, 0) + 1
+        pos.append((src, count[src]))
+        mine = []
+        if kind != "a":
+            k = know[q]
+            for j in sorted(need, reverse=True):
+                s, p = pos[j]
+                if k.get(s, 0) < p and not (q == "P" and s == "P"):
+                    mine.append(j)
+                    k[s] = p
+                    for s2, p2 in at[j].items():
+                        if k.get(s2, 0) < p2:
+                            k[s2] = p2
+            at.append(dict(k))
+        else:
+            at.append({})
+        waits.append(mine)
+    wanted = set(j for w in waits for j in w)
+    value, n, sent = {}, {}, 0
+    for i, op in enumerate(ops):
+        if op[4] == "c" and i in wanted:
+            n[op[0]] = n.get(op[0], 0) + 1
+            value[i] = ("q" + op[0], n[op[0]])
+        elif op[4] == "d":
+            value[i] = (op[5], 16)
+        elif op[4] == "a":
+            value[i] = op[5]
+    for i, op in enumerate(ops):
+        if op[4] == "a":
+            continue
+        for j in waits[i]:
+            queue[op[0]].wait_ge(T.sem[value[j][0]], value[j][1])
+        ins = op[1]()
+        if op[4] == "r":
+            sent += op[5]
+        elif i in value:
+            ins.then_inc(T.sem[value[i][0]], 16 if op[4] == "d" else 1)
+    g.wait_ge(T.sem.sent, sent)
+    for i, op in enumerate(ops):
+        if op[4] == "d" and i not in wanted:
+            queue[op[0]].wait_ge(T.sem[op[5]], 16)

@@ -97,8 +97,8 @@ SEMAPHORES = ["qV", "qS", "qP", "qG", "sent"] + ["d%d" % _i for _i in range(NDMA
 
 GATHERS = [(0, 64, "V"), (64, 128, "S"), (128, 192, "S"), (192, 256, "S")]
 CHUNKS = [(0, 64), (64, 128), (128, 192), (192, 256)]
-OPT = {"ulay": True, "cmpv": ((False, False), (False, False)), "hlv": (False, False), "early": False,
-       "selS": False, "eqS": 0, "cyc": 1.04, "pe": 0.52, "gat": 1.56, "sca": 3.8, "hop": 70.0, "far": 2600.0,
+OPT = {"fix": 0.0, "parts": 6, "nx": 2, "nb": 2, "ulay": True, "cmpv": ((False, False), (False, False)), "hlv": (False, False), "early": False,
+       "selS": False, "eqS": 0, "cyc": 0.9, "pe": 0.48, "gat": 1.56, "sca": 3.8, "hop": 230.0, "far": 2600.0,
        "seed": 0, "tries": 12, "rounds": 2, "noise": 1000.0, "boost": (0.0, 0.0, 0.0)}
 ORDER = {}
 MAGIC = 12582912.0
@@ -144,7 +144,7 @@ def rank_program(g, core, T, topo):
 
     def add(q, call, outs, ins, cyc, kind="c", extra=None, done=None):
         rd, wr = [], []
-        t = max(64, cyc) * OPT["cyc"] if q != "P" and kind == "c" else cyc
+        t = OPT["fix"] + max(64, cyc) * OPT["cyc"] if q != "P" and kind == "c" else cyc
         for x in ins:
             rd += regs(x)
             if len(regs(x)) == 2:
@@ -579,8 +579,11 @@ def rank_program(g, core, T, topo):
         equal(j0, 16)
         merge(0)
         own(1)
-        for h in range(2):
-            copy(ind(v("X"), v("vc", 16 + 8 * h, 24 + 8 * h)), hv("xn", h))
+        if OPT["nx"] == 1:
+            copy(ind(v("X"), v("vc", 16, 32)), v("xn"))
+        else:
+            for h in range(2):
+                copy(ind(v("X"), v("vc", 16 + 8 * h, 24 + 8 * h)), hv("xn", h))
         if last:
             dma("Y", T.yx[:], v("X"), 6000)
         tot = v("b0", 0, 256)
@@ -596,7 +599,8 @@ def rank_program(g, core, T, topo):
         copy(v("oU"), v("o1", 16, 32))
         nw = 16 if last else 32
         tt(v("dd", 0, nw), v("alt", 0, nw), v(st, 0, nw), ALU.subtract)
-        copy(ind(v("B"), v("oU", 0, 8)), hv("Ff", 0))
+        if OPT["nb"] == 2:
+            copy(ind(v("B"), v("oU", 0, 8)), hv("Ff", 0))
         merge(1)
         amb = v("lc%d" % t)
         act(v(zn, 0, 256), ind(v(zw), amb), ACT.Identity)
@@ -611,7 +615,10 @@ def rank_program(g, core, T, topo):
         else:
             send(v(zn, 0, 256), "zl%d" % (t + 1), "az%d" % (t + 1), hz[t + 1])
             copy(v("vc"), v(sn))
-        copy(ind(v("B"), v("oU", 8, 16)), hv("Ff", 1))
+        if OPT["nb"] == 2:
+            copy(ind(v("B"), v("oU", 8, 16)), hv("Ff", 1))
+        else:
+            copy(ind(v("B"), v("oU")), v("Ff"))
     for h in range(2):
         bank = v("b%d" % h)
         ts(bank, v("B", 1024 + 512 * h, 1536 + 512 * h), 4096.0, ALU.mult)

@@ -7,15 +7,17 @@ ACT = ActivationFunctionType
 SCRATCH = {
     "X": ("sbuf", [128, 4096], "bfloat16"),
     "B": ("sbuf", [128, 2304], "int32"),
+    "Bf": ("sbuf", [128, 2304], "float32"),
+    "xs": ("sbuf", [128, 256], "int32"),
+    "xi": ("sbuf", [128, 256], "int32"),
     "xg": ("sbuf", [128, 4096], "bfloat16"),
     "mx": ("sbuf", [128, 4096], "bfloat16"),
     "Pu": ("sbuf", [128, 256], "uint16"),
-    "Ph": ("sbuf", [128, 256], "float16"),
+    "vR": ("sbuf", [128, 256], "float16"),
     "Uh": ("sbuf", [128, 256], "float16"),
     "Dh": ("sbuf", [128, 256], "float16"),
     "cm": ("sbuf", [128, 1792], "bfloat16"),
     "ys": ("sbuf", [128, 256], "float16"),
-    "hl": ("sbuf", [128, 512], "bfloat16"),
     "sd": ("sbuf", [128, 256], "bfloat16"),
     "Q0": ("sbuf", [128, 256], "bfloat16"),
     "Q1": ("sbuf", [128, 256], "bfloat16"),
@@ -31,16 +33,13 @@ SCRATCH = {
     "sg": ("sbuf", [128, 256], "bfloat16"),
     "xn": ("sbuf", [128, 256], "bfloat16"),
     "av": ("sbuf", [128, 256], "float32"),
-    "wR": ("sbuf", [128, 256], "uint16"),
+    "wR": ("sbuf", [128, 256], "float16"),
     "eq": ("sbuf", [128, 16, 272], "bfloat16"),
     "one": ("sbuf", [128, 2], "bfloat16"),
     "sc": ("sbuf", [128, 256], "float32"),
     "iot": ("sbuf", [128, 2048], "float32"),
-    "wF": ("sbuf", [128, 128], "float32"),
-    "wA": ("sbuf", [128, 576], "float32"),
     "yo": ("sbuf", [128, 1024], "float32"),
     "vc": ("sbuf", [128, 32], "uint16"),
-    "wU": ("sbuf", [128, 16], "uint16"),
     "oU": ("sbuf", [128, 16], "uint16"),
     "v21": ("sbuf", [128, 16], "float32"),
     "wi": ("sbuf", [128, 32], "int32"),
@@ -67,7 +66,7 @@ SCRATCH = {
     "pat": ("sbuf", [128, 14, 16], "bfloat16"),
     "pq": ("sbuf", [128, 224], "bfloat16"),
     "SR": ("sbuf", [128, 14, 128], "bfloat16"),
-    "M": ("sbuf", [128, 19, 128], "bfloat16"),
+    "M": ("sbuf", [128, 21, 128], "bfloat16"),
     "BI": ("sbuf", [128, 128], "float32"),
     "Wi": ("sbuf", [128, 2, 128], "int32"),
     "Wf": ("sbuf", [128, 128], "float32"),
@@ -78,10 +77,11 @@ SCRATCH = {
     "rst": ("sbuf", [128, 256], "float32"),
     "tmp": ("sbuf", [128, 768], "float32"),
 }
-WIDE = True
 for _t in range(RO):
     for _s in ("ma", "mb", "la", "lb"):
-        SCRATCH[_s + str(_t)] = ("sbuf", [128, 128], "float32" if WIDE else "uint16")
+        SCRATCH[_s + str(_t)] = ("sbuf", [128, 256], "bfloat16")
+    SCRATCH["Ph%d" % _t] = ("sbuf", [128, 256], "float16")
+    SCRATCH["pl%d" % _t] = ("sbuf", [128, 256], "float16")
     SCRATCH["mc%d" % _t] = ("sbuf", [128, 16], "uint16")
     SCRATCH["lc%d" % _t] = ("sbuf", [128, 16], "uint16")
     SCRATCH["zl%d" % _t] = ("sbuf", [128, 256], "bfloat16")
@@ -93,13 +93,13 @@ for _b in range(8):
 
 NDMA = 16
 SEMAPHORES = ["qV", "qS", "qP", "qG", "sent"] + ["d%d" % _i for _i in range(NDMA)] \
-    + [_s + str(_t) for _t in range(RO) for _s in ("az", "aa", "ab", "ac")]
+    + [_s + str(_t) for _t in range(RO) for _s in ("az", "aa", "ab", "ac", "ap")]
 
 GATHERS = [(0, 64, "V"), (64, 128, "S"), (128, 192, "S"), (192, 256, "S")]
 CHUNKS = [(0, 64), (64, 128), (128, 192), (192, 256)]
-OPT = {"fix": 0.0, "parts": 6, "nx": 2, "nb": 2, "ulay": True, "cmpv": ((False, False), (False, False)), "hlv": (False, False), "early": False,
-       "selS": False, "eqS": 0, "cyc": 0.9, "pe": 0.48, "gat": 1.56, "sca": 3.8, "hop": 230.0, "far": 2600.0,
-       "seed": 0, "tries": 12, "rounds": 2, "noise": 1000.0, "boost": (0.0, 0.0, 0.0)}
+OPT = {"hib": False, "xv": True, "fix": 0.0, "parts": 6, "nx": 2, "nb": 2, "ulay": True, "cmpv": ((False, False), (False, True)), "hlv": (False, False), "early": False,
+       "selS": False, "eqS": 0, "cyc": 0.9, "pe": 0.5, "gat": 1.56, "sca": 3.8, "hop": 250.0, "far": 3000.0,
+       "seed": 0, "tries": 20, "rounds": 2, "noise": 1000.0, "boost": (0.0, 0.0, 0.0)}
 ORDER = {}
 MAGIC = 12582912.0
 SIZE = {"bfloat16": 2, "float16": 2, "uint16": 2, "float32": 4, "int32": 4}
@@ -213,12 +213,12 @@ def rank_program(g, core, T, topo):
     hn = T.tables.get("HN", [1] * RO)
     hz = T.tables.get("HZ", [1] * RO)
 
-    dma("Y", v("uwi"), T.uw[:], 2000)
-    dma("S", v("zw0", 0, 256), T.z0[:], 2200)
+    dma("S", v("uwi"), T.uw[:], 2000)
     dma("Y", v("v0i"), T.v0[:], 2000)
-    dma("Y", v("B", 0, 2048), T.bag[:], 7000)
-    dma("S", v("X"), T.xt[:], 8000)
-    dma("S", v("bti"), T.bt[:], 3000)
+    dma("S", v("zw0", 0, 256), T.z0[:], 2200)
+    dma("Y", v("bti"), T.bt[:], 2000)
+    dma("Y", v("B", 0, 2048), T.bag[:], 6000)
+    dma("Y", v("X"), T.xt[:], 9000)
 
     ncol = [0]
 
@@ -232,7 +232,7 @@ def rank_program(g, core, T, topo):
     iota(v3("pa", 1), [[1, 7], [1, 16]], 1, 0)
     iota(v("s8i"), [[1, 8], [0, 16]], 0, -1)
     send(v("zw0", 0, 256), "zl0", "az0", hz[0])
-    iota(v("iot"), [[1, 2048]], 0, 0)
+    iota(v("iot"), [[0, 2], [2, 1024]], 1, 0)
 
     cr, cg, ct, c0, c1, cp, cu = col(), col(), col(), col(), col(), col(), col()
     ts(v("coi", 1, 2), v("coi", 0, 1), 15, ALU.bitwise_and)
@@ -241,7 +241,7 @@ def rank_program(g, core, T, topo):
     ts(ct, cg, 15.0, ALU.add)
     ts(c0, cr, 0.0, ALU.is_equal)
     ts(c1, cr, 1.0, ALU.is_ge)
-    I, NBO, IP, NIP, BOP, NBOP, QY, AQ, AQ2, IM, IG, SQ, CQ, IZ, BOA, BOD, IX, IH, NIH = range(19)
+    I, NBO, IP, NIP, BOP, NBOP, QY, AQ, AQ2, IM, IG, SQ, CQ, IZ, BOA, BOD, IX, IH, NIH, FQ, C2 = range(21)
 
     def m(i):
         return v3("M", i)
@@ -305,7 +305,7 @@ def rank_program(g, core, T, topo):
     tt(pa(4), pa(4), pa(2), ALU.add)
     tt(v("pq", 0, 112), pa(4), pa(5), ALU.mult)
     pat = (T.pat[:], "pat", 0, 224, None, 224)
-    dma("Y", pat, v("pq"), 2000)
+    dma("S", pat, v("pq"), 3000)
     for gg in range(8):
         o = (T.SR[:, :, 16 * gg:16 * gg + 16], "SR", 0, 14 * 128, (gg,), 224)
         if gg % 2:
@@ -336,10 +336,15 @@ def rank_program(g, core, T, topo):
     ts(c3, cr, 3.0, ALU.is_equal, -1.0, ALU.mult)
     act(m(CQ), m(NBO), ACT.Identity, scale=c2)
     act(m(SQ), m(NBO), ACT.Identity, scale=c3)
-    ts(cam, ca, 64.0, ALU.mult)
     tt(cfa, c2, c3, ALU.not_equal)
-    ts(cfa, cfa, 0.5, ALU.mult, cam, ALU.add)
-    ts(v3("TT", TAM), v("io144"), ct, ALU.is_equal, cfa, ALU.mult)
+    ts(cfa, cfa, 0.5, ALU.mult)
+    ts(cam, ca, 64.0, ALU.mult, cfa, ALU.add)
+    ts(v3("TT", TAM), v("io144"), ct, ALU.is_equal, cam, ALU.mult)
+    ts(cam, cfa, -1.0, ALU.mult)
+    act(m(FQ), m(NBO), ACT.Identity, scale=cam)
+    c2b = col()
+    ts(c2b, cr, 2.0, ALU.is_equal, 2048.0, ALU.mult)
+    act(m(C2), m(NBO), ACT.Identity, scale=c2b)
     tt(v("BI"), m(NBO), m(I), ALU.add)
     act(v("BI"), v("BI"), ACT.Identity, scale=-1.0)
     memset(v("tmp", 640, 656), 2.0)
@@ -398,21 +403,27 @@ def rank_program(g, core, T, topo):
         z = v(zw, 0, 256)
         Q, Qp = "Q%d" % (t % 2), "Q%d" % ((t + 1) % 2)
         copy(v("Pu"), ind(v("B", 0, 2048), v("vc", 0, 16)))
-        ts(v("Ph"), v("Pu"), -2048.0, ALU.add)
-        mm(v("b4", 0, 256), v("W"), z, True, False)
-        mm(v("b4", 0, 256), m(I), v("Ph"), False, True)
-        ts(v("Hs"), v("b4", 0, 256), 2048.0, ALU.add)
-        ts(v("H"), v("Hs"), 4095, ALU.bitwise_and)
-        tt(v("v21"), v(st, 0, 16), v("cL", 0, 16), ALU.add)
-        act(v("v21"), v("v21"), ACT.Identity, scale=2.0)
-        act(v("old"), ind(v("X"), v("vc", 16, 32)), ACT.Identity)
-        mm(v("b7", 256, 512), m(I), v("old"), True, False)
-        mm(v("b7", 256, 512), m(I), z, False, True)
-        act(v("sg"), v("b7", 256, 512), ACT.Sign, bias=-255.5)
-        mm(v("b7", 256, 512), m(I), v("old"), True, False)
-        mm(v("b7", 256, 512), m(I), z, False, False)
-        mm(v("b7", 256, 512), m(IX), v("sg"), False, True)
-        act(v("xn"), v("b7", 256, 512), ACT.Identity, bias=-128.0)
+        Ph = "Ph%d" % t
+        ts(v(Ph), v("Pu"), -2048.0, ALU.add)
+        send(v(Ph), "pl%d" % t, "ap%d" % t, hn[t])
+        if last:
+            for h in range(4):
+                copy(v("Bf", 512 * h, 512 * h + 512), v("B", 512 * h, 512 * h + 512))
+        copy(v("vR"), ind(v("iot"), v("vc", 0, 16)))
+        if OPT["xv"]:
+            src = ind(v("X"), v("vc", 16, 32))
+            add("V", lambda src=src, z=z: g.vector.tensor_tensor(T.xs[:], src[0], z[0], ALU.add), [v("xs")], [src, z], 256)
+            ts(v("xi"), v("xs"), 255, ALU.bitwise_and)
+        else:
+            act(v("old"), ind(v("X"), v("vc", 16, 32)), ACT.Identity)
+            mm(v("b7", 256, 512), m(I), v("old"), True, False)
+            mm(v("b7", 256, 512), m(I), z, False, True)
+            act(v("sg"), v("b7", 256, 512), ACT.Sign, bias=-255.5)
+            mm(v("b7", 256, 512), m(I), v("old"), True, False)
+            mm(v("b7", 256, 512), m(I), z, False, False)
+            mm(v("b7", 256, 512), m(IX), v("sg"), False, True)
+            act(v("xn"), v("b7", 256, 512), ACT.Identity, bias=-128.0)
+        xn = "xi" if OPT["xv"] else "xn"
         mm(v("b6", 0, 256), m(I), z, True, False)
         mm(v("b6", 0, 256), m(I), v("zl%d" % t), False, True)
         act(v("av"), v("b6", 0, 256), ACT.Identity, bias=MAGIC, scale=0.5 - 2.0 ** -11)
@@ -425,7 +436,12 @@ def rank_program(g, core, T, topo):
             tt(v("alt", 16, 32), v("ui", 16, 32), v("cL", 16, 32), ALU.add)
 
         def hv(name, h, off=0):
+            if name == "Ph":
+                name = Ph
             return v(name, off + 128 * h, off + 128 * h + 128)
+
+        def hl(side, h, i):
+            return v(side + "ab"[h] + str(t), 128 * i, 128 * i + 128)
 
         def distances(i):
             a, b = CHUNKS[i]
@@ -477,69 +493,66 @@ def rank_program(g, core, T, topo):
             else:
                 ts(v(bd, 128, 256), R, coff[h], ALU.is_equal, csg, ALU.mult)
             tt(ys, Dh, v(bd, 128, 256), ALU.mult)
-            qb, hi, lo = v(br, 128, 256), v(bd, 256, 384), v(bd, 384, 512)
+            qb, hi, lo = v(br, 128, 256), v("b%d" % h, 0, 128), v(bd, 384, 512)
+            if OPT["hib"]:
+                hi, lo = v("b%d" % h, 0, 128), v("b%d" % h, 128, 256)
             if t:
                 mm(qb, m(AQ2), hv(Qp, h), True, False)
-            mm(qb, m(QY), ys, t == 0, True)
             for o, mi, mb in ((hi, IP, BOP), (lo, NIP, NBOP)):
                 mm(o, m(mi), Dh, True, False)
                 if t:
                     mm(o, m(AQ), hv(Qp, h), False, False)
                 mm(o, m(mb), ys, False, True)
+            mm(qb, m(QY), ys, t == 0, True)
             act(hv(Q, h), qb, ACT.Sign, bias=v("th", 8 + t, 9 + t))
-            if OPT["hlv"][h]:
-                ts(hv("hl", h), hi, v("th", 12 + t, 13 + t), ALU.is_gt, 2.0, ALU.mult)
-                ts(hv("hl", h, 256), lo, v("th", 16 + t, 17 + t), ALU.is_gt, 2.0, ALU.mult)
-            else:
-                act(hv("hl", h), hi, ACT.Sign, bias=v("th", t, t + 1))
-                act(hv("hl", h, 256), lo, ACT.Sign, bias=v("th", 4 + t, 5 + t))
-            mm(v(br, 256, 384), m(I), hv("Ph", h), True, False)
-            mm(v(br, 256, 384), m(IM), hv("hl", h), False, False)
-            mm(v(br, 256, 384), m(IM), hv("hl", h, 256), False, True)
-            ms = v("m" + "ab"[h] + str(t))
-            if WIDE:
-                act(ms, v(br, 256, 384), ACT.Identity, bias=6144.0 if OPT["hlv"][h] else -2048.0)
-            else:
-                ts(ms, v(br, 256, 384), 10240.0 if OPT["hlv"][h] else 2048.0, ALU.add)
-            send(ms, "l" + "ab"[h] + str(t), "a" + "ab"[h] + str(t), hn[t])
+            act(hl("m", h, 0), hi, ACT.Sign, bias=v("th", t, t + 1))
+            act(hl("m", h, 1), lo, ACT.Sign, bias=v("th", 4 + t, 5 + t))
+            send(v("m" + "ab"[h] + str(t)), "l" + "ab"[h] + str(t), "a" + "ab"[h] + str(t), hn[t])
 
         def own(h):
             bd, R = "b%d" % (2 + h), v("b%d" % (6 + h), 0, 128)
             act(hv("Es", h), R, ACT.Sign, bias=cx[h])
             act(R, R, ACT.Relu, bias=ce[h])
-            mm(v(bd, 0, 128), m(IH), hv("hl", h), True, False)
-            mm(v(bd, 0, 128), m(NIH), hv("hl", h, 256), False, False)
+            mm(v(bd, 0, 128), m(IH), hl("m", h, 0), True, False)
+            mm(v(bd, 0, 128), m(NIH), hl("m", h, 1), False, False)
             mm(v(bd, 0, 128), m(SQ), hv(Q, h), False, True)
             act(hv("sd", h), v(bd, 0, 128), ACT.Abs)
             mm(v(bd, 128, 256), m(I), hv("Ph", h), True, False)
             mm(v(bd, 128, 256), m(CQ), hv(Q, h), False, False)
             mm(v(bd, 128, 256), m(IG), hv("sd", h), False, True)
-            tt(v(bd, 256, 384) if WIDE else hv("Ge", h), hv("H", h), v(bd, 128, 256), ALU.max)
+            tt(hv("Ge", h), hv("H", h), v(bd, 128, 256), ALU.max)
+            mm(v("b%d" % (6 + h), 256, 384), m(I), hv("pl%d" % t, h), True, False)
+            mm(v("b%d" % (6 + h), 256, 384), m(C2), hv(Q, h), False, False)
             mm(v(bd, 384, 512), m(IZ), hv("Es", h), True, False)
 
         def merge(h):
             bd, R = "b%d" % (2 + h), v("b%d" % (6 + h), 0, 128)
-            if WIDE:
-                tt(hv("Fe", h), v("l" + "ab"[h] + str(t)), v(bd, 256, 384), ALU.max)
-            else:
-                ts(v(bd, 256, 384), v("l" + "ab"[h] + str(t), 0, 128), -4096.0, ALU.add)
-                tt(hv("Fe", h), hv("Ge", h), v(bd, 256, 384), ALU.max)
+            mm(v("b%d" % (6 + h), 256, 384), m(IM), hl("l", h, 0), False, False)
+            mm(v("b%d" % (6 + h), 256, 384), m(IM), hl("l", h, 1), False, True)
+            tt(hv("Fe", h), hv("Ge", h), v("b%d" % (6 + h), 256, 384), ALU.max)
             tt(hv("tE", h), hv("Fe", h), R, ALU.mult)
             mm(v(bd, 384, 512), v("BI"), hv("tE", h), False, True)
             tt(hv("Fs", h), hv("Fe", h), v(bd, 384, 512), ALU.max)
             ts(hv("Ff", h), hv("Fs", h), 4095, ALU.bitwise_and)
 
         def lists(j0, j1, bank):
-            y = v(bank, 384, 384 + j1 - j0)
-            mm(y, m(I), v("cLh", j0, j1), True, False)
+            y, kr = v("b5", 0, 16), v("b4", 0, 256)
+            copy(v("wi", 0, 16), v(st, 0, 16))
+            ts(v("wi", 16, 32), v("wi", 0, 16), 1023, ALU.bitwise_and)
+            tt(v("am", 16, 32), v("wi", 16, 32), v("cL", 0, 16), ALU.add)
+            act(v("am", 0, 16), v("am", 16, 32), ACT.Identity, scale=2.0)
+            mm(kr, m(I), v("vR"), True, False)
+            mm(y, m(I), v("cLh"), True, False)
+            mm(kr, m(FQ), v(Q), False, True)
             for p in range(16):
-                mm(y, slide(TAM, p), v(Q, 16 * j0 + p, 16 * j1, 16), False, p == 15)
-            tt(v("wi", j0, j1), v("v21", j0, j1), y, ALU.add)
-            ts(v("mc%d" % t, j0, j1), y, 0.125, ALU.mult)
-            ts(v("wi", 16 + j0, 16 + j1), v("wi", j0, j1), 2047, ALU.bitwise_and)
-            copy(v("wU", j0, j1), v("wi", 16 + j0, 16 + j1))
-            copy(v(st, j0, j1), v("wi", 16 + j0, 16 + j1))
-            copy(v("wR", 16 * j0, 16 * j1), ind(v("iot"), v("wU", j0, j1)))
+                mm(y, slide(TAM, p), v(Q, p, 256, 16), False, p == 15)
+            copy(v("wR"), kr)
+            tt(v("v21"), v("am", 0, 16), y, ALU.add)
+            ts(v("o1", 0, 16), y, 2047.5, ALU.is_gt, 2048.0, ALU.mult)
+            ts(v("mc%d" % t), y, 0.125, ALU.mult)
+            copy(v("wi", 0, 16), v("v21"))
+            ts(v("wi", 16, 32), v("wi", 0, 16), 2047, ALU.bitwise_and)
+            copy(v(st, 0, 16), v("wi", 16, 32))
 
         def equal(j0, j1):
             ns = OPT["eqS"] if j0 == 0 else 0
@@ -552,7 +565,8 @@ def rank_program(g, core, T, topo):
                     act(v3("eq", j, 256 - 16 * j, 272), v("wA", 16 * j * (j + 1) // 2, 16 * (j + 1) * (j + 2) // 2), ACT.Relu,
                         bias=1.0, scale=-1.0)
             for j in range(j1 - 1, j0 + ns - 1, -1):
-                ts(v3("eq", j, 256 - 16 * j, 272), v("wR", 0, 16 * j + 16), v(st, j, j + 1), ALU.is_equal)
+                ts(v3("eq", j, 256 - 16 * j, 272), v("wR", 0, 16 * j + 16), v("o1", j, j + 1), ALU.add,
+                   v("v21", j, j + 1), ALU.is_equal)
 
         for a, b, e in GATHERS:
             src = ind(v("X"), v("Pu", a, b))
@@ -562,6 +576,12 @@ def rank_program(g, core, T, topo):
                 act(v("xg", 16 * a, 16 * b), src, ACT.Identity)
         for i, ch in enumerate(CHUNKS):
             distances(i)
+            if i == 0:
+                mm(v("b7", 256, 512), v("W"), z, True, False)
+                mm(v("b7", 256, 512), m(I), v(Ph), False, True)
+                ts(v("Hs"), v("b7", 256, 512), 2048.0, ALU.add)
+                ts(v("H"), v("Hs"), 4095, ALU.bitwise_and)
+        for i, ch in enumerate(CHUNKS):
             if ch[1] == 128:
                 boost[0] = OPT["boost"][0]
                 ranks(0)
@@ -580,10 +600,10 @@ def rank_program(g, core, T, topo):
         merge(0)
         own(1)
         if OPT["nx"] == 1:
-            copy(ind(v("X"), v("vc", 16, 32)), v("xn"))
+            copy(ind(v("X"), v("vc", 16, 32)), v(xn))
         else:
             for h in range(2):
-                copy(ind(v("X"), v("vc", 16 + 8 * h, 24 + 8 * h)), hv("xn", h))
+                copy(ind(v("X"), v("vc", 16 + 8 * h, 24 + 8 * h)), hv(xn, h))
         if last:
             dma("Y", T.yx[:], v("X"), 6000)
         tot = v("b0", 0, 256)
@@ -600,7 +620,7 @@ def rank_program(g, core, T, topo):
         nw = 16 if last else 32
         tt(v("dd", 0, nw), v("alt", 0, nw), v(st, 0, nw), ALU.subtract)
         if OPT["nb"] == 2:
-            copy(ind(v("B"), v("oU", 0, 8)), hv("Ff", 0))
+            copy(ind(v("Bf" if last else "B"), v("oU", 0, 8)), hv("Ff", 0))
         merge(1)
         amb = v("lc%d" % t)
         act(v(zn, 0, 256), ind(v(zw), amb), ACT.Identity)
@@ -616,14 +636,18 @@ def rank_program(g, core, T, topo):
             send(v(zn, 0, 256), "zl%d" % (t + 1), "az%d" % (t + 1), hz[t + 1])
             copy(v("vc"), v(sn))
         if OPT["nb"] == 2:
-            copy(ind(v("B"), v("oU", 8, 16)), hv("Ff", 1))
+            copy(ind(v("Bf" if last else "B"), v("oU", 8, 16)), hv("Ff", 1))
         else:
-            copy(ind(v("B"), v("oU")), v("Ff"))
-    for h in range(2):
-        bank = v("b%d" % h)
-        ts(bank, v("B", 1024 + 512 * h, 1536 + 512 * h), 4096.0, ALU.mult)
-        tt(v("yo", 512 * h, 512 * h + 512), v("B", 512 * h, 512 * h + 512), bank, ALU.add)
-        dma("YS"[h], T.yb[:, 512 * h:512 * h + 512], v("yo", 512 * h, 512 * h + 512), 3000)
+            copy(ind(v("Bf" if last else "B"), v("oU")), v("Ff"))
+    for h in range(4):
+        bank = v("b%d" % h, 0, 256)
+        if h:
+            act(bank, v("Bf", 1024 + 256 * h, 1280 + 256 * h), ACT.Identity, scale=4096.0)
+        else:
+            ts(bank, v("Bf", 1024, 1280), 4096.0, ALU.mult)
+        tt(v("yo", 256 * h, 256 * h + 256), v("Bf", 256 * h, 256 * h + 256), bank, ALU.add)
+        if h % 2:
+            dma("YS"[h // 2], T.yb[:, 256 * h - 256:256 * h + 256], v("yo", 256 * h - 256, 256 * h + 256), 3000)
 
     emit(g, T, arrange(ops))
 

@@ -1,4 +1,4 @@
-from concourse.mybir import AluOpType, AxisListType, ActivationFunctionType
+from concourse.mybir import AluOpType, ActivationFunctionType
 
 RO = 4
 ALU = AluOpType
@@ -10,17 +10,17 @@ SCRATCH = {
     "Bf": ("sbuf", [128, 2304], "float32"),
     "xs": ("sbuf", [128, 256], "int32"),
     "xi": ("sbuf", [128, 256], "int32"),
-    "xg": ("sbuf", [128, 4096], "bfloat16"),
-    "mx": ("sbuf", [128, 4096], "bfloat16"),
+    "xm": ("sbuf", [128, 8192], "bfloat16"),
     "Pu": ("sbuf", [128, 256], "uint16"),
     "vR": ("sbuf", [128, 256], "float16"),
-    "Uh": ("sbuf", [128, 256], "float16"),
+    "Uh": ("sbuf", [128, 512], "float16"),
     "Dh": ("sbuf", [128, 256], "float16"),
     "cm": ("sbuf", [128, 1792], "bfloat16"),
     "ys": ("sbuf", [128, 256], "float16"),
     "sd": ("sbuf", [128, 256], "bfloat16"),
     "Q0": ("sbuf", [128, 256], "bfloat16"),
     "Q1": ("sbuf", [128, 256], "bfloat16"),
+    "Qi": ("sbuf", [128, 128], "bfloat16"),
     "Es": ("sbuf", [128, 256], "bfloat16"),
     "Hs": ("sbuf", [128, 256], "int32"),
     "H": ("sbuf", [128, 256], "int32"),
@@ -33,73 +33,84 @@ SCRATCH = {
     "sg": ("sbuf", [128, 256], "bfloat16"),
     "xn": ("sbuf", [128, 256], "bfloat16"),
     "av": ("sbuf", [128, 256], "float32"),
-    "wR": ("sbuf", [128, 256], "float16"),
-    "eq": ("sbuf", [128, 16, 272], "bfloat16"),
-    "one": ("sbuf", [128, 2], "bfloat16"),
-    "sc": ("sbuf", [128, 256], "float32"),
+    "ks": ("sbuf", [128, 256], "float32"),
+    "wR": ("sbuf", [128, 16, 17], "float16"),
+    "eq": ("sbuf", [128, 16, 136], "bfloat16"),
+    "ab": ("sbuf", [128, 16, 136], "bfloat16"),
+    "sc": ("sbuf", [128, 272], "float32"),
     "iot": ("sbuf", [128, 2048], "float32"),
     "yo": ("sbuf", [128, 1024], "float32"),
     "vc": ("sbuf", [128, 32], "uint16"),
     "oU": ("sbuf", [128, 16], "uint16"),
-    "v21": ("sbuf", [128, 16], "float32"),
-    "wi": ("sbuf", [128, 32], "int32"),
     "ui": ("sbuf", [128, 32], "int32"),
     "alt": ("sbuf", [128, 32], "int32"),
-    "dd": ("sbuf", [128, 32], "float32"),
-    "am": ("sbuf", [128, 32], "float32"),
-    "o1": ("sbuf", [128, 32], "float32"),
+    "am": ("sbuf", [128, 64], "float32"),
+    "vo": ("sbuf", [128, 16], "float32"),
     "v0i": ("sbuf", [128, 16], "int32"),
     "uwi": ("sbuf", [128, 1], "int32"),
     "bti": ("sbuf", [8, 4], "int32"),
     "btb": ("sbuf", [8, 4], "bfloat16"),
     "s8": ("sbuf", [8, 128], "bfloat16"),
-    "s8i": ("sbuf", [8, 128], "float32"),
-    "th": ("sbuf", [128, 20], "float32"),
-    "col": ("sbuf", [128, 40], "float32"),
+    "th": ("sbuf", [128, 8], "float32"),
+    "col": ("sbuf", [128, 32], "float32"),
+    "oh": ("sbuf", [128, 24], "float32"),
     "coi": ("sbuf", [128, 2], "int32"),
-    "io144": ("sbuf", [128, 144], "float32"),
-    "i16": ("sbuf", [128, 256], "float32"),
-    "cL": ("sbuf", [128, 48], "float32"),
+    "io": ("sbuf", [128, 144], "bfloat16"),
+    "i16": ("sbuf", [128, 128], "bfloat16"),
+    "blk": ("sbuf", [128, 128], "bfloat16"),
+    "i17": ("sbuf", [128, 272], "bfloat16"),
+    "cL": ("sbuf", [128, 16], "float32"),
     "cLh": ("sbuf", [128, 16], "float16"),
     "g8": ("sbuf", [128, 16], "bfloat16"),
-    "pa": ("sbuf", [128, 6, 112], "float32"),
-    "pat": ("sbuf", [128, 14, 16], "bfloat16"),
+    "pa": ("sbuf", [128, 6, 112], "bfloat16"),
+    "pb": ("sbuf", [128, 64], "bfloat16"),
     "pq": ("sbuf", [128, 224], "bfloat16"),
     "SR": ("sbuf", [128, 14, 128], "bfloat16"),
-    "M": ("sbuf", [128, 21, 128], "bfloat16"),
+    "SP": ("sbuf", [128, 1792], "bfloat16"),
+    "M": ("sbuf", [128, 16, 128], "bfloat16"),
     "BI": ("sbuf", [128, 128], "float32"),
-    "Wi": ("sbuf", [128, 2, 128], "int32"),
-    "Wf": ("sbuf", [128, 128], "float32"),
+    "R2": ("sbuf", [128, 64], "bfloat16"),
+    "Wi": ("sbuf", [128, 32], "int32"),
+    "Wf": ("sbuf", [128, 32], "float32"),
     "W": ("sbuf", [128, 128], "float16"),
-    "TT": ("sbuf", [128, 4, 144], "bfloat16"),
+    "TT": ("sbuf", [128, 3, 144], "bfloat16"),
     "Tu": ("sbuf", [128, 144], "float16"),
-    "thr": ("sbuf", [128, 256], "bfloat16"),
-    "rst": ("sbuf", [128, 256], "float32"),
-    "tmp": ("sbuf", [128, 768], "float32"),
+    "ne": ("sbuf", [128, 272], "bfloat16"),
+    "thr": ("sbuf", [128, 272], "bfloat16"),
+    "rst": ("sbuf", [128, 272], "float32"),
+    "mk": ("sbuf", [128, 128], "bfloat16"),
+    "rs": ("sbuf", [128, 128], "float32"),
 }
 for _t in range(RO):
-    for _s in ("ma", "mb", "la", "lb"):
-        SCRATCH[_s + str(_t)] = ("sbuf", [128, 256], "bfloat16")
+    SCRATCH["ms%d" % _t] = ("sbuf", [128, 512], "bfloat16")
     SCRATCH["Ph%d" % _t] = ("sbuf", [128, 256], "float16")
     SCRATCH["pl%d" % _t] = ("sbuf", [128, 256], "float16")
     SCRATCH["mc%d" % _t] = ("sbuf", [128, 16], "uint16")
     SCRATCH["lc%d" % _t] = ("sbuf", [128, 16], "uint16")
     SCRATCH["zl%d" % _t] = ("sbuf", [128, 256], "bfloat16")
+    SCRATCH["ls%d" % _t] = ("sbuf", [128, 512], "bfloat16")
 for _t in range(RO + 1):
     SCRATCH["zw%d" % _t] = ("sbuf", [128, 512], "bfloat16")
-    SCRATCH["st%d" % _t] = ("sbuf", [128, 32], "float32")
+    SCRATCH["ds%d" % _t] = ("sbuf", [128, 64], "float32")
 for _b in range(8):
     SCRATCH["b%d" % _b] = ("psum", [128, 512], "float32")
 
 NDMA = 16
 SEMAPHORES = ["qV", "qS", "qP", "qG", "sent"] + ["d%d" % _i for _i in range(NDMA)] \
-    + [_s + str(_t) for _t in range(RO) for _s in ("az", "aa", "ab", "ac", "ap")]
+    + [_s + str(_t) for _t in range(RO) for _s in ("az", "ac", "ap", "aa", "ab", "ad", "ae")]
 
-GATHERS = [(0, 64, "V"), (64, 128, "S"), (128, 192, "S"), (192, 256, "S")]
-CHUNKS = [(0, 64), (64, 128), (128, 192), (192, 256)]
-OPT = {"hib": False, "xv": True, "fix": 0.0, "parts": 6, "nx": 2, "nb": 2, "ulay": True, "cmpv": ((False, False), (False, True)), "hlv": (False, False), "early": False,
-       "selS": False, "eqS": 0, "cyc": 0.9, "pe": 0.5, "gat": 1.56, "sca": 3.8, "hop": 250.0, "far": 3000.0,
-       "seed": 0, "tries": 20, "rounds": 2, "noise": 1000.0, "boost": (0.0, 0.0, 0.0)}
+OPT = {
+    "units": [(0, 96, 1, "4SV", "222222011"), (96, 192, 1, "4SV", "333333455"), (192, 256, 0, "4SV", "667645071")],
+    "bags": [(0, 64), (64, 256)],
+    "gathers": [(0, 32, "S"), (32, 80, "V"), (80, 96, "S"), (96, 144, "S"), (144, 192, "S"), (192, 224, "S"), (224, 256, "S")],
+    "chunks": [(0, 32), (32, 96), (96, 144), (144, 192), (192, 224), (224, 256)],
+    "aside": "677", "yb": "5",
+    "order": "d0 a1 a0 d1 d2 d3 d4 d5 r0 r1 r2 y0 a2 s0 o0 s1 o1 s2 o2 m0 m1 m2",
+    "eqS": (2, 2, 0, 0), "rep": (2, 2, 2, 2, 2, 2, 2, 2), "xmode": 0, "nx": 2, "bint": True,
+    "onS": ("vR", "wR", "w", "oU", "mc", "ui", "Dh2"),
+    "loads": (5000, 8000), "seed": 1, "tries": 3000}
+COSTS = [(0.87, 0.45, 1.56, 3.8, 230.0, 2200.0, 300.0, 1.0), (1.15, 0.58, 1.9, 5.0, 200.0, 2500.0, 400.0, 1.1),
+         (0.85, 0.43, 1.2, 2.5, 320.0, 3200.0, 600.0, 0.8)]
 ORDER = {}
 MAGIC = 12582912.0
 SIZE = {"bfloat16": 2, "float16": 2, "uint16": 2, "float32": 4, "int32": 4}
@@ -111,7 +122,8 @@ def rank_program(g, core, T, topo):
         return
     n = len(T.cores)
     ops = []
-    boost = [0.0]
+    now = [""]
+    units = OPT["units"]
 
     def v(name, a=None, b=None, s=None, keys=None):
         w = SCRATCH[name][1][-1]
@@ -120,14 +132,26 @@ def rank_program(g, core, T, topo):
         ap_ = T[name][:, lo:hi] if s is None else T[name][:, lo:hi:s]
         return (ap_, name, lo, hi, keys, len(range(lo, hi, s or 1)))
 
+    def vp(name, p0, p1, a, b, s=1):
+        return (T[name][p0:p1, a:b:s], name, a, b, None, len(range(a, b, s)))
+
     def v3(name, i0, a=None, b=None):
         w = SCRATCH[name][1][-1]
         lo = 0 if a is None else a
         hi = w if b is None else b
         return (T[name][:, i0, lo:hi], name, i0 * w + lo, i0 * w + hi, None, hi - lo)
 
+    def vs(name, i0, i1, a, b):
+        w = SCRATCH[name][1][-1]
+        return (T[name][:, i0:i1, a:b], name, i0 * w + a, (i1 - 1) * w + b, None, (i1 - i0) * (b - a))
+
     def vk(name, a, b, k, step=16):
-        return v(name, 16 * a + k, 16 * b, step, tuple(range(k, 16, step)))
+        ua, ub = [u[:2] for u in units if u[0] <= a < u[1]][0]
+        o = 16 * (ub if name == "mx" else ua)
+        return v("xm", o + 16 * a + k, o + 16 * b, step, tuple(range(k, 16, step)))
+
+    def both(a, b, k):
+        return v("xm", 32 * a + k, 32 * b, 16, (k,))
 
     def ind(win, off):
         return (win[0].indirect(off[0]), win, off)
@@ -135,38 +159,35 @@ def rank_program(g, core, T, topo):
     def regs(x):
         if not isinstance(x, tuple):
             return []
-        if isinstance(x[1], tuple):
-            return [x[1], x[2]]
-        return [x]
+        return [x[1], x[2]] if len(x) == 3 else [x]
 
     def ap(x):
         return x[0] if isinstance(x, tuple) else x
 
-    def add(q, call, outs, ins, cyc, kind="c", extra=None, done=None):
+    def add(q, call, outs, ins, cost, kind="c", extra=None):
         rd, wr = [], []
-        t = OPT["fix"] + max(64, cyc) * OPT["cyc"] if q != "P" and kind == "c" else cyc
         for x in ins:
             rd += regs(x)
             if len(regs(x)) == 2:
-                t = 70 + 16 * x[2][5] * OPT["gat"] * OPT["cyc"]
+                cost = ("g", 16 * x[2][5])
         for x in outs:
             r = regs(x)
             wr.append(r[0])
             rd += r[1:]
             if len(r) == 2:
-                t = 70 + 16 * x[2][5] * OPT["sca"] * OPT["cyc"]
-        ops.append((q, call, rd, wr, kind, extra, t, done or t, boost[0]))
+                cost = ("s", 16 * x[2][5])
+        ops.append((q, call, rd, wr, kind, extra, now[0], cost))
 
-    def cnt(out, a):
-        x, y = regs(out)[0], regs(a)[0]
-        return x[5] * (0.5 if SIZE[SCRATCH[x[1]][2]] == 2 and SIZE[SCRATCH[y[1]][2]] == 2 else 1)
+    def cnt(out, *ins):
+        two = all(SIZE[SCRATCH[regs(x)[0][1]][2]] == 2 for x in (out,) + ins)
+        return ("v", regs(out)[0][5] * (0.5 if two else 1))
 
     def copy(out, in_):
         add("V", lambda: g.vector.tensor_copy(ap(out), ap(in_)), [out], [in_], cnt(out, in_))
 
     def tt(out, a, b, op):
-        two = 1 if "psum" in (SCRATCH[a[1]][0], SCRATCH[b[1]][0]) else 2
-        add("V", lambda: g.vector.tensor_tensor(ap(out), ap(a), ap(b), op), [out], [a, b], two * out[5])
+        two = 1 if "psum" in (SCRATCH[regs(a)[0][1]][0], SCRATCH[b[1]][0]) else 2
+        add("V", lambda: g.vector.tensor_tensor(ap(out), ap(a), ap(b), op), [out], [a, b], ("v", two * b[5]))
 
     def ts(out, a, s1, op0, s2=None, op1=None):
         if op1 is None:
@@ -175,40 +196,54 @@ def rank_program(g, core, T, topo):
             add("V", lambda: g.vector.tensor_scalar(ap(out), ap(a), ap(s1), ap(s2), op0, op1), [out], [a, s1, s2], cnt(out, a))
 
     def scan(out, d0, d1, init, op0, op1):
-        add("V", lambda: g.vector.tensor_tensor_scan(ap(out), ap(d0), ap(d1), init, op0, op1), [out], [d0, d1], out[5])
+        add("V", lambda: g.vector.tensor_tensor_scan(ap(out), ap(d0), ap(d1), init, op0, op1), [out], [d0, d1], ("v", out[5]))
 
     def memset(out, c_):
-        add("V", lambda: g.vector.memset(ap(out), c_), [out], [], out[5])
+        add("V", lambda: g.vector.memset(ap(out), c_), [out], [], ("v", out[5]))
 
-    def act(out, a, f, bias=0.0, scale=1.0):
-        add("S", lambda: g.scalar.activation(ap(out), ap(a), f, bias=ap(bias), scale=ap(scale)), [out], [a, bias, scale], out[5])
+    def act(out, a, f=ACT.Identity, bias=0.0, scale=1.0):
+        add("S", lambda: g.scalar.activation(ap(out), ap(a), f, bias=ap(bias), scale=ap(scale)), [out], [a, bias, scale],
+            ("v", out[5]))
+
+    def move(what, out, a, bias=0.0):
+        if what in OPT["onS"]:
+            act(out, a, bias=bias)
+        elif bias:
+            ts(out, a, bias, ALU.add)
+        else:
+            copy(out, a)
 
     def mm(out, l, r, start, stop):
-        t = max(min(64, l[5]), r[5]) * OPT["pe"] * (4 if SCRATCH[l[1]][2] == "float32" else 1)
-        add("P", lambda: g.tensor.matmul(ap(out), ap(l), ap(r), start, stop), [out], [l, r], t)
+        c_ = max(min(64, l[5]), r[5]) * (4 if SCRATCH[r[1]][2] == "float32" else 1)
+        add("P", lambda: g.tensor.matmul(ap(out), ap(l), ap(r), start, stop), [out], [l, r], ("p", c_))
+
+    def group(terms):
+        for i, (o, l, r) in enumerate(terms):
+            mm(o, l, r, i == 0, i == len(terms) - 1)
 
     def iota(out, pattern, base, cmul):
         if SCRATCH[out[1]][2] == "int32":
-            add("G", lambda: g.iota(ap(out), pattern, base, cmul), [out], [], 160 + 2 * out[5])
+            add("G", lambda: g.iota(ap(out), pattern, base, cmul), [out], [], ("x", 2 * out[5]))
         else:
-            add("G", lambda: g.iota(ap(out), pattern, base, cmul, allow_small_or_imprecise_dtypes=True), [out], [], 160 + 2 * out[5])
+            add("G", lambda: g.iota(ap(out), pattern, base, cmul, allow_small_or_imprecise_dtypes=True), [out], [],
+                ("x", 2 * out[5]))
 
     ndma = [0]
 
     def dma(q, out, in_, done):
         eng = g.sync if q == "Y" else g.scalar
-        add(q, lambda: eng.dma_start(ap(out), ap(in_)), [out] if isinstance(out, tuple) else [], [in_], 100, "d",
-            "d%d" % ndma[0], done)
+        add(q, lambda: eng.dma_start(ap(out), ap(in_)), [out] if isinstance(out, tuple) else [], [in_], ("d", done), "d",
+            "d%d" % ndma[0])
         ndma[0] += 1
 
     def send(src, dst, sem, hop):
         to = T.cores[(rank + hop) % n]
         rid, pid, _ = topo.addr(to)
         mask = topo.mask(core, to)
-        add("G", lambda: g.remote_dma(T[dst][:], ap(src), T.sem[sem], T.sem.sent, pid, rid, mask), [], [src], 300, "r",
-            len(topo.engines(core, to)), OPT["far"])
+        add("G", lambda: g.remote_dma(ap(dst), ap(src), T.sem[sem], T.sem.sent, pid, rid, mask), [], [src],
+            ("r", src[5]), "r", (sem, len(topo.engines(core, to))))
         frm = T.cores[(rank - hop) % n]
-        add("X", None, [v(dst)], [], 0, "a", (sem, len(topo.engines(frm, core))))
+        add("X", None, [dst], [], ("a", 0), "a", (sem, len(topo.engines(frm, core))))
 
     hn = T.tables.get("HN", [1] * RO)
     hz = T.tables.get("HZ", [1] * RO)
@@ -217,435 +252,363 @@ def rank_program(g, core, T, topo):
     dma("Y", v("v0i"), T.v0[:], 2000)
     dma("S", v("zw0", 0, 256), T.z0[:], 2200)
     dma("Y", v("bti"), T.bt[:], 2000)
-    dma("Y", v("B", 0, 2048), T.bag[:], 6000)
-    dma("Y", v("X"), T.xt[:], 9000)
+    dma("Y", v("B", 256, 2304), T.bag[:], OPT["loads"][0])
+    dma("Y", v("X"), T.xt[:], OPT["loads"][1])
 
+    now[0] = "c"
+    iota(v("coi", 0, 1), [[1, 1]], 0, 1)
+    iota(v("io"), [[1, 144]], 0, 0)
+    iota(v("i16"), [[0, 8], [1, 16]], 0, 0)
+    iota(v("blk"), [[16, 8], [0, 16]], 0, 0)
+    iota(v3("pa", 0), [[1, 7], [1, 16]], 1, 0)
+    send(v("zw0", 0, 256), v("zl0"), "az0", hz[0])
+    iota(v("i17"), [[0, 16], [1, 17]], 0, 0)
+    iota(v("rst"), [[0, 272]], 8000000, 0)
+    iota(v("rs"), [[0, 128]], 8000000, 0)
+    for h in range(2):
+        iota(v("iot", 1024 * h, 1024 * h + 1024), [[2, 1024]], -1023, 0)
     ncol = [0]
 
-    def col():
+    def col(src=None, scale=1.0, bias=0.0):
         ncol[0] += 1
-        return v("col", ncol[0] - 1, ncol[0])
-    iota(v("io144"), [[1, 144]], 0, 0)
-    iota(v("coi", 0, 1), [[1, 1]], 0, 1)
-    iota(v("i16"), [[0, 16], [1, 16]], 0, 0)
-    iota(v3("pa", 0), [[-1, 7], [1, 16]], -1, 0)
-    iota(v3("pa", 1), [[1, 7], [1, 16]], 1, 0)
-    iota(v("s8i"), [[1, 8], [0, 16]], 0, -1)
-    send(v("zw0", 0, 256), "zl0", "az0", hz[0])
-    iota(v("iot"), [[0, 2], [2, 1024]], 1, 0)
+        c_ = v("col", ncol[0] - 1, ncol[0])
+        if src is not None:
+            act(c_, src, bias=bias, scale=scale)
+        return c_
 
-    cr, cg, ct, c0, c1, cp, cu = col(), col(), col(), col(), col(), col(), col()
+    def row(k):
+        return v("oh", k, k + 1)
+
+    def own16(gg):
+        return v("oh", 16 + gg, 17 + gg)
+    cr, cg, cp, c16 = col(), col(), col(), col()
     ts(v("coi", 1, 2), v("coi", 0, 1), 15, ALU.bitwise_and)
+    copy(cp, v("coi", 0, 1))
     copy(cr, v("coi", 1, 2))
-    tt(cg, v("coi", 0, 1), cr, ALU.subtract)
-    ts(ct, cg, 15.0, ALU.add)
-    ts(c0, cr, 0.0, ALU.is_equal)
-    ts(c1, cr, 1.0, ALU.is_ge)
-    I, NBO, IP, NIP, BOP, NBOP, QY, AQ, AQ2, IM, IG, SQ, CQ, IZ, BOA, BOD, IX, IH, NIH, FQ, C2 = range(21)
+    tt(cg, v("coi", 0, 1), v("coi", 1, 2), ALU.subtract)
+    ct = col(cg, bias=15.0)
+    i16 = v("i16", 0, 16)
+    ts(v("oh", 0, 16), i16, cr, ALU.is_equal)
+    ts(v("oh", 16, 24), v("blk", 0, 128, 16), cg, ALU.is_equal)
+    ts(c16, cr, 1.5, ALU.is_lt, 16.0, ALU.mult)
+    I, NBO, IP, NIP, BOP, NBOP, IM, IG, SQ, CQ, IZ, BOA, IH, NIH, FQ, C2 = range(16)
+    AQ, AH, AL, QY, VQ, BOD, BIB = range(7, 14)
+    T2, TM1, TAM = range(3)
 
     def m(i):
         return v3("M", i)
-    copy(cp, v("coi", 0, 1))
-    ts(m(I), v("io144", 0, 128), cp, ALU.is_equal)
-    ts(v("tmp", 0, 128), v("io144", 0, 128), cg, ALU.is_ge)
-    ts(v("tmp", 128, 256), v("io144", 0, 128), ct, ALU.is_le, -1.0, ALU.mult)
-    tt(m(NBO), v("tmp", 0, 128), v("tmp", 128, 256), ALU.mult)
-    T2, TM1, TAM, TFA = range(4)
-    gsel = v("col", 32, 40)
-    ts(gsel, v("io144", 0, 8), 16.0, ALU.mult, cg, ALU.is_equal)
-    if OPT["ulay"]:
-        ts(v("g8", 0, 8), gsel, 2.0, ALU.mult)
-        ts(v("g8", 8, 16), gsel, -1.0, ALU.mult)
-    else:
-        ts(v3("TT", T2), v("io144"), ct, ALU.is_equal, 2.0, ALU.mult)
-        ts(v3("TT", TM1), v("io144"), ct, ALU.is_equal, -1.0, ALU.mult)
-    copy(cu, v("uwi"))
-    ts(v("Wf"), v("i16", 0, 128), 2.0, ALU.mult, 1.0, ALU.add)
-    ts(v3("Wi", 0), v("Wf"), cu, ALU.mult, 2048.0, ALU.add)
-    ts(v3("Wi", 1), v3("Wi", 0), 4095, ALU.bitwise_and)
-    ts(v("Wf"), v3("Wi", 1), -1.0, ALU.mult, 2048.0, ALU.add)
-    tt(v("W"), v("Wf"), m(NBO), ALU.mult)
-    ts(cu, v("Wf", 0, 1), -1.0, ALU.mult)
-    ts(v("Tu"), v("io144"), ct, ALU.is_equal, cu, ALU.mult)
-    ts(v("cL", 0, 16), v("io144", 0, 16), 16.0, ALU.mult, cr, ALU.add)
-    ts(v("cL", 16, 32), v("cL", 0, 16), 16.0, ALU.mult)
-    ts(v("cL", 32, 48), v("cL", 0, 16), 2048.0, ALU.add)
-    ts(v("cLh"), v("cL", 0, 16), 8.0, ALU.mult)
-    ts(v("cL", 0, 16), v("cL", 0, 16), -4.0, ALU.mult, 0.5, ALU.add)
-
-    def ulist(zv, bank):
-        for p in range(16):
-            mm(bank, v("Tu", 15 - p, 143 - p), v(zv[1], zv[2] + p, zv[3], 16), p == 0, p == 15)
-
-    ulist(v("zw0", 0, 256), v("b6", 0, 16))
-    copy(v("st0", 0, 16), v("v0i"))
-    copy(v("vc", 0, 16), v("v0i"))
-    copy(v("ui", 0, 16), v("b6", 0, 16))
-    ts(v("ui", 16, 32), v("ui", 0, 16), 15, ALU.bitwise_and)
-    tt(v("st0", 16, 32), v("ui", 16, 32), v("cL", 16, 32), ALU.add)
-    copy(v("vc", 16, 32), v("st0", 16, 32))
-
-    def pa(i):
-        return v3("pa", i)
-    cm15, cp15 = col(), col()
-    ts(cm15, cr, -15.0, ALU.add)
-    ts(pa(2), pa(1), 15.5, ALU.is_lt, 0.5, ALU.subtract)
-    ts(pa(3), v("i16", 0, 112), cr, ALU.is_equal, -2.0, ALU.mult)
-    tt(pa(2), pa(2), pa(3), ALU.mult)
-    ts(pa(3), pa(0), cr, ALU.is_equal)
-    ts(pa(4), pa(0), cm15, ALU.is_equal)
-    tt(pa(3), pa(3), pa(4), ALU.subtract)
-    tt(pa(3), pa(3), pa(2), ALU.add)
-    ts(pa(5), v("i16", 0, 112), 1.0, ALU.is_ge, c1, ALU.mult)
-    tt(v("pq", 112, 224), pa(3), pa(5), ALU.mult)
-    ts(cp15, cr, 15.0, ALU.add)
-    ts(pa(4), pa(1), cr, ALU.is_equal)
-    ts(pa(0), pa(1), cp15, ALU.is_equal)
-    tt(pa(4), pa(4), pa(0), ALU.subtract)
-    tt(pa(4), pa(4), pa(2), ALU.add)
-    tt(v("pq", 0, 112), pa(4), pa(5), ALU.mult)
-    pat = (T.pat[:], "pat", 0, 224, None, 224)
-    dma("S", pat, v("pq"), 3000)
-    for gg in range(8):
-        o = (T.SR[:, :, 16 * gg:16 * gg + 16], "SR", 0, 14 * 128, (gg,), 224)
-        if gg % 2:
-            act(o, pat, ACT.Identity, scale=v("col", 32 + gg, 33 + gg))
-        else:
-            ts(o, pat, v("col", 32 + gg, 33 + gg), ALU.mult)
-    act(m(IP), m(I), ACT.Identity, scale=c1)
-    act(m(NIP), m(IP), ACT.Identity, scale=-1.0)
-    act(m(NBOP), m(NBO), ACT.Identity, scale=c1)
-    act(m(BOP), m(NBOP), ACT.Identity, scale=-1.0)
-    act(m(IM), m(I), ACT.Identity, scale=-4096.0)
-    act(m(IG), m(I), ACT.Identity, scale=16384.0)
-    act(m(IZ), m(I), ACT.Identity, scale=32768.0)
-    act(m(IX), m(I), ACT.Identity, scale=-128.0)
-    act(m(IH), m(I), ACT.Identity, scale=0.5)
-    act(m(NIH), m(I), ACT.Identity, scale=-0.5)
-    act(m(BOA), m(NBO), ACT.Identity, scale=-float(2 ** 28))
-    ca, c2, c3, cam, cfa, c12, c13, c14, c15, c16, csg, ce0 = [col() for _ in range(12)]
-    ts(ca, cr, 1.5, ALU.is_lt, -16.0, ALU.mult)
-    act(m(AQ), m(NBO), ACT.Identity, scale=ca)
-    ts(v("tmp", 256, 384), v("i16", 0, 128), 1.5, ALU.is_lt)
-    tt(m(AQ2), m(AQ), v("tmp", 256, 384), ALU.mult)
-    ts(v("tmp", 512, 640), v("i16", 0, 128), 1.0, ALU.is_equal, 2.0, ALU.mult)
-    ts(v("tmp", 384, 512), v("i16", 0, 128), 2.0, ALU.not_equal)
-    tt(v("tmp", 384, 512), v("tmp", 512, 640), v("tmp", 384, 512), ALU.subtract)
-    tt(m(QY), v("tmp", 384, 512), m(NBO), ALU.mult)
-    ts(c2, cr, 2.0, ALU.is_equal, 22528.0, ALU.mult)
-    ts(c3, cr, 3.0, ALU.is_equal, -1.0, ALU.mult)
-    act(m(CQ), m(NBO), ACT.Identity, scale=c2)
-    act(m(SQ), m(NBO), ACT.Identity, scale=c3)
-    tt(cfa, c2, c3, ALU.not_equal)
-    ts(cfa, cfa, 0.5, ALU.mult)
-    ts(cam, ca, 64.0, ALU.mult, cfa, ALU.add)
-    ts(v3("TT", TAM), v("io144"), ct, ALU.is_equal, cam, ALU.mult)
-    ts(cam, cfa, -1.0, ALU.mult)
-    act(m(FQ), m(NBO), ACT.Identity, scale=cam)
-    c2b = col()
-    ts(c2b, cr, 2.0, ALU.is_equal, 2048.0, ALU.mult)
-    act(m(C2), m(NBO), ACT.Identity, scale=c2b)
-    tt(v("BI"), m(NBO), m(I), ALU.add)
-    act(v("BI"), v("BI"), ACT.Identity, scale=-1.0)
-    memset(v("tmp", 640, 656), 2.0)
-    memset(v("tmp", 656, 672), 0.0)
-    scan(v("tmp", 672, 688), v("tmp", 640, 656), v("tmp", 656, 672), 2048.0, ALU.mult, ALU.add)
-    ts(v("tmp", 688, 704), v("i16", 0, 16), cr, ALU.is_equal)
-    tt(v("tmp", 672, 688), v("tmp", 672, 688), v("tmp", 688, 704), ALU.mult)
-    add("V", lambda: g.vector.tensor_reduce(c12[0], T.tmp[:, 672:688], AxisListType.X, ALU.add, negate=True),
-        [c12], [v("tmp", 672, 688)], 16)
-    act(m(BOD), m(NBO), ACT.Identity, scale=c12)
-    ts(c13, c12, 2.0, ALU.mult, float(2 ** 36), ALU.add)
-    ts(v("sc"), v("i16"), cr, ALU.is_equal, c13, ALU.mult)
-    act(v("thr"), v("sc"), ACT.Identity, bias=-float(2 ** 36))
-    ts(v("rst"), v("i16"), 0.5, ALU.is_ge, 0.5, ALU.subtract)
-    act(v("rst"), v("rst"), ACT.Identity, scale=float(2 ** 41))
-    ts(v("s8"), v("s8i"), 0.0, ALU.is_equal)
-    copy(v("btb"), v("bti"))
-    mm(v("b7", 0, 4), v("s8"), v("btb"), True, True)
-    ts(c14, c0, -2040.0, ALU.mult, -0.5, ALU.add)
-    ts(c16, c0, 2040.0, ALU.mult, -0.5, ALU.add)
-    ts(v("th", 0, 4), v("b7", 0, 4), -1.0, ALU.mult, c14, ALU.add)
-    ts(v("th", 4, 8), v("b7", 0, 4), -1.0, ALU.mult, c16, ALU.add)
-    ts(c14, cr, 1.5, ALU.is_lt, -1.0, ALU.mult)
-    ts(c15, c14, 0.5, ALU.add)
-    ts(v("th", 8, 12), v("b7", 0, 4), c14, ALU.mult, c15, ALU.add)
-    ts(csg, c0, 2.0, ALU.mult, -1.0, ALU.add)
-    ts(ce0, c0, 14.0, ALU.mult, -13.0, ALU.add)
-    if True in OPT["hlv"]:
-        ts(v("th", 12, 20), v("th", 0, 8), -1.0, ALU.mult)
 
     def sr(i):
         return v3("SR", i)
-    memset(v("one"), 1.0)
-    coff, ce, cx = [], [], []
-    for h in range(2):
-        onv = [s for s in range(7) if OPT["cmpv"][h][s // 4]]
-        ce.append(col())
-        cx.append(col())
-        if onv:
-            coff.append(col())
-            for s in onv:
-                mm(v("b5", 0, 2), sr(7 + s), v("one"), s == onv[0], s == onv[-1])
-            copy(coff[h], v("b5", 0, 1))
-            tt(ce[h], ce0, coff[h], ALU.subtract)
+
+    def pa(i):
+        return v3("pa", i)
+
+    def pq(i):
+        return v("pq", 16 * i, 16 * i + 16)
+    ts(m(I), v("io", 0, 128), cp, ALU.is_equal)
+    ts(m(NBO), v("blk"), cg, ALU.is_equal, -1.0, ALU.mult)
+    act(v("g8", 0, 8), v("oh", 16, 24), scale=2.0)
+    act(v("g8", 8, 16), v("oh", 16, 24), scale=-1.0)
+    ts(v3("TT", TM1), v("io"), ct, ALU.is_equal, -1.0, ALU.mult)
+    act(v3("TT", T2), v3("TT", TM1), scale=-2.0)
+    act(v3("TT", TAM), v3("TT", TM1), scale=col(c16, 8.0))
+    act(vp("R2", 0, 64, 0, 64), (T.M[0:64, I, 0:64],) + m(I)[1:])
+    act(vp("R2", 64, 128, 0, 64), (T.M[64:128, I, 64:128],) + m(I)[1:], scale=-2.0)
+    cu = col()
+    copy(cu, v("uwi"))
+    act(v("Wf", 0, 16), i16, scale=2.0, bias=1.0)
+    ts(v("Wi", 0, 16), v("Wf", 0, 16), cu, ALU.mult, 2048.0, ALU.add)
+    ts(v("Wi", 16, 32), v("Wi", 0, 16), 4095, ALU.bitwise_and)
+    ts(v("Wf", 16, 32), v("Wi", 16, 32), -2048.0, ALU.add)
+    act(v("Tu"), v3("TT", TM1), scale=col(v("Wf", 16, 17), -1.0))
+    for gg in range(8):
+        act(v("W", 16 * gg, 16 * gg + 16), v("Wf", 16, 32), scale=own16(gg))
+    ts(v("cLh"), v("io", 0, 16), 16.0, ALU.mult, cr, ALU.add)
+    act(v("cL"), v("cLh"), scale=16.0)
+
+    def ulist(zv, bank):
+        group([(bank, v("Tu", 15 - p, 143 - p), v(zv[1], zv[2] + p, zv[3], 16)) for p in range(16)])
+
+    ulist(v("zw0", 0, 256), v("b6", 0, 16))
+    copy(v("vc", 0, 16), v("v0i"))
+    copy(v("ui", 0, 16), v("b6", 0, 16))
+    ts(v("ui", 16, 32), v("ui", 0, 16), 15, ALU.bitwise_and)
+    tt(v("ds0", 33, 64, 2), v("ui", 16, 32), v("cL"), ALU.add)
+    copy(v("vc", 16, 32), v("ds0", 33, 64, 2))
+    memset(v("am"), 0.0)
+    memset(vs("wR", 0, 16, 16, 17), -1.0)
+    c1 = col(row(0), -1.0, 1.0)
+    memset((T.pa[:, 0, 0:112:16],) + pa(0)[1:5] + (7,), -100.0)
+    ts(pa(1), pa(0), cr, ALU.is_equal)
+    ts(pa(2), pa(0), col(cr, bias=15.0), ALU.is_equal, col(c1, -1.0), ALU.mult)
+    ts(pa(3), pa(0), 15.5, ALU.is_lt, 0.5, ALU.subtract)
+    ts(pa(4), v("i16", 0, 112), cr, ALU.is_equal, col(c1, -2.0), ALU.mult)
+    tt(pa(5), pa(3), pa(4), ALU.mult)
+    group([(v("b5", 0, 112), m(I), pa(i)) for i in (1, 2, 5)])
+    act(v("pq", 0, 112), v("b5", 0, 112))
+    ts(v("pb", 0, 16), i16, 0.0, ALU.is_equal)
+    ts(pq(AQ), i16, 1.5, ALU.is_lt, c16, ALU.mult)
+    act(pq(AH), v("pb", 0, 16), scale=col(row(2), -2040.0), bias=c16)
+    act(pq(AL), v("pb", 0, 16), scale=col(row(2), 2040.0), bias=c16)
+    ts(pq(VQ), i16, 4.0, ALU.is_equal, col(row(0), 4096.0), ALU.mult)
+    ts(pq(BOD), i16, cr, ALU.is_lt, -float(2 ** 28), ALU.mult)
+    ts(pq(BIB), i16, cr, ALU.not_equal)
+    ts(v("pb", 16, 32), i16, 1.0, ALU.is_equal, -2.0, ALU.mult)
+    ts(v("pb", 32, 48), i16, 2.0, ALU.not_equal)
+    tt(v("pb", 48, 64), v("pb", 16, 32), v("pb", 32, 48), ALU.add)
+    act(pq(QY), v("pb", 48, 64), scale=col(row(0), 2.0, -1.0))
+    for gg in range(8):
+        o = (T.SR[:, :, 16 * gg:16 * gg + 16], "SR", 0, 14 * 128, (gg,), 224)
+        if gg % 4 == 3:
+            act(o, v("pq"), scale=own16(gg))
         else:
-            coff.append(0.0)
-            copy(ce[h], ce0)
-        ts(cx[h], ce[h], -0.5, ALU.add)
+            ts(o, v("pq"), own16(gg), ALU.mult)
+    act(v("BI"), sr(BIB))
+    for bank, s0, s1 in (("b4", 0, 4), ("b5", 4, 7)):
+        for s in range(s0, s1):
+            mm(v(bank, 128 * (s - s0), 128 * (s - s0 + 1)), sr(s), m(I), True, True)
+        for e, off, scale in (("S", 0, 2048.0), ("V", 896, 4096.0)):
+            used = [s for s in range(s0, s1) if any(u[3][1 + (s >= int(u[3][0]))] == e for u in units)]
+            if used:
+                act(v("SP", off + 128 * used[0], off + 128 * used[-1] + 128),
+                    v(bank, 128 * (used[0] - s0), 128 * (used[-1] - s0 + 1)), scale=scale)
+    for i, src, scale in ((IP, I, c1), (NBOP, NBO, c1), (IM, I, -4096.0), (IG, I, 16384.0), (IZ, I, 32768.0), (IH, I, 0.5),
+                          (NIH, I, -0.5), (BOA, NBO, float(2 ** 28)), (NIP, IP, -1.0), (BOP, NBOP, -1.0),
+                          (CQ, NBO, col(row(2), 22528.0)), (C2, NBO, col(row(2), 2048.0)), (SQ, NBO, col(row(3), -1.0)),
+                          (FQ, NBO, col(row(4), 1024.0, col(row(3), -0.5, col(row(2), -0.5))))):
+        act(m(i), m(src), scale=scale)
+    act(v("Qi"), m(I), bias=row(2), scale=0.0)
+    ts(v("ne"), v("i17"), cr, ALU.not_equal)
+    act(v("thr"), v("ne"), scale=-float(2 ** 30), bias=4096.0)
+    copy(v("thr", 16, 272, 17), v("cLh"))
+    ts(v("mk"), v("i16"), cr, ALU.not_equal, -float(2 ** 20), ALU.mult)
+    memset(v("rst", 0, 272, 17), -8000000.0)
+    memset(v("rs", 0, 128, 16), -8000000.0)
+    c8 = col(cp, 16.0)
+    ts(v("s8"), vp("blk", 0, 8, 0, 128), vp("col", 0, 8, c8[2], c8[3]), ALU.is_equal)
+    copy(v("btb"), v("bti"))
+    mm(v("b7", 0, 4), v("s8"), v("btb"), True, True)
+    act(v("th", 0, 4), v("b7", 0, 4), scale=-1.0, bias=-0.5)
+    cq = col(c16, -1.0 / 16)
+    act(v("th", 4, 8), v("b7", 0, 4), scale=cq, bias=col(row(4), -4096.0 * 1023, col(cq, bias=0.5)))
+    cE = col(row(0), 30720.0, -26624.0)
 
     def slide(i, p):
         return v3("TT", i, 15 - p, 143 - p)
 
     for t in range(RO):
+        now[0] = ""
         last = t == RO - 1
-        zw, zn, st, sn = "zw%d" % t, "zw%d" % (t + 1), "st%d" % t, "st%d" % (t + 1)
+        zw, zn, ds, dn = "zw%d" % t, "zw%d" % (t + 1), "ds%d" % t, "ds%d" % (t + 1)
         z = v(zw, 0, 256)
-        Q, Qp = "Q%d" % (t % 2), "Q%d" % ((t + 1) % 2)
-        copy(v("Pu"), ind(v("B", 0, 2048), v("vc", 0, 16)))
-        Ph = "Ph%d" % t
-        ts(v(Ph), v("Pu"), -2048.0, ALU.add)
-        send(v(Ph), "pl%d" % t, "ap%d" % t, hn[t])
-        if last:
+        Q, Qp, Ph, ms, ls = "Q%d" % (t % 2), "Q%d" % ((t + 1) % 2), "Ph%d" % t, "ms%d" % t, "ls%d" % t
+        B = "B" if OPT["bint"] else "Bf"
+        for a, b in OPT["bags"]:
+            copy(v("Pu", a, b), ind(v(B if t else "B", 256, 2304), v("vc", a // 16, b // 16)))
+        move("Ph", v(Ph), v("Pu"), -2048.0)
+        send(v(Ph), v("pl%d" % t), "ap%d" % t, hn[t])
+        if t == 0 and B == "Bf":
             for h in range(4):
-                copy(v("Bf", 512 * h, 512 * h + 512), v("B", 512 * h, 512 * h + 512))
-        copy(v("vR"), ind(v("iot"), v("vc", 0, 16)))
-        if OPT["xv"]:
+                copy(v("Bf", 256 + 512 * h, 768 + 512 * h), v("B", 256 + 512 * h, 768 + 512 * h))
+        move("vR", v("vR"), ind(v("iot"), v("vc", 0, 16)))
+
+        def changed(bank):
             src = ind(v("X"), v("vc", 16, 32))
-            add("V", lambda src=src, z=z: g.vector.tensor_tensor(T.xs[:], src[0], z[0], ALU.add), [v("xs")], [src, z], 256)
-            ts(v("xi"), v("xs"), 255, ALU.bitwise_and)
-        else:
-            act(v("old"), ind(v("X"), v("vc", 16, 32)), ACT.Identity)
-            mm(v("b7", 256, 512), m(I), v("old"), True, False)
-            mm(v("b7", 256, 512), m(I), z, False, True)
-            act(v("sg"), v("b7", 256, 512), ACT.Sign, bias=-255.5)
-            mm(v("b7", 256, 512), m(I), v("old"), True, False)
-            mm(v("b7", 256, 512), m(I), z, False, False)
-            mm(v("b7", 256, 512), m(IX), v("sg"), False, True)
-            act(v("xn"), v("b7", 256, 512), ACT.Identity, bias=-128.0)
-        xn = "xi" if OPT["xv"] else "xn"
-        mm(v("b6", 0, 256), m(I), z, True, False)
-        mm(v("b6", 0, 256), m(I), v("zl%d" % t), False, True)
-        act(v("av"), v("b6", 0, 256), ACT.Identity, bias=MAGIC, scale=0.5 - 2.0 ** -11)
-        act(v(zw, 256, 512), v("av"), ACT.Identity, bias=-MAGIC)
-        ulist(v(zw, 256, 512), v("b7", 0, 16))
-        copy(v("ui", 0, 16), v("b7", 0, 16))
-        ts(v("alt", 0, 16), v("ui", 0, 16), 2047, ALU.bitwise_and)
-        if not last:
-            ts(v("ui", 16, 32), v("ui", 0, 16), 15, ALU.bitwise_and)
-            tt(v("alt", 16, 32), v("ui", 16, 32), v("cL", 16, 32), ALU.add)
+            if OPT["xmode"] == 0:
+                tt(v("xs"), src, z, ALU.add)
+                ts(v("xi"), v("xs"), 255, ALU.bitwise_and)
+            else:
+                o = v(bank, 256, 512)
+                act(v("old"), src)
+                group([(o, m(I), v("old")), (o, m(I), z)])
+                act(v("xn"), o, bias=-256.0)
+                ts(v("sg"), o, 255.5, ALU.is_lt, 256.0, ALU.mult)
 
-        def hv(name, h, off=0):
-            if name == "Ph":
-                name = Ph
-            return v(name, off + 128 * h, off + 128 * h + 128)
+        def mean(bank):
+            group([(v(bank, 0, 256), m(I), z), (v(bank, 0, 256), m(I), v("zl%d" % t))])
+            act(v("av"), v(bank, 0, 256), bias=MAGIC, scale=0.5 - 2.0 ** -11)
+            act(v(zw, 256, 512), v("av"), bias=-MAGIC)
+            ulist(v(zw, 256, 512), v(bank, 0, 16))
+            move("ui", v("ui", 0, 16), v(bank, 0, 16))
+            ts(v("alt", 0, 16), v("ui", 0, 16), 2047, ALU.bitwise_and)
+            if not last:
+                ts(v("ui", 16, 32), v("ui", 0, 16), 15, ALU.bitwise_and)
+                tt(v("alt", 16, 32), v("ui", 16, 32), v("cL"), ALU.add)
 
-        def hl(side, h, i):
-            return v(side + "ab"[h] + str(t), 128 * i, 128 * i + 128)
+        def hashed(bank):
+            group([(v(bank, 256, 512), v("W"), z), (v(bank, 256, 512), m(I), v(Ph))])
+            move("Hs", v("Hs"), v(bank, 256, 512), 2048.0)
+            ts(v("H"), v("Hs"), 4095, ALU.bitwise_and)
 
         def distances(i):
-            a, b = CHUNKS[i]
-            bank, w = "b%d" % (i % 2), 4 * (b - a)
-            for r in range(4):
-                mm(v(bank, r, w, 4), m(I), vk("xg", a, b, 0), True, True)
-            d = v("b%d" % (2 + a // 128), a % 128, a % 128 + b - a)
-            if not OPT["ulay"]:
-                mm(d, m(NBO), vk("xg", a, b, 0), True, False)
-                mm(d, slide(TM1, 0), v(zw, a, b), False, False)
-                for k in range(1, 16):
-                    mm(d, slide(TM1, k), vk("xg", a, b, k), False, False)
-            parts = [(1, 4), (2, 4), (3, 4), (4, 8), (8, 16), (0, 16)]
+            a, b = OPT["chunks"][i]
+            u = [j for j, u_ in enumerate(units) if u_[0] <= a < u_[1]][0]
+            ua, ub, form, _, banks = units[u]
+            rep = OPT["rep"][i]
+            bank, w, bs = "b%d" % (i % 2), rep * (b - a), "b" + banks[0]
+            for r in range(rep):
+                mm(v(bank, r, w, rep), m(I), vk("xg", a, b, 0), True, True)
+            s = 16 // rep
+            parts = [(k0, s) for k0 in range(1, s)]
+            while s < 16:
+                parts.append((s, 2 * s))
+                s *= 2
+            parts.append((0, 16))
             for k0, s in parts:
-                tt(vk("mx", a, b, k0, s), vk("xg", a, b, k0, s) if k0 else v(zw, a, b), v(bank, 0, w, s // 4), ALU.max)
-                if not OPT["ulay"]:
-                    for k in range(k0, 16, s):
-                        mm(d, slide(T2, k), vk("mx", a, b, k), False, k == 0)
-            if OPT["ulay"] and b % 128 == 0:
-                h, bank = a // 128, "b%d" % (2 + a // 128)
-                a, b = 128 * h, 128 * h + 128
-                mm(v(bank, 384, 512), vk("xg", a, b, 0), m(NBO), True, False)
-                for k in range(16):
-                    mm(v(bank, 384 + k, 512, 16), vk("xg", a, b, k) if k else v(zw, a, b), v("g8", 8, 16), False, False)
-                ks = [k for k0, s in parts for k in range(k0, 16, s)]
-                for k in ks:
-                    mm(v(bank, 384 + k, 512, 16), vk("mx", a, b, k), v("g8", 0, 8), False, k == ks[-1])
-                ts(hv("Uh", h), v(bank, 384, 512), -2040.0, ALU.add)
-                mm(v(bank, 0, 128), hv("Uh", h), m(I), True, True)
-
-        def ranks(h):
-            bd, br = "b%d" % (2 + h), "b%d" % (6 + h)
-            Dh, R, ys = hv("Dh", h), v(br, 0, 128), hv("ys", h)
-            ts(Dh, v(bd, 0, 128), 0.0 if OPT["ulay"] else -2040.0, ALU.add)
-            for bank, s0, s1, onv in (("b4", 0, 4, OPT["cmpv"][h][0]), ("b5", 4, 7, OPT["cmpv"][h][1])):
-                for s in range(s0, s1):
-                    mm(v(bank, 128 * (s - s0), 128 * (s - s0) + 128), sr(s), Dh, True, True)
-                o, i_ = v("cm", 896 * h + 128 * s0, 896 * h + 128 * s1), v(bank, 0, 128 * (s1 - s0))
-                if onv:
-                    ts(o, i_, -0.5, ALU.is_gt, 2.0, ALU.mult)
-                else:
-                    act(o, i_, ACT.Sign, bias=0.5)
-            for s in range(7):
-                mm(R, sr(7 + s), v("cm", 896 * h + 128 * s, 896 * h + 128 * s + 128), s == 0, s == 6)
-            if OPT["selS"]:
-                act(v(bd, 128, 256), R, ACT.Square)
-                act(v(bd, 128, 256), v(bd, 128, 256), ACT.Sign)
-                act(v(bd, 128, 256), v(bd, 128, 256), ACT.Identity, bias=csg, scale=cns)
+                tt(vk("mx", a, b, k0, s), vk("xg", a, b, k0, s) if k0 else v(zw, a, b), v(bank, 0, w, s * rep // 16), ALU.max)
+            if b != ub:
+                return
+            a, nl = ua, ub - ua
+            ks = [k for k0, s in parts for k in range(k0, 16, s)]
+            Uh = v("Uh", 2 * a, 2 * a + 128)
+            if form == 2:
+                group([(v(bs, 384 + k, 512, 16), both(a, b, k), v("g8", 8, 16)) for k in ks if k]
+                      + [(vp(bs, 0, 64, 384, 512, 16), v(zw, a, b), v("g8", 8, 16))])
+                mm(vp(bs, 64, 128, 384, 512, 16), vk("mx", a, b, 0), v("g8", 8, 16), False, True)
+                move("Uh%d" % u, Uh, v(bs, 384, 512), 2040.0)
+                group([(v(bs, 0, nl), m(NBO), vk("xg", a, b, 0)), (v(bs, 0, nl), Uh, v("R2"))])
+            elif form == 1:
+                Uh = vp("Uh", 0, nl, 2 * a, 2 * a + 128)
+                group([(vp(bs, 0, nl, 384, 512), vk("xg", a, b, 0), m(NBO))]
+                      + [(vp(bs, 0, nl, 384 + k, 512, 16), vk("xg", a, b, k) if k else v(zw, a, b), v("g8", 8, 16)) for k in range(16)]
+                      + [(vp(bs, 0, nl, 384 + k, 512, 16), vk("mx", a, b, k), v("g8", 0, 8)) for k in ks])
+                move("Uh%d" % u, Uh, vp(bs, 0, nl, 384, 512), -2040.0)
+                mm(v(bs, 0, nl), Uh, (T.M[0:nl, I, 0:nl],) + v3("M", I, 0, nl)[1:], True, True)
             else:
-                ts(v(bd, 128, 256), R, coff[h], ALU.is_equal, csg, ALU.mult)
-            tt(ys, Dh, v(bd, 128, 256), ALU.mult)
-            qb, hi, lo = v(br, 128, 256), v("b%d" % h, 0, 128), v(bd, 384, 512)
-            if OPT["hib"]:
-                hi, lo = v("b%d" % h, 0, 128), v("b%d" % h, 128, 256)
-            if t:
-                mm(qb, m(AQ2), hv(Qp, h), True, False)
-            for o, mi, mb in ((hi, IP, BOP), (lo, NIP, NBOP)):
-                mm(o, m(mi), Dh, True, False)
-                if t:
-                    mm(o, m(AQ), hv(Qp, h), False, False)
-                mm(o, m(mb), ys, False, True)
-            mm(qb, m(QY), ys, t == 0, True)
-            act(hv(Q, h), qb, ACT.Sign, bias=v("th", 8 + t, 9 + t))
-            act(hl("m", h, 0), hi, ACT.Sign, bias=v("th", t, t + 1))
-            act(hl("m", h, 1), lo, ACT.Sign, bias=v("th", 4 + t, 5 + t))
-            send(v("m" + "ab"[h] + str(t)), "l" + "ab"[h] + str(t), "a" + "ab"[h] + str(t), hn[t])
+                d = v(bs, 0, nl)
+                group([(d, m(NBO), vk("xg", a, b, 0))]
+                      + [(d, slide(TM1, k), vk("xg", a, b, k) if k else v(zw, a, b)) for k in range(16)]
+                      + [(d, slide(T2, k), vk("mx", a, b, k)) for k in ks])
 
-        def own(h):
-            bd, R = "b%d" % (2 + h), v("b%d" % (6 + h), 0, 128)
-            act(hv("Es", h), R, ACT.Sign, bias=cx[h])
-            act(R, R, ACT.Relu, bias=ce[h])
-            mm(v(bd, 0, 128), m(IH), hl("m", h, 0), True, False)
-            mm(v(bd, 0, 128), m(NIH), hl("m", h, 1), False, False)
-            mm(v(bd, 0, 128), m(SQ), hv(Q, h), False, True)
-            act(hv("sd", h), v(bd, 0, 128), ACT.Abs)
-            mm(v(bd, 128, 256), m(I), hv("Ph", h), True, False)
-            mm(v(bd, 128, 256), m(CQ), hv(Q, h), False, False)
-            mm(v(bd, 128, 256), m(IG), hv("sd", h), False, True)
-            tt(hv("Ge", h), hv("H", h), v(bd, 128, 256), ALU.max)
-            mm(v("b%d" % (6 + h), 256, 384), m(I), hv("pl%d" % t, h), True, False)
-            mm(v("b%d" % (6 + h), 256, 384), m(C2), hv(Q, h), False, False)
-            mm(v(bd, 384, 512), m(IZ), hv("Es", h), True, False)
+        def ranks(u):
+            a, b, form, ns, banks = units[u]
+            nl = b - a
+            Dh, ys, R = v("Dh", a, b), v("ys", a, b), v("b" + banks[1], 384, 384 + nl)
+            move("Dh%d" % u, Dh, v("b" + banks[0], 0, nl), 0.0 if form else -2040.0)
+            terms = [(R, m(I), Dh)]
+            cuts = [(0, int(ns[0]), ns[1] == "S"), (int(ns[0]), 7, ns[2] == "S")]
+            for bank, (s0, s1, on_s) in zip(("b4", "b5"), cuts):
+                for s in range(s0, s1):
+                    mm(v(bank, nl * (s - s0), nl * (s - s0 + 1)), sr(s), Dh, True, True)
+                o, i_ = v("cm", 7 * a + nl * s0, 7 * a + nl * s1), v(bank, 0, nl * (s1 - s0))
+                if on_s:
+                    act(o, i_, ACT.Sign, bias=0.5)
+                else:
+                    ts(o, i_, -0.5, ALU.is_gt, 0.5, ALU.subtract)
+                off = 0 if on_s else 896
+                terms += [(R, v("SP", off + 128 * s, off + 128 * s + 128), v("cm", 7 * a + nl * s, 7 * a + nl * (s + 1)))
+                          for s in range(s0, s1)]
+            group(terms)
+            ts(ys, R, -2048.0, ALU.max, 2048.0, ALU.min)
+            be = "b" + banks[2]
+            hi, lo, qb = v(be, 0, nl), v(be, nl, 2 * nl), v(be, 256, 256 + nl)
+            qp = v(Qp, a, b) if t else v("Qi", 0, nl)
+            group([(hi, m(IP), Dh), (lo, m(NIP), Dh), (hi, sr(AH), qp), (lo, sr(AL), qp), (qb, sr(VQ), v("vR", a, b))]
+                  + ([(qb, sr(AQ), qp)] if t else []) + [(hi, m(NBOP), ys), (lo, m(BOP), ys), (qb, sr(QY), ys)])
+            act(v(ms, 2 * a, 2 * b), v(be, 0, 2 * nl), ACT.Sign, bias=v("th", t, t + 1))
+            act(v(Q, a, b), qb, ACT.Sign, bias=v("th", 4 + t, 5 + t))
+            send(v(ms, 2 * a, 2 * b), v(ls, 2 * a, 2 * b), "a" + "abde"[u] + str(t), hn[t])
+            act(v("Es", a, b), R, ACT.Sign, bias=cE)
 
-        def merge(h):
-            bd, R = "b%d" % (2 + h), v("b%d" % (6 + h), 0, 128)
-            mm(v("b%d" % (6 + h), 256, 384), m(IM), hl("l", h, 0), False, False)
-            mm(v("b%d" % (6 + h), 256, 384), m(IM), hl("l", h, 1), False, True)
-            tt(hv("Fe", h), hv("Ge", h), v("b%d" % (6 + h), 256, 384), ALU.max)
-            tt(hv("tE", h), hv("Fe", h), R, ALU.mult)
-            mm(v(bd, 384, 512), v("BI"), hv("tE", h), False, True)
-            tt(hv("Fs", h), hv("Fe", h), v(bd, 384, 512), ALU.max)
-            ts(hv("Ff", h), hv("Fs", h), 4095, ALU.bitwise_and)
+        def single(u):
+            a, b, _, _, banks = units[u]
+            nl, c0, c1_ = b - a, a // 16, b // 16
+            kr, kl, tot = v("b" + banks[6], 0, nl), v("b" + banks[7], 128, 128 + nl), "b" + banks[8]
+            group([(kr, m(I), v("vR", a, b)), (kr, m(FQ), v(Q, a, b))])
+            move("wR", vs("wR", c0, c1_, 0, 16), kr)
+            group([(kl, m(I), v("mk", 0, nl)), (kl, m(I), v("vR", a, b)), (kl, m(FQ), v(Q, a, b))])
+            scan(v("ks", a, b), v("rs", 0, nl), kl, 0.0, ALU.min, ALU.max)
+            act(v("rst", 17 * c0 + 16, 17 * c1_, 17), v("ks", a + 15, b, 16), bias=256.0)
+            for j in range(c1_ - 1, c0 - 1, -1):
+                o, i_, key = v3("eq", j, 119 - 17 * (j - c0), 136), vs("wR", c0, j + 1, 0, 17), v("ks", 16 * j + 15, 16 * j + 16)
+                if j - c0 < OPT["eqS"][u]:
+                    act(v3("ab", j, 119 - 17 * (j - c0), 136), i_, ACT.Abs, bias=key, scale=-1.0)
+                    act(o, v3("ab", j, 119 - 17 * (j - c0), 136), ACT.Relu, bias=1.0, scale=-1.0)
+                else:
+                    ts(o, i_, key, ALU.is_equal)
+            w = 17 * (c1_ - c0)
+            group([(v(tot, 256, 256 + w), m(I), v("thr", 17 * c0, 17 * c1_))]
+                  + [(v(tot, 256, 256 + 17 * (j - c0)), m(BOA), v3("eq", j, 119 - 17 * (j - c0), 119)) for j in range(c1_ - 1, c0, -1)]
+                  + [(v(tot, 256, 256 + w), sr(BOD), vs("eq", c0, c1_, 119, 136))])
+            scan(v("sc", 17 * c0, 17 * c1_), v("rst", 17 * c0, 17 * c1_), v(tot, 256, 256 + w), 0.0, ALU.min, ALU.max)
+            move("oU", v("oU", c0, c1_), v("sc", 17 * c0 + 16, 17 * c1_, 17))
 
-        def lists(j0, j1, bank):
-            y, kr = v("b5", 0, 16), v("b4", 0, 256)
-            copy(v("wi", 0, 16), v(st, 0, 16))
-            ts(v("wi", 16, 32), v("wi", 0, 16), 1023, ALU.bitwise_and)
-            tt(v("am", 16, 32), v("wi", 16, 32), v("cL", 0, 16), ALU.add)
-            act(v("am", 0, 16), v("am", 16, 32), ACT.Identity, scale=2.0)
-            mm(kr, m(I), v("vR"), True, False)
-            mm(y, m(I), v("cLh"), True, False)
-            mm(kr, m(FQ), v(Q), False, True)
-            for p in range(16):
-                mm(y, slide(TAM, p), v(Q, p, 256, 16), False, p == 15)
-            copy(v("wR"), kr)
-            tt(v("v21"), v("am", 0, 16), y, ALU.add)
-            ts(v("o1", 0, 16), y, 2047.5, ALU.is_gt, 2048.0, ALU.mult)
-            ts(v("mc%d" % t), y, 0.125, ALU.mult)
-            copy(v("wi", 0, 16), v("v21"))
-            ts(v("wi", 16, 32), v("wi", 0, 16), 2047, ALU.bitwise_and)
-            copy(v(st, 0, 16), v("wi", 16, 32))
+        def own(u):
+            a, b, _, _, banks = units[u]
+            nl, bo = b - a, "b" + banks[3]
+            o = v(bo, 0, nl)
+            group([(o, m(IH), v(ms, 2 * a, a + b)), (o, m(NIH), v(ms, a + b, 2 * b)), (o, m(SQ), v(Q, a, b))])
+            act(v("sd", a, b), o, ACT.Abs)
+            act(v(bo, 256, 256 + nl), v("Es", a, b), ACT.Relu)
+            o = v(bo, 128, 128 + nl)
+            group([(o, m(I), v(Ph, a, b)), (o, m(CQ), v(Q, a, b)), (o, m(IG), v("sd", a, b))])
+            tt(v("Ge", a, b), v("H", a, b), o, ALU.max)
 
-        def equal(j0, j1):
-            ns = OPT["eqS"] if j0 == 0 else 0
-            if ns:
-                act(v("wF", 0, 16 * ns), ind(v("iot"), v("wU", 0, ns)), ACT.Identity)
-                for j in range(ns):
-                    act(v("wA", 16 * j * (j + 1) // 2, 16 * (j + 1) * (j + 2) // 2), v("wF", 0, 16 * j + 16), ACT.Abs,
-                        bias=v(st, j, j + 1), scale=-1.0)
-                for j in range(ns):
-                    act(v3("eq", j, 256 - 16 * j, 272), v("wA", 16 * j * (j + 1) // 2, 16 * (j + 1) * (j + 2) // 2), ACT.Relu,
-                        bias=1.0, scale=-1.0)
-            for j in range(j1 - 1, j0 + ns - 1, -1):
-                ts(v3("eq", j, 256 - 16 * j, 272), v("wR", 0, 16 * j + 16), v("o1", j, j + 1), ALU.add,
-                   v("v21", j, j + 1), ALU.is_equal)
+        def merge(u):
+            a, b, _, _, banks = units[u]
+            o = v("b" + banks[4], 384, 384 + b - a)
+            group([(o, m(I), v("pl%d" % t, a, b)), (o, m(C2), v(Q, a, b)), (o, m(IM), v(ls, 2 * a, a + b)),
+                   (o, m(IM), v(ls, a + b, 2 * b))])
+            tt(v("Fe", a, b), v("Ge", a, b), o, ALU.max)
+            tt(v("tE", a, b), v("Fe", a, b), v("b" + banks[3], 256, 256 + b - a), ALU.mult)
+            o = v("b" + banks[5], 0, b - a)
+            group([(o, m(IZ), v("Es", a, b)), (o, v("BI"), v("tE", a, b))])
+            tt(v("Fs", a, b), v("Fe", a, b), o, ALU.max)
+            ts(v("Ff", a, b), v("Fs", a, b), 4095, ALU.bitwise_and)
+            copy(ind(v(B), v("oU", a // 16, b // 16)), v("Ff", a, b))
 
-        for a, b, e in GATHERS:
+        def ambiguous(_):
+            y = v("b" + OPT["yb"], 384, 400)
+            group([(y, m(I), v("cLh"))] + [(y, slide(TAM, p), v(Q, p, 256, 16)) for p in range(16)])
+            move("mc", v("mc%d" % t), y)
+            send(v("mc%d" % t), v("lc%d" % t), "ac%d" % t, hz[t])
+
+        for a, b, e in OPT["gathers"]:
             src = ind(v("X"), v("Pu", a, b))
             if e == "V":
-                copy(v("xg", 16 * a, 16 * b), src)
+                copy(vk("xg", a, b, 0, 1), src)
             else:
-                act(v("xg", 16 * a, 16 * b), src, ACT.Identity)
-        for i, ch in enumerate(CHUNKS):
-            distances(i)
-            if i == 0:
-                mm(v("b7", 256, 512), v("W"), z, True, False)
-                mm(v("b7", 256, 512), m(I), v(Ph), False, True)
-                ts(v("Hs"), v("b7", 256, 512), 2048.0, ALU.add)
-                ts(v("H"), v("Hs"), 4095, ALU.bitwise_and)
-        for i, ch in enumerate(CHUNKS):
-            if ch[1] == 128:
-                boost[0] = OPT["boost"][0]
-                ranks(0)
-                boost[0] = OPT["boost"][1]
-                if OPT["early"]:
-                    lists(0, 8, "b6")
-                    equal(0, 8)
-                boost[0] = OPT["boost"][2]
-                own(0)
-                boost[0] = 0.0
-        ranks(1)
-        j0 = 8 if OPT["early"] else 0
-        lists(j0, 16, "b7" if j0 else "b1")
-        send(v("mc%d" % t), "lc%d" % t, "ac%d" % t, hz[t])
-        equal(j0, 16)
-        merge(0)
-        own(1)
-        if OPT["nx"] == 1:
-            copy(ind(v("X"), v("vc", 16, 32)), v(xn))
-        else:
-            for h in range(2):
-                copy(ind(v("X"), v("vc", 16 + 8 * h, 24 + 8 * h)), hv(xn, h))
+                act(vk("xg", a, b, 0, 1), src)
+        stage = {"d": distances, "r": ranks, "s": single, "o": own, "m": merge, "y": ambiguous,
+                 "a": lambda i: (changed, hashed, mean)[i]("b" + OPT["aside"][i])}
+        for word in OPT["order"].split():
+            now[0] = word
+            stage[word[0]](int(word[1:]))
+        now[0] = ""
+        w = 16 // OPT["nx"]
+        for h in range(OPT["nx"]):
+            o = ind(v("X"), v("vc", 16 + w * h, 16 + w * (h + 1)))
+            if OPT["xmode"] == 0:
+                copy(o, v("xi", 16 * w * h, 16 * w * (h + 1)))
+            else:
+                tt(o, v("xn", 16 * w * h, 16 * w * (h + 1)), v("sg", 16 * w * h, 16 * w * (h + 1)), ALU.add)
         if last:
-            dma("Y", T.yx[:], v("X"), 6000)
-        tot = v("b0", 0, 256)
-        mm(tot, m(I), v("thr"), True, False)
-        for j in list(range(j0 - 1, 0, -1)) + list(range(15, max(j0 - 1, 0), -1)):
-            mm(v("b0", 0, 16 * j), m(BOA), v3("eq", j, 256 - 16 * j, 256), False, False)
-        for h in range(2):
-            mm(v("b0", 128 * h, 128 * h + 128), m(BOD),
-               (T.eq[:, 8 * h:8 * h + 8, 256:272], "eq", 272 * 8 * h, 272 * (8 * h + 8), None, 128), False, h == 1)
-        scan(v("sc"), v("rst"), tot, 0.0, ALU.min, ALU.max)
-        tt(v("o1", 0, 16), v("sc", 15, 256, 16), v("cL", 32, 48), ALU.min)
-        tt(v("o1", 16, 32), v("o1", 0, 16), v(st, 0, 16), ALU.max)
-        copy(v("oU"), v("o1", 16, 32))
-        nw = 16 if last else 32
-        tt(v("dd", 0, nw), v("alt", 0, nw), v(st, 0, nw), ALU.subtract)
-        if OPT["nb"] == 2:
-            copy(ind(v("Bf" if last else "B"), v("oU", 0, 8)), hv("Ff", 0))
-        merge(1)
+            dma("Y", T.yx[:], v("X"), 5000)
+        nw = 32 if last else 64
+        move("w", v(ds, 1, 32, 2), v("ks", 15, 256, 16))
+        tt(v(ds, 0, nw, 2), v("alt", 0, nw // 2), v(ds, 1, nw, 2), ALU.subtract)
         amb = v("lc%d" % t)
-        act(v(zn, 0, 256), ind(v(zw), amb), ACT.Identity)
-        ts(v("am", 0, 16), amb, 255.5, ALU.is_gt)
+        act(v(zn, 0, 256), ind(v(zw), amb))
+        ts(v("am", 1, 32, 2), amb, 255.5, ALU.is_gt)
         if not last:
-            ts(v("am", 16, 32), amb, 255.5, ALU.is_gt)
-        tt(v("dd", 0, nw), v("dd", 0, nw), v("am", 0, nw), ALU.mult)
-        tt(v(sn, 0, nw), v("dd", 0, nw), v(st, 0, nw), ALU.add)
+            ts(v("am", 33, 64, 2), amb, 255.5, ALU.is_gt)
+        scan(v(dn, 0, nw), v("am", 0, nw), v(ds, 0, nw), 0.0, ALU.mult, ALU.add)
         if last:
+            act(v("vo"), v(dn, 1, 32, 2))
             dma("Y", T.yz[:], v(zn, 0, 256), 2500)
-            dma("Y", T.yv[:], v(sn, 0, 16), 2500)
+            dma("Y", T.yv[:], v("vo"), 2500)
         else:
-            send(v(zn, 0, 256), "zl%d" % (t + 1), "az%d" % (t + 1), hz[t + 1])
-            copy(v("vc"), v(sn))
-        if OPT["nb"] == 2:
-            copy(ind(v("Bf" if last else "B"), v("oU", 8, 16)), hv("Ff", 1))
-        else:
-            copy(ind(v("Bf" if last else "B"), v("oU")), v("Ff"))
+            send(v(zn, 0, 256), v("zl%d" % (t + 1)), "az%d" % (t + 1), hz[t + 1])
+            move("vc", v("vc"), v(dn, 1, 64, 2))
+    now[0] = "e"
     for h in range(4):
         bank = v("b%d" % h, 0, 256)
         if h:
-            act(bank, v("Bf", 1024 + 256 * h, 1280 + 256 * h), ACT.Identity, scale=4096.0)
+            act(bank, v(B, 1280 + 256 * h, 1536 + 256 * h), scale=4096.0)
         else:
-            ts(bank, v("Bf", 1024, 1280), 4096.0, ALU.mult)
-        tt(v("yo", 256 * h, 256 * h + 256), v("Bf", 256 * h, 256 * h + 256), bank, ALU.add)
+            ts(bank, v(B, 1280, 1536), 4096.0, ALU.mult)
+        tt(v("yo", 256 * h, 256 * h + 256), v(B, 256 * h + 256, 256 * h + 512), bank, ALU.add)
         if h % 2:
             dma("YS"[h // 2], T.yb[:, 256 * h - 256:256 * h + 256], v("yo", 256 * h - 256, 256 * h + 256), 3000)
 
@@ -686,11 +649,18 @@ def needs(ops):
     return out
 
 
+def spans(op, c):
+    k, x = op[7]
+    t = {"v": max(64, x) * c[0], "p": x * c[1], "g": 60 + x * c[2] * c[0], "s": 60 + x * c[3] * c[0], "x": 150 + x * c[0],
+         "r": c[6], "d": 100.0, "a": 0.0}[k]
+    return t, {"r": c[5] + 2 * x, "d": x * c[7]}.get(k, t)
+
+
 def arrange(ops):
-    if len(ops) in ORDER:
-        return [ops[i] for i in ORDER[len(ops)]]
-    need = needs(ops)
-    prev = {}
+    num = len(ops)
+    if num in ORDER:
+        return [ops[i] for i in ORDER[num]]
+    need, prev = needs(ops), {}
     for i, op in enumerate(ops):
         if op[4] == "a":
             need[i].add(i - 1)
@@ -698,61 +668,108 @@ def arrange(ops):
             if op[0] in prev:
                 need[i].add(-1 - prev[op[0]])
             prev[op[0]] = i
-    num = len(ops)
-    fwd, bwd = [[] for _ in ops], [[] for _ in ops]
-    for i in range(num):
-        for j in need[i]:
-            if j < 0:
-                j, gap = -1 - j, ops[-1 - j][6]
-            else:
-                gap = ops[j][7] + (0.0 if ops[i][0] == "P" and ops[j][0] == "P" else OPT["hop"])
-            fwd[i].append((j, gap))
-            bwd[j].append((i, gap + ops[i][6] - ops[j][6]))
-    level = [op[7] for op in ops]
+    que = [op[0] for op in ops]
+    sets = []
+    for c in COSTS:
+        dur, done = [spans(op, c)[0] for op in ops], [spans(op, c)[1] for op in ops]
+        fwd = [[(-1 - j, dur[-1 - j]) if j < 0 else (j, done[j] + (0.0 if que[i] == que[j] == "P" or que[i] == "X" else c[4]))
+                for j in need[i]] for i in range(num)]
+        sets.append((dur, done, fwd))
+    dur, done, fwd = sets[0]
+    bwd, level = [[] for _ in ops], list(done)
     for i in range(num - 1, -1, -1):
         for j, gap in fwd[i]:
+            bwd[j].append(i)
             level[j] = max(level[j], level[i] + gap)
+    ids, like = {}, []
+    for op in ops:
+        w = (op[3] or op[2])[0]
+        nm = (op[0], op[6], w[1] if w[1][0] == "b" else w[1].rstrip("0123456789"), w[2] // (128 if op[0] == "P" else 1))
+        like.append(ids.setdefault(nm, len(ids)))
 
-    def place(order, before, least):
-        start, busy = [0.0] * num, {}
-        for i in order:
-            t = least[i]
-            for j, gap in before[i]:
-                t = max(t, start[j] + gap)
-            lst = busy.setdefault(ops[i][0], [])
-            lo, hi = 0, len(lst)
-            while lo < hi:
-                mid = (lo + hi) // 2
-                if lst[mid][1] <= t:
-                    lo = mid + 1
-                else:
-                    hi = mid
-            while lo < len(lst) and lst[lo][0] < t + ops[i][6] - 1e-6:
-                t = max(t, lst[lo][1])
-                lo += 1
-            if ops[i][4] != "a":
-                lst.insert(lo, (t, t + ops[i][6]))
-            start[i] = t
-        return start
-    zero, tail = [0.0] * num, [op[7] - op[6] for op in ops]
-    best, seed = None, OPT["seed"]
-    for trial in range(OPT["tries"]):
-        key = list(level)
+    def place(delta):
+        key = [0.0] * num
         for i in range(num - 1, -1, -1):
-            seed = (seed * 1103515245 + 12345) % 2147483648
-            key[i] = level[i] + ops[i][8] + (OPT["noise"] * seed / 2147483648.0 if trial else 0.0)
-            for j, gap in bwd[i]:
-                key[i] = max(key[i], key[j] + 1e-3)
-        start = place(sorted(range(num), key=lambda e: (-key[e], e)), fwd, zero)
-        for rnd in range(OPT["rounds"] + 1):
-            end = max(start[i] + ops[i][7] for i in range(num))
-            if best is None or end < best[0]:
-                best = (end, start)
-            if rnd < OPT["rounds"]:
-                back = place(sorted(range(num), key=lambda e: (-start[e] - ops[e][6], -e)), bwd, tail)
-                start = place(sorted(range(num), key=lambda e: (-back[e] - ops[e][6], e)), fwd, zero)
-    start = best[1]
-    ORDER[num] = sorted(range(num), key=lambda e: (start[e], e))
+            k = level[i] + delta[like[i]]
+            for j in bwd[i]:
+                if key[j] + 1e-3 > k:
+                    k = key[j] + 1e-3
+            key[i] = k
+        start, why, busy = [0.0] * num, [None] * num, {q: ([], [], []) for q in "VSPGY"}
+        for i in sorted(range(num), key=lambda e: -key[e]):
+            t, w = 0.0, None
+            for j, gap in fwd[i]:
+                if start[j] + gap > t:
+                    t, w = start[j] + gap, j
+            if que[i] != "X":
+                s, e, o = busy[que[i]]
+                lo, hi, d = 0, len(s), dur[i] - 1e-6
+                while lo < hi:
+                    mid = (lo + hi) // 2
+                    if e[mid] <= t:
+                        lo = mid + 1
+                    else:
+                        hi = mid
+                hi = len(s)
+                while lo < hi and s[lo] < t + d:
+                    if e[lo] > t:
+                        t, w = e[lo], -1 - o[lo]
+                    lo += 1
+                s.insert(lo, t)
+                e.insert(lo, t + dur[i])
+                o.insert(lo, i)
+            start[i], why[i] = t, w
+        end = max(range(num), key=lambda x: start[x] + done[x])
+        order = sorted(range(num), key=lambda e: (start[e], e))
+        total = start[end] + done[end]
+        for dur2, done2, fwd2 in sets[1:]:
+            at, free, top = [0.0] * num, {q: 0.0 for q in "VSPGYX"}, 0.0
+            for i in order:
+                t = free[que[i]]
+                for j, gap in fwd2[i]:
+                    if at[j] + gap > t:
+                        t = at[j] + gap
+                at[i] = t
+                if que[i] != "X":
+                    free[que[i]] = t + dur2[i]
+                if t + done2[i] > top:
+                    top = t + done2[i]
+            total += 0.4 * top
+        return total, order, why, end, key
+
+    seed = [OPT["seed"]]
+
+    def rnd():
+        seed[0] = (seed[0] * 1103515245 + 12345) % 2147483648
+        return seed[0] / 2147483648.0
+    delta = [0.0] * len(ids)
+    best = cur = place(delta)
+    for trial in range(OPT["tries"]):
+        pairs, i = [], cur[3]
+        while i is not None:
+            w = cur[2][i]
+            if w is not None and w < 0:
+                w = -1 - w
+                if like[w] != like[i]:
+                    pairs.append((i, w))
+            i = w
+        d = list(delta)
+        if pairs and rnd() < 0.7:
+            i, w = pairs[int(rnd() * len(pairs))]
+            gap = cur[4][w] - cur[4][i] + 300 * rnd()
+            if rnd() < 0.5:
+                d[like[i]] += gap
+            else:
+                d[like[w]] -= gap
+        else:
+            for _ in range(1 + int(3 * rnd())):
+                d[int(rnd() * len(d))] += 2000 * (rnd() - rnd())
+        new = place(d)
+        if new[0] <= cur[0] + 250.0 * (1 - trial / OPT["tries"]) * rnd() * rnd():
+            cur, delta = new, d
+            if new[0] < best[0]:
+                best = new
+    ORDER[num] = best[1]
     return [ops[i] for i in ORDER[num]]
 
 
@@ -797,7 +814,7 @@ def emit(g, T, ops):
             queue[op[0]].wait_ge(T.sem[value[j][0]], value[j][1])
         ins = op[1]()
         if op[4] == "r":
-            sent += op[5]
+            sent += op[5][1]
         elif i in value:
             ins.then_inc(T.sem[value[i][0]], 16 if op[4] == "d" else 1)
     g.wait_ge(T.sem.sent, sent)

from concourse.mybir import AluOpType, ActivationFunctionType

RO = 4
ALU = AluOpType
ACT = ActivationFunctionType

SCRATCH = {
    "X": ("sbuf", [128, 4096], "bfloat16"),
    "B": ("sbuf", [128, 2304], "int32"),
    "Bf": ("sbuf", [128, 2304], "float32"),
    "xs": ("sbuf", [128, 256], "int32"),
    "xi": ("sbuf", [128, 256], "int32"),
    "xm": ("sbuf", [128, 8192], "bfloat16"),
    "Pu": ("sbuf", [128, 256], "uint16"),
    "vR": ("sbuf", [128, 256], "float16"),
    "Uh": ("sbuf", [128, 512], "float16"),
    "Dh": ("sbuf", [128, 256], "float16"),
    "cm": ("sbuf", [128, 1792], "bfloat16"),
    "ys": ("sbuf", [128, 256], "float16"),
    "sd": ("sbuf", [128, 256], "bfloat16"),
    "Q0": ("sbuf", [128, 256], "bfloat16"),
    "Q1": ("sbuf", [128, 256], "bfloat16"),
    "Qi": ("sbuf", [128, 128], "bfloat16"),
    "Es": ("sbuf", [128, 256], "bfloat16"),
    "Hs": ("sbuf", [128, 256], "int32"),
    "H": ("sbuf", [128, 256], "int32"),
    "Ge": ("sbuf", [128, 256], "float32"),
    "Fe": ("sbuf", [128, 256], "float32"),
    "tE": ("sbuf", [128, 256], "float32"),
    "Fs": ("sbuf", [128, 256], "int32"),
    "Ff": ("sbuf", [128, 256], "int32"),
    "old": ("sbuf", [128, 256], "bfloat16"),
    "sg": ("sbuf", [128, 256], "bfloat16"),
    "xn": ("sbuf", [128, 256], "bfloat16"),
    "av": ("sbuf", [128, 256], "float32"),
    "ks": ("sbuf", [128, 256], "float32"),
    "wR": ("sbuf", [128, 16, 17], "float16"),
    "eq": ("sbuf", [128, 16, 136], "bfloat16"),
    "ab": ("sbuf", [128, 16, 136], "bfloat16"),
    "sc": ("sbuf", [128, 272], "float32"),
    "iot": ("sbuf", [128, 2048], "float32"),
    "yo": ("sbuf", [128, 1024], "float32"),
    "vc": ("sbuf", [128, 32], "uint16"),
    "oU": ("sbuf", [128, 16], "uint16"),
    "ui": ("sbuf", [128, 32], "int32"),
    "alt": ("sbuf", [128, 32], "int32"),
    "am": ("sbuf", [128, 64], "float32"),
    "vo": ("sbuf", [128, 16], "float32"),
    "v0i": ("sbuf", [128, 16], "int32"),
    "uwi": ("sbuf", [128, 1], "int32"),
    "bti": ("sbuf", [8, 4], "int32"),
    "btb": ("sbuf", [8, 4], "bfloat16"),
    "s8": ("sbuf", [8, 128], "bfloat16"),
    "th": ("sbuf", [128, 8], "float32"),
    "col": ("sbuf", [128, 32], "float32"),
    "oh": ("sbuf", [128, 24], "float32"),
    "coi": ("sbuf", [128, 2], "int32"),
    "io": ("sbuf", [128, 144], "bfloat16"),
    "i16": ("sbuf", [128, 128], "bfloat16"),
    "blk": ("sbuf", [128, 128], "bfloat16"),
    "i17": ("sbuf", [128, 272], "bfloat16"),
    "cL": ("sbuf", [128, 16], "float32"),
    "cLh": ("sbuf", [128, 16], "float16"),
    "g8": ("sbuf", [128, 16], "bfloat16"),
    "pa": ("sbuf", [128, 6, 112], "bfloat16"),
    "pb": ("sbuf", [128, 64], "bfloat16"),
    "pq": ("sbuf", [128, 224], "bfloat16"),
    "SR": ("sbuf", [128, 14, 128], "bfloat16"),
    "SP": ("sbuf", [128, 1792], "bfloat16"),
    "M": ("sbuf", [128, 16, 128], "bfloat16"),
    "BI": ("sbuf", [128, 128], "float32"),
    "R2": ("sbuf", [128, 64], "bfloat16"),
    "Wi": ("sbuf", [128, 32], "int32"),
    "Wf": ("sbuf", [128, 32], "float32"),
    "W": ("sbuf", [128, 128], "float16"),
    "TT": ("sbuf", [128, 3, 144], "bfloat16"),
    "Tu": ("sbuf", [128, 144], "float16"),
    "ne": ("sbuf", [128, 272], "bfloat16"),
    "thr": ("sbuf", [128, 272], "bfloat16"),
    "rst": ("sbuf", [128, 272], "float32"),
    "mk": ("sbuf", [128, 128], "bfloat16"),
    "rs": ("sbuf", [128, 128], "float32"),
}
for _t in range(RO):
    SCRATCH["ms%d" % _t] = ("sbuf", [128, 512], "bfloat16")
    SCRATCH["Ph%d" % _t] = ("sbuf", [128, 256], "float16")
    SCRATCH["pl%d" % _t] = ("sbuf", [128, 256], "float16")
    SCRATCH["mc%d" % _t] = ("sbuf", [128, 16], "uint16")
    SCRATCH["lc%d" % _t] = ("sbuf", [128, 16], "uint16")
    SCRATCH["zl%d" % _t] = ("sbuf", [128, 256], "bfloat16")
    SCRATCH["ls%d" % _t] = ("sbuf", [128, 512], "bfloat16")
for _t in range(RO + 1):
    SCRATCH["zw%d" % _t] = ("sbuf", [128, 512], "bfloat16")
    SCRATCH["ds%d" % _t] = ("sbuf", [128, 64], "float32")
for _b in range(8):
    SCRATCH["b%d" % _b] = ("psum", [128, 512], "float32")

NDMA = 16
SEMAPHORES = ["qV", "qS", "qP", "qG", "sent"] + ["d%d" % _i for _i in range(NDMA)] \
    + [_s + str(_t) for _t in range(RO) for _s in ("az", "ac", "ap", "aa", "ab", "ad", "ae")]

OPT = {
    "units": [(0, 96, 1, "4SV", "222222011"), (96, 192, 1, "4SV", "333333455"), (192, 256, 0, "4SV", "667645071")],
    "bags": [(0, 64), (64, 256)],
    "gathers": [(0, 32, "S"), (32, 80, "V"), (80, 96, "S"), (96, 144, "S"), (144, 192, "S"), (192, 224, "S"), (224, 256, "S")],
    "chunks": [(0, 32), (32, 96), (96, 144), (144, 192), (192, 224), (224, 256)],
    "aside": "677", "yb": "5",
    "order": "d0 a1 a0 d1 d2 d3 d4 d5 r0 r1 r2 y0 a2 s0 o0 s1 o1 s2 o2 m0 m1 m2",
    "eqS": (2, 2, 0, 0), "rep": (2, 2, 2, 2, 2, 2, 2, 2), "xmode": 0, "nx": 2, "bint": True,
    "onS": ("vR", "wR", "w", "oU", "mc", "ui", "Dh2"),
    "loads": (5000, 8000), "seed": 1, "tries": 3000}
COSTS = [(0.87, 0.45, 1.56, 3.8, 230.0, 2200.0, 300.0, 1.0), (1.15, 0.58, 1.9, 5.0, 200.0, 2500.0, 400.0, 1.1),
         (0.85, 0.43, 1.2, 2.5, 320.0, 3200.0, 600.0, 0.8)]
ORDER = {}
MAGIC = 12582912.0
SIZE = {"bfloat16": 2, "float16": 2, "uint16": 2, "float32": 4, "int32": 4}


def rank_program(g, core, T, topo):
    rank = T.rank_of(core)
    if rank is None:
        return
    n = len(T.cores)
    ops = []
    now = [""]
    units = OPT["units"]

    def v(name, a=None, b=None, s=None, keys=None):
        w = SCRATCH[name][1][-1]
        lo = 0 if a is None else a
        hi = w if b is None else b
        ap_ = T[name][:, lo:hi] if s is None else T[name][:, lo:hi:s]
        return (ap_, name, lo, hi, keys, len(range(lo, hi, s or 1)))

    def vp(name, p0, p1, a, b, s=1):
        return (T[name][p0:p1, a:b:s], name, a, b, None, len(range(a, b, s)))

    def v3(name, i0, a=None, b=None):
        w = SCRATCH[name][1][-1]
        lo = 0 if a is None else a
        hi = w if b is None else b
        return (T[name][:, i0, lo:hi], name, i0 * w + lo, i0 * w + hi, None, hi - lo)

    def vs(name, i0, i1, a, b):
        w = SCRATCH[name][1][-1]
        return (T[name][:, i0:i1, a:b], name, i0 * w + a, (i1 - 1) * w + b, None, (i1 - i0) * (b - a))

    def vk(name, a, b, k, step=16):
        ua, ub = [u[:2] for u in units if u[0] <= a < u[1]][0]
        o = 16 * (ub if name == "mx" else ua)
        return v("xm", o + 16 * a + k, o + 16 * b, step, tuple(range(k, 16, step)))

    def both(a, b, k):
        return v("xm", 32 * a + k, 32 * b, 16, (k,))

    def ind(win, off):
        return (win[0].indirect(off[0]), win, off)

    def regs(x):
        if not isinstance(x, tuple):
            return []
        return [x[1], x[2]] if len(x) == 3 else [x]

    def ap(x):
        return x[0] if isinstance(x, tuple) else x

    def add(q, call, outs, ins, cost, kind="c", extra=None):
        rd, wr = [], []
        for x in ins:
            rd += regs(x)
            if len(regs(x)) == 2:
                cost = ("g", 16 * x[2][5])
        for x in outs:
            r = regs(x)
            wr.append(r[0])
            rd += r[1:]
            if len(r) == 2:
                cost = ("s", 16 * x[2][5])
        ops.append((q, call, rd, wr, kind, extra, now[0], cost))

    def cnt(out, *ins):
        two = all(SIZE[SCRATCH[regs(x)[0][1]][2]] == 2 for x in (out,) + ins)
        return ("v", regs(out)[0][5] * (0.5 if two else 1))

    def copy(out, in_):
        add("V", lambda: g.vector.tensor_copy(ap(out), ap(in_)), [out], [in_], cnt(out, in_))

    def tt(out, a, b, op):
        two = 1 if "psum" in (SCRATCH[regs(a)[0][1]][0], SCRATCH[b[1]][0]) else 2
        add("V", lambda: g.vector.tensor_tensor(ap(out), ap(a), ap(b), op), [out], [a, b], ("v", two * b[5]))

    def ts(out, a, s1, op0, s2=None, op1=None):
        if op1 is None:
            add("V", lambda: g.vector.tensor_scalar(ap(out), ap(a), ap(s1), None, op0), [out], [a, s1], cnt(out, a))
        else:
            add("V", lambda: g.vector.tensor_scalar(ap(out), ap(a), ap(s1), ap(s2), op0, op1), [out], [a, s1, s2], cnt(out, a))

    def scan(out, d0, d1, init, op0, op1):
        add("V", lambda: g.vector.tensor_tensor_scan(ap(out), ap(d0), ap(d1), init, op0, op1), [out], [d0, d1], ("v", out[5]))

    def memset(out, c_):
        add("V", lambda: g.vector.memset(ap(out), c_), [out], [], ("v", out[5]))

    def act(out, a, f=ACT.Identity, bias=0.0, scale=1.0):
        add("S", lambda: g.scalar.activation(ap(out), ap(a), f, bias=ap(bias), scale=ap(scale)), [out], [a, bias, scale],
            ("v", out[5]))

    def move(what, out, a, bias=0.0):
        if what in OPT["onS"]:
            act(out, a, bias=bias)
        elif bias:
            ts(out, a, bias, ALU.add)
        else:
            copy(out, a)

    def mm(out, l, r, start, stop):
        c_ = max(min(64, l[5]), r[5]) * (4 if SCRATCH[r[1]][2] == "float32" else 1)
        add("P", lambda: g.tensor.matmul(ap(out), ap(l), ap(r), start, stop), [out], [l, r], ("p", c_))

    def group(terms):
        for i, (o, l, r) in enumerate(terms):
            mm(o, l, r, i == 0, i == len(terms) - 1)

    def iota(out, pattern, base, cmul):
        if SCRATCH[out[1]][2] == "int32":
            add("G", lambda: g.iota(ap(out), pattern, base, cmul), [out], [], ("x", 2 * out[5]))
        else:
            add("G", lambda: g.iota(ap(out), pattern, base, cmul, allow_small_or_imprecise_dtypes=True), [out], [],
                ("x", 2 * out[5]))

    ndma = [0]

    def dma(q, out, in_, done):
        eng = g.sync if q == "Y" else g.scalar
        add(q, lambda: eng.dma_start(ap(out), ap(in_)), [out] if isinstance(out, tuple) else [], [in_], ("d", done), "d",
            "d%d" % ndma[0])
        ndma[0] += 1

    def send(src, dst, sem, hop):
        to = T.cores[(rank + hop) % n]
        rid, pid, _ = topo.addr(to)
        mask = topo.mask(core, to)
        add("G", lambda: g.remote_dma(ap(dst), ap(src), T.sem[sem], T.sem.sent, pid, rid, mask), [], [src],
            ("r", src[5]), "r", (sem, len(topo.engines(core, to))))
        frm = T.cores[(rank - hop) % n]
        add("X", None, [dst], [], ("a", 0), "a", (sem, len(topo.engines(frm, core))))

    hn = T.tables.get("HN", [1] * RO)
    hz = T.tables.get("HZ", [1] * RO)

    dma("S", v("uwi"), T.uw[:], 2000)
    dma("Y", v("v0i"), T.v0[:], 2000)
    dma("S", v("zw0", 0, 256), T.z0[:], 2200)
    dma("Y", v("bti"), T.bt[:], 2000)
    dma("Y", v("B", 256, 2304), T.bag[:], OPT["loads"][0])
    dma("Y", v("X"), T.xt[:], OPT["loads"][1])

    now[0] = "c"
    iota(v("coi", 0, 1), [[1, 1]], 0, 1)
    iota(v("io"), [[1, 144]], 0, 0)
    iota(v("i16"), [[0, 8], [1, 16]], 0, 0)
    iota(v("blk"), [[16, 8], [0, 16]], 0, 0)
    iota(v3("pa", 0), [[1, 7], [1, 16]], 1, 0)
    send(v("zw0", 0, 256), v("zl0"), "az0", hz[0])
    iota(v("i17"), [[0, 16], [1, 17]], 0, 0)
    iota(v("rst"), [[0, 272]], 8000000, 0)
    iota(v("rs"), [[0, 128]], 8000000, 0)
    for h in range(2):
        iota(v("iot", 1024 * h, 1024 * h + 1024), [[2, 1024]], -1023, 0)
    ncol = [0]

    def col(src=None, scale=1.0, bias=0.0):
        ncol[0] += 1
        c_ = v("col", ncol[0] - 1, ncol[0])
        if src is not None:
            act(c_, src, bias=bias, scale=scale)
        return c_

    def row(k):
        return v("oh", k, k + 1)

    def own16(gg):
        return v("oh", 16 + gg, 17 + gg)
    cr, cg, cp, c16 = col(), col(), col(), col()
    ts(v("coi", 1, 2), v("coi", 0, 1), 15, ALU.bitwise_and)
    copy(cp, v("coi", 0, 1))
    copy(cr, v("coi", 1, 2))
    tt(cg, v("coi", 0, 1), v("coi", 1, 2), ALU.subtract)
    ct = col(cg, bias=15.0)
    i16 = v("i16", 0, 16)
    ts(v("oh", 0, 16), i16, cr, ALU.is_equal)
    ts(v("oh", 16, 24), v("blk", 0, 128, 16), cg, ALU.is_equal)
    ts(c16, cr, 1.5, ALU.is_lt, 16.0, ALU.mult)
    I, NBO, IP, NIP, BOP, NBOP, IM, IG, SQ, CQ, IZ, BOA, IH, NIH, FQ, C2 = range(16)
    AQ, AH, AL, QY, VQ, BOD, BIB = range(7, 14)
    T2, TM1, TAM = range(3)

    def m(i):
        return v3("M", i)

    def sr(i):
        return v3("SR", i)

    def pa(i):
        return v3("pa", i)

    def pq(i):
        return v("pq", 16 * i, 16 * i + 16)
    ts(m(I), v("io", 0, 128), cp, ALU.is_equal)
    ts(m(NBO), v("blk"), cg, ALU.is_equal, -1.0, ALU.mult)
    act(v("g8", 0, 8), v("oh", 16, 24), scale=2.0)
    act(v("g8", 8, 16), v("oh", 16, 24), scale=-1.0)
    ts(v3("TT", TM1), v("io"), ct, ALU.is_equal, -1.0, ALU.mult)
    act(v3("TT", T2), v3("TT", TM1), scale=-2.0)
    act(v3("TT", TAM), v3("TT", TM1), scale=col(c16, 8.0))
    act(vp("R2", 0, 64, 0, 64), (T.M[0:64, I, 0:64],) + m(I)[1:])
    act(vp("R2", 64, 128, 0, 64), (T.M[64:128, I, 64:128],) + m(I)[1:], scale=-2.0)
    cu = col()
    copy(cu, v("uwi"))
    act(v("Wf", 0, 16), i16, scale=2.0, bias=1.0)
    ts(v("Wi", 0, 16), v("Wf", 0, 16), cu, ALU.mult, 2048.0, ALU.add)
    ts(v("Wi", 16, 32), v("Wi", 0, 16), 4095, ALU.bitwise_and)
    ts(v("Wf", 16, 32), v("Wi", 16, 32), -2048.0, ALU.add)
    act(v("Tu"), v3("TT", TM1), scale=col(v("Wf", 16, 17), -1.0))
    for gg in range(8):
        act(v("W", 16 * gg, 16 * gg + 16), v("Wf", 16, 32), scale=own16(gg))
    ts(v("cLh"), v("io", 0, 16), 16.0, ALU.mult, cr, ALU.add)
    act(v("cL"), v("cLh"), scale=16.0)

    def ulist(zv, bank):
        group([(bank, v("Tu", 15 - p, 143 - p), v(zv[1], zv[2] + p, zv[3], 16)) for p in range(16)])

    ulist(v("zw0", 0, 256), v("b6", 0, 16))
    copy(v("vc", 0, 16), v("v0i"))
    copy(v("ui", 0, 16), v("b6", 0, 16))
    ts(v("ui", 16, 32), v("ui", 0, 16), 15, ALU.bitwise_and)
    tt(v("ds0", 33, 64, 2), v("ui", 16, 32), v("cL"), ALU.add)
    copy(v("vc", 16, 32), v("ds0", 33, 64, 2))
    memset(v("am"), 0.0)
    memset(vs("wR", 0, 16, 16, 17), -1.0)
    c1 = col(row(0), -1.0, 1.0)
    memset((T.pa[:, 0, 0:112:16],) + pa(0)[1:5] + (7,), -100.0)
    ts(pa(1), pa(0), cr, ALU.is_equal)
    ts(pa(2), pa(0), col(cr, bias=15.0), ALU.is_equal, col(c1, -1.0), ALU.mult)
    ts(pa(3), pa(0), 15.5, ALU.is_lt, 0.5, ALU.subtract)
    ts(pa(4), v("i16", 0, 112), cr, ALU.is_equal, col(c1, -2.0), ALU.mult)
    tt(pa(5), pa(3), pa(4), ALU.mult)
    group([(v("b5", 0, 112), m(I), pa(i)) for i in (1, 2, 5)])
    act(v("pq", 0, 112), v("b5", 0, 112))
    ts(v("pb", 0, 16), i16, 0.0, ALU.is_equal)
    ts(pq(AQ), i16, 1.5, ALU.is_lt, c16, ALU.mult)
    act(pq(AH), v("pb", 0, 16), scale=col(row(2), -2040.0), bias=c16)
    act(pq(AL), v("pb", 0, 16), scale=col(row(2), 2040.0), bias=c16)
    ts(pq(VQ), i16, 4.0, ALU.is_equal, col(row(0), 4096.0), ALU.mult)
    ts(pq(BOD), i16, cr, ALU.is_lt, -float(2 ** 28), ALU.mult)
    ts(pq(BIB), i16, cr, ALU.not_equal)
    ts(v("pb", 16, 32), i16, 1.0, ALU.is_equal, -2.0, ALU.mult)
    ts(v("pb", 32, 48), i16, 2.0, ALU.not_equal)
    tt(v("pb", 48, 64), v("pb", 16, 32), v("pb", 32, 48), ALU.add)
    act(pq(QY), v("pb", 48, 64), scale=col(row(0), 2.0, -1.0))
    for gg in range(8):
        o = (T.SR[:, :, 16 * gg:16 * gg + 16], "SR", 0, 14 * 128, (gg,), 224)
        if gg % 4 == 3:
            act(o, v("pq"), scale=own16(gg))
        else:
            ts(o, v("pq"), own16(gg), ALU.mult)
    act(v("BI"), sr(BIB))
    for bank, s0, s1 in (("b4", 0, 4), ("b5", 4, 7)):
        for s in range(s0, s1):
            mm(v(bank, 128 * (s - s0), 128 * (s - s0 + 1)), sr(s), m(I), True, True)
        for e, off, scale in (("S", 0, 2048.0), ("V", 896, 4096.0)):
            used = [s for s in range(s0, s1) if any(u[3][1 + (s >= int(u[3][0]))] == e for u in units)]
            if used:
                act(v("SP", off + 128 * used[0], off + 128 * used[-1] + 128),
                    v(bank, 128 * (used[0] - s0), 128 * (used[-1] - s0 + 1)), scale=scale)
    for i, src, scale in ((IP, I, c1), (NBOP, NBO, c1), (IM, I, -4096.0), (IG, I, 16384.0), (IZ, I, 32768.0), (IH, I, 0.5),
                          (NIH, I, -0.5), (BOA, NBO, float(2 ** 28)), (NIP, IP, -1.0), (BOP, NBOP, -1.0),
                          (CQ, NBO, col(row(2), 22528.0)), (C2, NBO, col(row(2), 2048.0)), (SQ, NBO, col(row(3), -1.0)),
                          (FQ, NBO, col(row(4), 1024.0, col(row(3), -0.5, col(row(2), -0.5))))):
        act(m(i), m(src), scale=scale)
    act(v("Qi"), m(I), bias=row(2), scale=0.0)
    ts(v("ne"), v("i17"), cr, ALU.not_equal)
    act(v("thr"), v("ne"), scale=-float(2 ** 30), bias=4096.0)
    copy(v("thr", 16, 272, 17), v("cLh"))
    ts(v("mk"), v("i16"), cr, ALU.not_equal, -float(2 ** 20), ALU.mult)
    memset(v("rst", 0, 272, 17), -8000000.0)
    memset(v("rs", 0, 128, 16), -8000000.0)
    c8 = col(cp, 16.0)
    ts(v("s8"), vp("blk", 0, 8, 0, 128), vp("col", 0, 8, c8[2], c8[3]), ALU.is_equal)
    copy(v("btb"), v("bti"))
    mm(v("b7", 0, 4), v("s8"), v("btb"), True, True)
    act(v("th", 0, 4), v("b7", 0, 4), scale=-1.0, bias=-0.5)
    cq = col(c16, -1.0 / 16)
    act(v("th", 4, 8), v("b7", 0, 4), scale=cq, bias=col(row(4), -4096.0 * 1023, col(cq, bias=0.5)))
    cE = col(row(0), 30720.0, -26624.0)

    def slide(i, p):
        return v3("TT", i, 15 - p, 143 - p)

    for t in range(RO):
        now[0] = ""
        last = t == RO - 1
        zw, zn, ds, dn = "zw%d" % t, "zw%d" % (t + 1), "ds%d" % t, "ds%d" % (t + 1)
        z = v(zw, 0, 256)
        Q, Qp, Ph, ms, ls = "Q%d" % (t % 2), "Q%d" % ((t + 1) % 2), "Ph%d" % t, "ms%d" % t, "ls%d" % t
        B = "B" if OPT["bint"] else "Bf"
        for a, b in OPT["bags"]:
            copy(v("Pu", a, b), ind(v(B if t else "B", 256, 2304), v("vc", a // 16, b // 16)))
        move("Ph", v(Ph), v("Pu"), -2048.0)
        send(v(Ph), v("pl%d" % t), "ap%d" % t, hn[t])
        if t == 0 and B == "Bf":
            for h in range(4):
                copy(v("Bf", 256 + 512 * h, 768 + 512 * h), v("B", 256 + 512 * h, 768 + 512 * h))
        move("vR", v("vR"), ind(v("iot"), v("vc", 0, 16)))

        def changed(bank):
            src = ind(v("X"), v("vc", 16, 32))
            if OPT["xmode"] == 0:
                tt(v("xs"), src, z, ALU.add)
                ts(v("xi"), v("xs"), 255, ALU.bitwise_and)
            else:
                o = v(bank, 256, 512)
                act(v("old"), src)
                group([(o, m(I), v("old")), (o, m(I), z)])
                act(v("xn"), o, bias=-256.0)
                ts(v("sg"), o, 255.5, ALU.is_lt, 256.0, ALU.mult)

        def mean(bank):
            group([(v(bank, 0, 256), m(I), z), (v(bank, 0, 256), m(I), v("zl%d" % t))])
            act(v("av"), v(bank, 0, 256), bias=MAGIC, scale=0.5 - 2.0 ** -11)
            act(v(zw, 256, 512), v("av"), bias=-MAGIC)
            ulist(v(zw, 256, 512), v(bank, 0, 16))
            move("ui", v("ui", 0, 16), v(bank, 0, 16))
            ts(v("alt", 0, 16), v("ui", 0, 16), 2047, ALU.bitwise_and)
            if not last:
                ts(v("ui", 16, 32), v("ui", 0, 16), 15, ALU.bitwise_and)
                tt(v("alt", 16, 32), v("ui", 16, 32), v("cL"), ALU.add)

        def hashed(bank):
            group([(v(bank, 256, 512), v("W"), z), (v(bank, 256, 512), m(I), v(Ph))])
            move("Hs", v("Hs"), v(bank, 256, 512), 2048.0)
            ts(v("H"), v("Hs"), 4095, ALU.bitwise_and)

        def distances(i):
            a, b = OPT["chunks"][i]
            u = [j for j, u_ in enumerate(units) if u_[0] <= a < u_[1]][0]
            ua, ub, form, _, banks = units[u]
            rep = OPT["rep"][i]
            bank, w, bs = "b%d" % (i % 2), rep * (b - a), "b" + banks[0]
            for r in range(rep):
                mm(v(bank, r, w, rep), m(I), vk("xg", a, b, 0), True, True)
            s = 16 // rep
            parts = [(k0, s) for k0 in range(1, s)]
            while s < 16:
                parts.append((s, 2 * s))
                s *= 2
            parts.append((0, 16))
            for k0, s in parts:
                tt(vk("mx", a, b, k0, s), vk("xg", a, b, k0, s) if k0 else v(zw, a, b), v(bank, 0, w, s * rep // 16), ALU.max)
            if b != ub:
                return
            a, nl = ua, ub - ua
            ks = [k for k0, s in parts for k in range(k0, 16, s)]
            Uh = v("Uh", 2 * a, 2 * a + 128)
            if form == 2:
                group([(v(bs, 384 + k, 512, 16), both(a, b, k), v("g8", 8, 16)) for k in ks if k]
                      + [(vp(bs, 0, 64, 384, 512, 16), v(zw, a, b), v("g8", 8, 16))])
                mm(vp(bs, 64, 128, 384, 512, 16), vk("mx", a, b, 0), v("g8", 8, 16), False, True)
                move("Uh%d" % u, Uh, v(bs, 384, 512), 2040.0)
                group([(v(bs, 0, nl), m(NBO), vk("xg", a, b, 0)), (v(bs, 0, nl), Uh, v("R2"))])
            elif form == 1:
                Uh = vp("Uh", 0, nl, 2 * a, 2 * a + 128)
                group([(vp(bs, 0, nl, 384, 512), vk("xg", a, b, 0), m(NBO))]
                      + [(vp(bs, 0, nl, 384 + k, 512, 16), vk("xg", a, b, k) if k else v(zw, a, b), v("g8", 8, 16)) for k in range(16)]
                      + [(vp(bs, 0, nl, 384 + k, 512, 16), vk("mx", a, b, k), v("g8", 0, 8)) for k in ks])
                move("Uh%d" % u, Uh, vp(bs, 0, nl, 384, 512), -2040.0)
                mm(v(bs, 0, nl), Uh, (T.M[0:nl, I, 0:nl],) + v3("M", I, 0, nl)[1:], True, True)
            else:
                d = v(bs, 0, nl)
                group([(d, m(NBO), vk("xg", a, b, 0))]
                      + [(d, slide(TM1, k), vk("xg", a, b, k) if k else v(zw, a, b)) for k in range(16)]
                      + [(d, slide(T2, k), vk("mx", a, b, k)) for k in ks])

        def ranks(u):
            a, b, form, ns, banks = units[u]
            nl = b - a
            Dh, ys, R = v("Dh", a, b), v("ys", a, b), v("b" + banks[1], 384, 384 + nl)
            move("Dh%d" % u, Dh, v("b" + banks[0], 0, nl), 0.0 if form else -2040.0)
            terms = [(R, m(I), Dh)]
            cuts = [(0, int(ns[0]), ns[1] == "S"), (int(ns[0]), 7, ns[2] == "S")]
            for bank, (s0, s1, on_s) in zip(("b4", "b5"), cuts):
                for s in range(s0, s1):
                    mm(v(bank, nl * (s - s0), nl * (s - s0 + 1)), sr(s), Dh, True, True)
                o, i_ = v("cm", 7 * a + nl * s0, 7 * a + nl * s1), v(bank, 0, nl * (s1 - s0))
                if on_s:
                    act(o, i_, ACT.Sign, bias=0.5)
                else:
                    ts(o, i_, -0.5, ALU.is_gt, 0.5, ALU.subtract)
                off = 0 if on_s else 896
                terms += [(R, v("SP", off + 128 * s, off + 128 * s + 128), v("cm", 7 * a + nl * s, 7 * a + nl * (s + 1)))
                          for s in range(s0, s1)]
            group(terms)
            ts(ys, R, -2048.0, ALU.max, 2048.0, ALU.min)
            be = "b" + banks[2]
            hi, lo, qb = v(be, 0, nl), v(be, nl, 2 * nl), v(be, 256, 256 + nl)
            qp = v(Qp, a, b) if t else v("Qi", 0, nl)
            group([(hi, m(IP), Dh), (lo, m(NIP), Dh), (hi, sr(AH), qp), (lo, sr(AL), qp), (qb, sr(VQ), v("vR", a, b))]
                  + ([(qb, sr(AQ), qp)] if t else []) + [(hi, m(NBOP), ys), (lo, m(BOP), ys), (qb, sr(QY), ys)])
            act(v(ms, 2 * a, 2 * b), v(be, 0, 2 * nl), ACT.Sign, bias=v("th", t, t + 1))
            act(v(Q, a, b), qb, ACT.Sign, bias=v("th", 4 + t, 5 + t))
            send(v(ms, 2 * a, 2 * b), v(ls, 2 * a, 2 * b), "a" + "abde"[u] + str(t), hn[t])
            act(v("Es", a, b), R, ACT.Sign, bias=cE)

        def single(u):
            a, b, _, _, banks = units[u]
            nl, c0, c1_ = b - a, a // 16, b // 16
            kr, kl, tot = v("b" + banks[6], 0, nl), v("b" + banks[7], 128, 128 + nl), "b" + banks[8]
            group([(kr, m(I), v("vR", a, b)), (kr, m(FQ), v(Q, a, b))])
            move("wR", vs("wR", c0, c1_, 0, 16), kr)
            group([(kl, m(I), v("mk", 0, nl)), (kl, m(I), v("vR", a, b)), (kl, m(FQ), v(Q, a, b))])
            scan(v("ks", a, b), v("rs", 0, nl), kl, 0.0, ALU.min, ALU.max)
            act(v("rst", 17 * c0 + 16, 17 * c1_, 17), v("ks", a + 15, b, 16), bias=256.0)
            for j in range(c1_ - 1, c0 - 1, -1):
                o, i_, key = v3("eq", j, 119 - 17 * (j - c0), 136), vs("wR", c0, j + 1, 0, 17), v("ks", 16 * j + 15, 16 * j + 16)
                if j - c0 < OPT["eqS"][u]:
                    act(v3("ab", j, 119 - 17 * (j - c0), 136), i_, ACT.Abs, bias=key, scale=-1.0)
                    act(o, v3("ab", j, 119 - 17 * (j - c0), 136), ACT.Relu, bias=1.0, scale=-1.0)
                else:
                    ts(o, i_, key, ALU.is_equal)
            w = 17 * (c1_ - c0)
            group([(v(tot, 256, 256 + w), m(I), v("thr", 17 * c0, 17 * c1_))]
                  + [(v(tot, 256, 256 + 17 * (j - c0)), m(BOA), v3("eq", j, 119 - 17 * (j - c0), 119)) for j in range(c1_ - 1, c0, -1)]
                  + [(v(tot, 256, 256 + w), sr(BOD), vs("eq", c0, c1_, 119, 136))])
            scan(v("sc", 17 * c0, 17 * c1_), v("rst", 17 * c0, 17 * c1_), v(tot, 256, 256 + w), 0.0, ALU.min, ALU.max)
            move("oU", v("oU", c0, c1_), v("sc", 17 * c0 + 16, 17 * c1_, 17))

        def own(u):
            a, b, _, _, banks = units[u]
            nl, bo = b - a, "b" + banks[3]
            o = v(bo, 0, nl)
            group([(o, m(IH), v(ms, 2 * a, a + b)), (o, m(NIH), v(ms, a + b, 2 * b)), (o, m(SQ), v(Q, a, b))])
            act(v("sd", a, b), o, ACT.Abs)
            act(v(bo, 256, 256 + nl), v("Es", a, b), ACT.Relu)
            o = v(bo, 128, 128 + nl)
            group([(o, m(I), v(Ph, a, b)), (o, m(CQ), v(Q, a, b)), (o, m(IG), v("sd", a, b))])
            tt(v("Ge", a, b), v("H", a, b), o, ALU.max)

        def merge(u):
            a, b, _, _, banks = units[u]
            o = v("b" + banks[4], 384, 384 + b - a)
            group([(o, m(I), v("pl%d" % t, a, b)), (o, m(C2), v(Q, a, b)), (o, m(IM), v(ls, 2 * a, a + b)),
                   (o, m(IM), v(ls, a + b, 2 * b))])
            tt(v("Fe", a, b), v("Ge", a, b), o, ALU.max)
            tt(v("tE", a, b), v("Fe", a, b), v("b" + banks[3], 256, 256 + b - a), ALU.mult)
            o = v("b" + banks[5], 0, b - a)
            group([(o, m(IZ), v("Es", a, b)), (o, v("BI"), v("tE", a, b))])
            tt(v("Fs", a, b), v("Fe", a, b), o, ALU.max)
            ts(v("Ff", a, b), v("Fs", a, b), 4095, ALU.bitwise_and)
            copy(ind(v(B), v("oU", a // 16, b // 16)), v("Ff", a, b))

        def ambiguous(_):
            y = v("b" + OPT["yb"], 384, 400)
            group([(y, m(I), v("cLh"))] + [(y, slide(TAM, p), v(Q, p, 256, 16)) for p in range(16)])
            move("mc", v("mc%d" % t), y)
            send(v("mc%d" % t), v("lc%d" % t), "ac%d" % t, hz[t])

        for a, b, e in OPT["gathers"]:
            src = ind(v("X"), v("Pu", a, b))
            if e == "V":
                copy(vk("xg", a, b, 0, 1), src)
            else:
                act(vk("xg", a, b, 0, 1), src)
        stage = {"d": distances, "r": ranks, "s": single, "o": own, "m": merge, "y": ambiguous,
                 "a": lambda i: (changed, hashed, mean)[i]("b" + OPT["aside"][i])}
        for word in OPT["order"].split():
            now[0] = word
            stage[word[0]](int(word[1:]))
        now[0] = ""
        w = 16 // OPT["nx"]
        for h in range(OPT["nx"]):
            o = ind(v("X"), v("vc", 16 + w * h, 16 + w * (h + 1)))
            if OPT["xmode"] == 0:
                copy(o, v("xi", 16 * w * h, 16 * w * (h + 1)))
            else:
                tt(o, v("xn", 16 * w * h, 16 * w * (h + 1)), v("sg", 16 * w * h, 16 * w * (h + 1)), ALU.add)
        if last:
            dma("Y", T.yx[:], v("X"), 5000)
        nw = 32 if last else 64
        move("w", v(ds, 1, 32, 2), v("ks", 15, 256, 16))
        tt(v(ds, 0, nw, 2), v("alt", 0, nw // 2), v(ds, 1, nw, 2), ALU.subtract)
        amb = v("lc%d" % t)
        act(v(zn, 0, 256), ind(v(zw), amb))
        ts(v("am", 1, 32, 2), amb, 255.5, ALU.is_gt)
        if not last:
            ts(v("am", 33, 64, 2), amb, 255.5, ALU.is_gt)
        scan(v(dn, 0, nw), v("am", 0, nw), v(ds, 0, nw), 0.0, ALU.mult, ALU.add)
        if last:
            act(v("vo"), v(dn, 1, 32, 2))
            dma("Y", T.yz[:], v(zn, 0, 256), 2500)
            dma("Y", T.yv[:], v("vo"), 2500)
        else:
            send(v(zn, 0, 256), v("zl%d" % (t + 1)), "az%d" % (t + 1), hz[t + 1])
            move("vc", v("vc"), v(dn, 1, 64, 2))
    now[0] = "e"
    for h in range(4):
        bank = v("b%d" % h, 0, 256)
        if h:
            act(bank, v(B, 1280 + 256 * h, 1536 + 256 * h), scale=4096.0)
        else:
            ts(bank, v(B, 1280, 1536), 4096.0, ALU.mult)
        tt(v("yo", 256 * h, 256 * h + 256), v(B, 256 * h + 256, 256 * h + 512), bank, ALU.add)
        if h % 2:
            dma("YS"[h // 2], T.yb[:, 256 * h - 256:256 * h + 256], v("yo", 256 * h - 256, 256 * h + 256), 3000)

    emit(g, T, arrange(ops))


def overlap(a, b):
    if a[3] <= b[2] or b[3] <= a[2]:
        return False
    if a[4] is not None and b[4] is not None:
        return any(k in b[4] for k in a[4])
    return True


def needs(ops):
    seen, wrote, out = {}, {}, []
    for i, op in enumerate(ops):
        q, rd, wr, kind = op[0], op[2], op[3], op[4]
        need = set()
        for x, w in [(x, False) for x in rd] + [(x, True) for x in wr]:
            psum = SCRATCH[x[1]][0] == "psum"
            hist = (seen if w or psum else wrote).get(x[1], [])
            for e in range(len(hist) - 1, -1, -1):
                j, y, wy = hist[e]
                same = ops[j][0] == q and ops[j][4] == "c" and kind == "c"
                if psum and (not same or q == "P"):
                    need.add(j)
                    if ops[j][0] == "P":
                        break
                elif (w or wy) and overlap(x, y):
                    need.add(j)
        out.append(need)
        for x in wr:
            seen.setdefault(x[1], []).append((i, x, True))
            wrote.setdefault(x[1], []).append((i, x, True))
        for x in rd:
            seen.setdefault(x[1], []).append((i, x, False))
    return out


def spans(op, c):
    k, x = op[7]
    t = {"v": max(64, x) * c[0], "p": x * c[1], "g": 60 + x * c[2] * c[0], "s": 60 + x * c[3] * c[0], "x": 150 + x * c[0],
         "r": c[6], "d": 100.0, "a": 0.0}[k]
    return t, {"r": c[5] + 2 * x, "d": x * c[7]}.get(k, t)


def arrange(ops):
    num = len(ops)
    if num in ORDER:
        return [ops[i] for i in ORDER[num]]
    need, prev = needs(ops), {}
    for i, op in enumerate(ops):
        if op[4] == "a":
            need[i].add(i - 1)
        if op[4] == "d":
            if op[0] in prev:
                need[i].add(-1 - prev[op[0]])
            prev[op[0]] = i
    que = [op[0] for op in ops]
    sets = []
    for c in COSTS:
        dur, done = [spans(op, c)[0] for op in ops], [spans(op, c)[1] for op in ops]
        fwd = [[(-1 - j, dur[-1 - j]) if j < 0 else (j, done[j] + (0.0 if que[i] == que[j] == "P" or que[i] == "X" else c[4]))
                for j in need[i]] for i in range(num)]
        sets.append((dur, done, fwd))
    dur, done, fwd = sets[0]
    bwd, level = [[] for _ in ops], list(done)
    for i in range(num - 1, -1, -1):
        for j, gap in fwd[i]:
            bwd[j].append(i)
            level[j] = max(level[j], level[i] + gap)
    ids, like = {}, []
    for op in ops:
        w = (op[3] or op[2])[0]
        nm = (op[0], op[6], w[1] if w[1][0] == "b" else w[1].rstrip("0123456789"), w[2] // (128 if op[0] == "P" else 1))
        like.append(ids.setdefault(nm, len(ids)))

    def place(delta):
        key = [0.0] * num
        for i in range(num - 1, -1, -1):
            k = level[i] + delta[like[i]]
            for j in bwd[i]:
                if key[j] + 1e-3 > k:
                    k = key[j] + 1e-3
            key[i] = k
        start, why, busy = [0.0] * num, [None] * num, {q: ([], [], []) for q in "VSPGY"}
        for i in sorted(range(num), key=lambda e: -key[e]):
            t, w = 0.0, None
            for j, gap in fwd[i]:
                if start[j] + gap > t:
                    t, w = start[j] + gap, j
            if que[i] != "X":
                s, e, o = busy[que[i]]
                lo, hi, d = 0, len(s), dur[i] - 1e-6
                while lo < hi:
                    mid = (lo + hi) // 2
                    if e[mid] <= t:
                        lo = mid + 1
                    else:
                        hi = mid
                hi = len(s)
                while lo < hi and s[lo] < t + d:
                    if e[lo] > t:
                        t, w = e[lo], -1 - o[lo]
                    lo += 1
                s.insert(lo, t)
                e.insert(lo, t + dur[i])
                o.insert(lo, i)
            start[i], why[i] = t, w
        end = max(range(num), key=lambda x: start[x] + done[x])
        order = sorted(range(num), key=lambda e: (start[e], e))
        total = start[end] + done[end]
        for dur2, done2, fwd2 in sets[1:]:
            at, free, top = [0.0] * num, {q: 0.0 for q in "VSPGYX"}, 0.0
            for i in order:
                t = free[que[i]]
                for j, gap in fwd2[i]:
                    if at[j] + gap > t:
                        t = at[j] + gap
                at[i] = t
                if que[i] != "X":
                    free[que[i]] = t + dur2[i]
                if t + done2[i] > top:
                    top = t + done2[i]
            total += 0.4 * top
        return total, order, why, end, key

    seed = [OPT["seed"]]

    def rnd():
        seed[0] = (seed[0] * 1103515245 + 12345) % 2147483648
        return seed[0] / 2147483648.0
    delta = [0.0] * len(ids)
    best = cur = place(delta)
    for trial in range(OPT["tries"]):
        pairs, i = [], cur[3]
        while i is not None:
            w = cur[2][i]
            if w is not None and w < 0:
                w = -1 - w
                if like[w] != like[i]:
                    pairs.append((i, w))
            i = w
        d = list(delta)
        if pairs and rnd() < 0.7:
            i, w = pairs[int(rnd() * len(pairs))]
            gap = cur[4][w] - cur[4][i] + 300 * rnd()
            if rnd() < 0.5:
                d[like[i]] += gap
            else:
                d[like[w]] -= gap
        else:
            for _ in range(1 + int(3 * rnd())):
                d[int(rnd() * len(d))] += 2000 * (rnd() - rnd())
        new = place(d)
        if new[0] <= cur[0] + 250.0 * (1 - trial / OPT["tries"]) * rnd() * rnd():
            cur, delta = new, d
            if new[0] < best[0]:
                best = new
    ORDER[num] = best[1]
    return [ops[i] for i in ORDER[num]]


def emit(g, T, ops):
    queue = {"V": g.vector, "S": g.scalar, "P": g.tensor, "G": g, "Y": g.sync}
    know = {q: {} for q in queue}
    at, waits, pos, count = [], [], [], {}
    for i, need in enumerate(needs(ops)):
        q, kind = ops[i][0], ops[i][4]
        src = q if kind == "c" else ("o", i)
        count[src] = count.get(src, 0) + 1
        pos.append((src, count[src]))
        mine = []
        if kind != "a":
            k = know[q]
            for j in sorted(need, reverse=True):
                s, p = pos[j]
                if k.get(s, 0) < p and not (q == "P" and s == "P"):
                    mine.append(j)
                    k[s] = p
                    for s2, p2 in at[j].items():
                        if k.get(s2, 0) < p2:
                            k[s2] = p2
            at.append(dict(k))
        else:
            at.append({})
        waits.append(mine)
    wanted = set(j for w in waits for j in w)
    value, n, sent = {}, {}, 0
    for i, op in enumerate(ops):
        if op[4] == "c" and i in wanted:
            n[op[0]] = n.get(op[0], 0) + 1
            value[i] = ("q" + op[0], n[op[0]])
        elif op[4] == "d":
            value[i] = (op[5], 16)
        elif op[4] == "a":
            value[i] = op[5]
    for i, op in enumerate(ops):
        if op[4] == "a":
            continue
        for j in waits[i]:
            queue[op[0]].wait_ge(T.sem[value[j][0]], value[j][1])
        ins = op[1]()
        if op[4] == "r":
            sent += op[5][1]
        elif i in value:
            ins.then_inc(T.sem[value[i][0]], 16 if op[4] == "d" else 1)
    g.wait_ge(T.sem.sent, sent)
    for i, op in enumerate(ops):
        if op[4] == "d" and i not in wanted:
            queue[op[0]].wait_ge(T.sem[op[5]], 16)
